import numpy as np
import ml_dtypes


def mxq(x, axis, fmt="e4m3"):
    dtype, down = {"e4m3": (ml_dtypes.float8_e4m3fn, 7), "e5m2": (ml_dtypes.float8_e5m2, 14)}[fmt]
    v = np.moveaxis(np.asarray(x, np.float32).astype(ml_dtypes.bfloat16).astype(np.float64), axis, -1)
    blocks = v.reshape(v.shape[:-1] + (-1, 32))
    amax = np.abs(blocks).max(-1, keepdims=True)
    byte = np.maximum(np.where(amax > 0, np.frexp(amax)[1] - 1 + 127, 0) - down, 1)
    scale = np.exp2(byte - 127.0)
    codes = (blocks / scale).astype(np.float32).astype(dtype).astype(np.float64)
    return np.moveaxis((codes * scale).reshape(v.shape), -1, axis)


WIDE = False


def mx_kscale(k):
    if not WIDE:
        return np.ones(k)
    levels = np.array([10, -10, 5, -5, 0])
    if k % 512:
        return np.exp2(np.random.permutation(np.resize(levels, k // 32))).repeat(32)
    a = np.empty((k // 512, 16))
    for p in range(k // 512):
        a[p, :8] = np.random.permutation(np.resize(levels, 8))
        for g in range(8):
            far = levels[np.abs(levels - a[p, g]) >= 10]
            a[p, g + 8] = far[np.random.randint(len(far))]
    return np.exp2(a.ravel()).repeat(32)


def f64(x):
    return np.asarray(x).astype(np.float64)


def striped(idx):
    return np.tile(idx.reshape(-1, 16).T, (8, 1)).astype(np.uint16)


def unstriped(offs):
    return offs[:16].T.reshape(-1).astype(np.int64)


E2M1 = np.array([0.0, 0.5, 1.0, 1.5, 2.0, 3.0, 4.0, 6.0, -0.0, -0.5, -1.0, -1.5, -2.0, -3.0, -4.0, -6.0])


def pack_weight(w, fmt):
    k, n = w.shape
    w = f64(np.asarray(w, np.float32).astype(ml_dtypes.bfloat16)).reshape(k // 32, 32, n)
    amax = np.abs(w).max(1)
    if fmt == "e4m3":
        byte = np.frexp(amax)[1] - 1 + 127 - 7
    else:
        mant, ex = np.frexp(amax / 6.0)
        byte = np.where(mant > 0.5, ex, ex - 1) + 127
    byte = np.clip(np.where(amax > 0, byte, 1), 1, 254)
    scaled = (w * np.exp2(127.0 - byte)[:, None, :]).reshape(k, n).astype(np.float32)
    by_word = np.ascontiguousarray(scaled.reshape(k // 512, 128, 4, n).transpose(0, 1, 3, 2))
    if fmt == "e4m3":
        words = by_word.astype(ml_dtypes.float8_e4m3fn).view(np.uint8)
    else:
        c = by_word.astype(ml_dtypes.float4_e2m1fn).view(np.uint8) & 0xF
        words = (c[..., 0::2] | (c[..., 1::2] << 4)).reshape(k // 512, 128, 2 * n)
    return np.ascontiguousarray(words), np.ascontiguousarray(byte.astype(np.uint8).reshape(k // 512, 16, n))


def unpack_weight(words, scales, fmt):
    g, _, n = scales.shape
    words = np.ascontiguousarray(words).reshape(g, 128, n, -1)
    if fmt == "e4m3":
        vals = words.view(ml_dtypes.float8_e4m3fn).astype(np.float64)
    else:
        nib = np.empty((g, 128, n, 4), np.uint8)
        nib[..., 0::2] = words & 0xF
        nib[..., 1::2] = words >> 4
        vals = E2M1[nib]
    vals = vals * np.repeat(np.exp2(scales.astype(np.float64) - 127.0), 8, axis=1)[..., None]
    return vals.transpose(0, 1, 3, 2).reshape(g * 512, n)


def gelu(v):
    return 0.5 * v * (1.0 + np.tanh(np.sqrt(2.0 / np.pi) * (v + 0.044715 * v**3)))


K, K2, T, T2, S, H, N = 1024, 512, 2048, 4096, 1024, 1024, 512

def setup_inputs():
    n = np.random.standard_normal
    s = mx_kscale(K)[:, None]
    s2 = mx_kscale(K2)[:, None]
    u = mx_kscale(H)[:, None]
    tab_words, tab_scales = pack_weight(n((K, T)) * s, "e4m3")
    tab2_words, tab2_scales = pack_weight(n((K2, T2)) * s2, "e4m3")
    wp_words, wp_scales = pack_weight(n((K2, H)) / np.sqrt(K2) / s2, "e2m1")
    return {
        "tab_words": tab_words, "tab_scales": tab_scales,
        "tab2_words": tab2_words, "tab2_scales": tab2_scales,
        "offs": striped(np.random.permutation(T)[:S]),
        "offs2": striped(np.random.permutation(T2)[:S]),
        "wc": (n((K, H)) / np.sqrt(K) / s).astype(np.float32),
        "wp_words": wp_words, "wp_scales": wp_scales,
        "amp": (np.exp(0.3 * n(H)) * u[:, 0]).astype(np.float32),
        "coef": (n((H, N)) / np.sqrt(H) / u).astype(np.float32),
    }

def reference(tab_words, tab_scales, tab2_words, tab2_scales, offs, offs2, wc, wp_words, wp_scales, amp, coef):
    v = unpack_weight(tab_words, tab_scales, "e4m3")[:, unstriped(offs)]
    v2 = unpack_weight(tab2_words, tab2_scales, "e4m3")[:, unstriped(offs2)]
    wcq = mxq(f64(wc), 0, "e4m3")
    wp = unpack_weight(wp_words, wp_scales, "e2m1")
    a = wcq.T @ v
    b = wp.T @ v2
    d = np.abs(a - b)
    h = f64(amp)[:, None] * np.exp(-d)
    hq = mxq(h, 0, "e4m3")
    cq = mxq(f64(coef), 0, "e4m3")
    return cq.T @ hq

@@ -1,0 +1,299 @@
+from contextlib import ExitStack
+
+import concourse.mybir as mybir
+
+K, K2, T, T2, S, H, N = 1024, 512, 2048, 4096, 1024, 1024, 512
+FLOPS = 2 * S * (K * H + K2 * H + H * N)
+
+F32 = mybir.dt.float32
+BF16 = mybir.dt.bfloat16
+I32 = mybir.dt.int32
+U32 = mybir.dt.uint32
+U16 = mybir.dt.uint16
+U8 = mybir.dt.uint8
+FP8X4 = mybir.dt.float8_e4m3fn_x4
+FP4X4 = mybir.dt.float4_e2m1fn_x4
+ACT = mybir.ActivationFunctionType
+ALU = mybir.AluOpType
+
+P = 128
+PACK = 4
+KP = P * PACK
+HALF = 512
+LIST_COLS = HALF // 16
+
+
+def tile_list_crystal_laplace_energies_kernel(
+    tc, tab_words, tab_scales, tab2_words, tab2_scales, offs, offs2, wc, wp_words, wp_scales, amp, coef, out
+):
+    nc = tc.nc
+    with ExitStack() as ctx:
+        lists = ctx.enter_context(tc.tile_pool(name="lists", bufs=1))
+        keep = ctx.enter_context(tc.tile_pool(name="keep", bufs=1))
+        work = ctx.enter_context(tc.tile_pool(name="work", bufs=2))
+        psum = ctx.enter_context(tc.psum_pool(name="psum", bufs=8))
+
+        def held(name, shape, dtype):
+            return keep.tile(shape, dtype, name=name, align_bytes=64)
+
+        idx = lists.tile([P, S // 16], U16, name="idx")
+        idx2 = lists.tile([P, S // 16], U16, name="idx2")
+
+        wc_sb, coef_sb, wc_bf = {}, {}, {}
+        amp_sb = held("amp_sb", [P, 2, PACK], F32)
+
+        def load_words(name, words):
+            dst = held(name, [P, words.shape[1]], I32)
+            nc.sync.dma_start(dst[:], words.rearrange("p t i -> p (t i)").bitcast(I32))
+            return dst
+
+        def load_wc(a, b):
+            wc_sb[a, b] = held("wc_sb%d%d" % (a, b), [P, PACK, KP], F32)
+            rows = wc[a * KP : (a + 1) * KP, b * KP : (b + 1) * KP]
+            nc.sync.dma_start(wc_sb[a, b][:], rows.rearrange("(p j) c -> p j c", j=PACK))
+
+        def load_plane(name, scales, first, queue):
+            passes, rows, width = scales.shape
+            plane = held(name, [P, width // 4], I32)
+            nc.vector.memset(plane[:], 0)
+            for q in range(4):
+                start = 32 * q + first
+                queue.dma_start(plane[start : start + 4 * passes, :], scales[:, 4 * q : 4 * q + 4, :].bitcast(I32))
+            return plane
+
+        def load_coef(b):
+            coef_sb[b] = held("coef_sb%d" % b, [P, PACK, N], F32)
+            nc.sync.dma_start(coef_sb[b][:], coef[b * KP : (b + 1) * KP, :].rearrange("(p j) n -> p j n", j=PACK))
+
+        nc.sync.dma_start(idx[:], offs)
+        tab_plane = load_plane("tab_plane", tab_scales, 4, nc.scalar)
+        tab2_plane = load_plane("tab2_plane", tab2_scales, 0, nc.scalar)
+        wp_plane = load_plane("wp_plane", wp_scales, 0, nc.gpsimd)
+        nc.gpsimd.dma_start(amp_sb[:], amp.rearrange("(b p t) -> p b t", b=2, t=PACK))
+        tab_sb0 = load_words("tab_sb0", tab_words[0])
+        load_wc(0, 0)
+        wp_sb = held("wp_sb", [P, H // 2], I32)
+        nc.sync.dma_start(wp_sb[:], wp_words[0].bitcast(I32))
+        nc.sync.dma_start(idx2[:], offs2)
+        load_wc(1, 0)
+        tab_sb1 = load_words("tab_sb1", tab_words[1])
+        tab2_sb = load_words("tab2_sb", tab2_words[0])
+        load_wc(0, 1)
+        load_wc(1, 1)
+        load_coef(0)
+        load_coef(1)
+
+        v_codes = {(a, s): held("v_codes%d%d" % (a, s), [P, HALF], U32) for a in range(2) for s in range(2)}
+        v_scales = [held("v_scales%d" % s, [P, HALF], U8) for s in range(2)]
+        v2_codes = [held("v2_codes%d" % s, [P, HALF], U32) for s in range(2)]
+        v2_scales = [held("v2_scales%d" % s, [P, HALF], U8) for s in range(2)]
+
+        def gather(dst, table, dtype, offsets, s):
+            window = table[:].bitcast(dtype)
+            nc.vector.tensor_copy(dst[:], window.indirect(offsets[:, s * LIST_COLS : (s + 1) * LIST_COLS]))
+
+        blocks = [(a, b) for a in range(2) for b in range(2)]
+        wc_codes = {key: held("wc_codes%d%d" % key, [P, KP], U32) for key in blocks}
+        wc_scales = {key: held("wc_scales%d%d" % key, [P, KP], U8) for key in blocks}
+
+        def round_wc(a, b, on_scalar):
+            wc_bf[a, b] = held("wc_bf%d%d" % (a, b), [P, PACK, P, PACK], BF16)
+            dst = wc_bf[a, b][:].rearrange("p t m j -> p m j t")
+            src = wc_sb[a, b][:].rearrange("p j (m t) -> p m j t", t=PACK)
+            if on_scalar:
+                nc.scalar.activation(dst, src, ACT.Copy, scale=-1.0)
+            else:
+                nc.vector.tensor_scalar(dst, src, -1.0, None, ALU.mult)
+
+        def quantize(codes, scales, grouped):
+            nc.vector.quantize_mx(out=codes.bitcast(FP8X4), scales=scales, in_=grouped)
+
+        def quantize_wc(a, b):
+            quantize(wc_codes[a, b][:], wc_scales[a, b][:], wc_bf[a, b][:].rearrange("p t m j -> p (t m j)"))
+
+        wp_codes = held("wp_codes", [P, 2 * H], U8)
+        wp_perm_scales = held("wp_perm_scales", [P, H], U8)
+
+        gather(v_scales[0], tab_plane, U8, idx, 0)
+        gather(v_codes[0, 0], tab_sb0, U32, idx, 0)
+        round_wc(0, 0, True)
+        quantize_wc(0, 0)
+        round_wc(1, 0, True)
+        quantize_wc(1, 0)
+        gather(v_codes[1, 0], tab_sb1, U32, idx, 0)
+        nc.vector.tensor_copy(
+            wp_codes[:].bitcast(U16).rearrange("p (b t m) -> p b m t", b=2, t=PACK),
+            wp_sb[:].bitcast(U16).rearrange("p (b m t) -> p b m t", b=2, t=PACK),
+        )
+        nc.vector.tensor_copy(
+            wp_perm_scales[:].rearrange("p (b t m) -> p b m t", b=2, t=PACK),
+            wp_plane[:].bitcast(U8).rearrange("p (b m t) -> p b m t", b=2, t=PACK),
+        )
+        gather(v2_scales[0], tab2_plane, U8, idx2, 0)
+        gather(v2_codes[0], tab2_sb, U32, idx2, 0)
+        gather(v_scales[1], tab_plane, U8, idx, 1)
+        gather(v_codes[0, 1], tab_sb0, U32, idx, 1)
+        gather(v_codes[1, 1], tab_sb1, U32, idx, 1)
+        gather(v2_scales[1], tab2_plane, U8, idx2, 1)
+        gather(v2_codes[1], tab2_sb, U32, idx2, 1)
+
+        def pass_a(bank, a, b, t, s):
+            cols = slice(t * P, (t + 1) * P)
+            nc.tensor.matmul_mx(
+                out=bank[:],
+                lhsT=wc_codes[a, b][:, cols].bitcast(FP8X4),
+                lhsT_scale=wc_scales[a, b][:, cols],
+                rhs=v_codes[a, s][:].bitcast(FP8X4),
+                rhs_scale=v_scales[s][4 * (a + 1) : P, :],
+                start=(a == 0),
+                stop=False,
+            )
+
+        def pass_b(bank, b, t, s):
+            first = b * KP + t * P
+            nc.tensor.matmul_mx(
+                out=bank[:],
+                lhsT=wp_codes[:, 2 * first : 2 * (first + P)].bitcast(FP4X4),
+                lhsT_scale=wp_perm_scales[:, first : first + P],
+                rhs=v2_codes[s][:].bitcast(FP8X4),
+                rhs_scale=v2_scales[s][:],
+                start=False,
+                stop=True,
+            )
+
+        def new_bank():
+            return psum.tile([P, HALF], F32, name="bank", tag="bank")
+
+        chunks = [(b, s) for b in range(2) for s in range(2)]
+        dist, kern = {}, {}
+        h_bf = {c: held("h_bf%d%d" % c, [P, HALF, PACK], BF16) for c in chunks}
+        h_codes = {c: held("h_codes%d%d" % c, [P, HALF], U32) for c in chunks}
+        h_scales = {c: held("h_scales%d%d" % c, [P, HALF], U8) for c in chunks}
+
+        def new_work(c):
+            dist[c] = work.tile([P, PACK, HALF], F32, name="dist", align_bytes=64)
+            kern[c] = work.tile([P, PACK, HALF], F32, name="kern", align_bytes=64)
+
+        def take_abs(c, banks, cols):
+            for t in range(PACK):
+                nc.scalar.activation(dist[c][:, t, cols], banks[t][:, cols], ACT.Abs)
+
+        def take_exp(c, cols):
+            nc.scalar.activation(kern[c][:, :, cols], dist[c][:, :, cols], ACT.Exp, scale=-1.0)
+
+        def weigh(c, cols):
+            runs = (cols.stop - cols.start) // 4
+            weights = amp_sb[:, c[0], :].unsqueeze(1).unsqueeze(3).to_broadcast([P, runs, PACK, 4])
+            nc.vector.tensor_tensor(
+                h_bf[c][:, cols, :].rearrange("p (u i) t -> p u t i", i=4),
+                kern[c][:, :, cols].rearrange("p t (u i) -> p u t i", i=4),
+                weights,
+                ALU.mult,
+            )
+
+        def quantize_h(c, cols):
+            quantize(h_codes[c][:, cols], h_scales[c][:, cols], h_bf[c][:, cols, :].rearrange("p j t -> p (j t)"))
+
+        coef_bf = [held("coef_bf%d" % b, [P, N, PACK], BF16) for b in range(2)]
+        coef_codes = [held("coef_codes%d" % b, [P, N], U32) for b in range(2)]
+        coef_scales = [held("coef_scales%d" % b, [P, N], U8) for b in range(2)]
+
+        def round_coef(b):
+            nc.vector.tensor_copy(
+                coef_bf[b][:].rearrange("p (u i) t -> p u t i", i=4),
+                coef_sb[b][:].rearrange("p t (u i) -> p u t i", i=4),
+            )
+
+        def quantize_coef(b):
+            quantize(coef_codes[b][:], coef_scales[b][:], coef_bf[b][:].rearrange("p n t -> p (n t)"))
+
+        def readout(dst, n_tile, s, cols):
+            rows = slice(n_tile * P, (n_tile + 1) * P)
+            for b in range(2):
+                nc.tensor.matmul_mx(
+                    out=dst,
+                    lhsT=coef_codes[b][:, rows].bitcast(FP8X4),
+                    lhsT_scale=coef_scales[b][:, rows],
+                    rhs=h_codes[b, s][:, cols].bitcast(FP8X4),
+                    rhs_scale=h_scales[b, s][:, cols],
+                    start=(b == 0),
+                    stop=(b == 1),
+                )
+
+        whole = slice(0, HALF)
+        halves = [slice(0, 256), slice(256, 512)]
+        quarters = [slice(128 * q, 128 * (q + 1)) for q in range(4)]
+
+        banks = {}
+        for s in range(2):
+            banks[0, s] = [new_bank() for t in range(PACK)]
+        for s in range(2):
+            for a in range(2):
+                for t in range(PACK):
+                    pass_a(banks[0, s][t], a, 0, t, s)
+            for t in range(PACK):
+                pass_b(banks[0, s][t], 0, t, s)
+
+        def project(b, s):
+            banks[b, s] = [new_bank() for t in range(PACK)]
+            for t in range(PACK):
+                for a in range(2):
+                    pass_a(banks[b, s][t], a, b, t, s)
+                pass_b(banks[b, s][t], b, t, s)
+
+        def laplace(c):
+            new_work(c)
+            take_abs(c, banks[c], whole)
+            for cols in halves:
+                take_exp(c, cols)
+
+        def finish_h(c):
+            for cols in halves:
+                weigh(c, cols)
+            for cols in halves:
+                quantize_h(c, cols)
+
+        round_wc(0, 1, False)
+        laplace((0, 0))
+        round_wc(1, 1, False)
+        quantize_wc(0, 1)
+        quantize_wc(1, 1)
+        laplace((0, 1))
+        project(1, 0)
+        finish_h((0, 0))
+        round_coef(0)
+        laplace((1, 0))
+        project(1, 1)
+        finish_h((0, 1))
+        round_coef(1)
+        quantize_coef(0)
+        quantize_coef(1)
+        finish_h((1, 0))
+
+        last = (1, 1)
+        new_work(last)
+        first_out = []
+        for n_tile in range(N // P):
+            bank = new_bank()
+            readout(bank[:], n_tile, 0, whole)
+            first_out.append(bank)
+        for q, cols in enumerate(quarters):
+            take_abs(last, banks[last], cols)
+            take_exp(last, cols)
+            weigh(last, cols)
+            if q > 0:
+                quantize_h(last, quarters[q - 1])
+            staged = held("staged%d" % q, [P, HALF], F32)
+            nc.scalar.copy(staged[:], first_out[q][:])
+            nc.sync.dma_start(out[q * P : (q + 1) * P, 0:HALF], staged[:])
+        quantize_h(last, quarters[3])
+        for q, cols in enumerate(quarters):
+            bank = new_bank()
+            for n_tile in range(N // P):
+                readout(bank[:, n_tile * P : (n_tile + 1) * P], n_tile, 1, cols)
+            staged = held("staged_last%d" % q, [P, HALF], F32)
+            nc.scalar.copy(staged[:], bank[:])
+            nc.sync.dma_start(
+                out[:, HALF + cols.start : HALF + cols.stop].rearrange("(a p) j -> p a j", p=P),
+                staged[:].rearrange("p (a j) -> p a j", j=P),
+            )

@@ -52,33 +52,36 @@ def tile_list_crystal_laplace_energies_kernel(
             rows = wc[a * KP : (a + 1) * KP, b * KP : (b + 1) * KP]
             nc.sync.dma_start(wc_sb[a, b][:], rows.rearrange("(p j) c -> p j c", j=PACK))
 
-        def load_plane(name, scales, first, queue):
+        def load_plane(plane, scales, first):
             passes, rows, width = scales.shape
-            plane = held(name, [P, width // 4], I32)
-            nc.vector.memset(plane[:], 0)
             for q in range(4):
                 start = 32 * q + first
-                queue.dma_start(plane[start : start + 4 * passes, :], scales[:, 4 * q : 4 * q + 4, :].bitcast(I32))
-            return plane
+                nc.sync.dma_start(plane[start : start + 4 * passes, :], scales[:, 4 * q : 4 * q + 4, :].bitcast(I32))
 
         def load_coef(b):
             coef_sb[b] = held("coef_sb%d" % b, [P, PACK, N], F32)
             nc.sync.dma_start(coef_sb[b][:], coef[b * KP : (b + 1) * KP, :].rearrange("(p j) n -> p j n", j=PACK))
 
+        tab_plane = held("tab_plane", [P, T // 4], I32)
+        tab2_plane = held("tab2_plane", [P, T2 // 4], I32)
+        wp_plane = held("wp_plane", [P, H // 4], I32)
+        for plane in (tab_plane, tab2_plane, wp_plane):
+            nc.vector.memset(plane[:], 0)
+
         nc.sync.dma_start(idx[:], offs)
-        tab_plane = load_plane("tab_plane", tab_scales, 4, nc.scalar)
-        tab2_plane = load_plane("tab2_plane", tab2_scales, 0, nc.scalar)
-        wp_plane = load_plane("wp_plane", wp_scales, 0, nc.gpsimd)
-        nc.gpsimd.dma_start(amp_sb[:], amp.rearrange("(b p t) -> p b t", b=2, t=PACK))
         tab_sb0 = load_words("tab_sb0", tab_words[0])
+        load_plane(tab_plane, tab_scales, 4)
+        nc.sync.dma_start(idx2[:], offs2)
         load_wc(0, 0)
+        load_plane(tab2_plane, tab2_scales, 0)
+        tab_sb1 = load_words("tab_sb1", tab_words[1])
+        load_wc(1, 0)
         wp_sb = held("wp_sb", [P, H // 2], I32)
         nc.sync.dma_start(wp_sb[:], wp_words[0].bitcast(I32))
-        nc.sync.dma_start(idx2[:], offs2)
-        load_wc(1, 0)
-        tab_sb1 = load_words("tab_sb1", tab_words[1])
+        load_plane(wp_plane, wp_scales, 0)
         tab2_sb = load_words("tab2_sb", tab2_words[0])
         load_wc(0, 1)
+        nc.sync.dma_start(amp_sb[:], amp.rearrange("(b p t) -> p b t", b=2, t=PACK))
         load_wc(1, 1)
         load_coef(0)
         load_coef(1)
@@ -292,7 +295,10 @@ def tile_list_crystal_laplace_energies_kernel(
             for n_tile in range(N // P):
                 readout(bank[:, n_tile * P : (n_tile + 1) * P], n_tile, 1, cols)
             staged = held("staged_last%d" % q, [P, HALF], F32)
-            nc.scalar.copy(staged[:], bank[:])
+            if q == 2:
+                nc.vector.tensor_copy(staged[:], bank[:])
+            else:
+                nc.scalar.copy(staged[:], bank[:])
             nc.sync.dma_start(
                 out[:, HALF + cols.start : HALF + cols.stop].rearrange("(a p) j -> p a j", p=P),
                 staged[:].rearrange("p (a j) -> p a j", j=P),

@@ -30,7 +30,6 @@ def tile_list_crystal_laplace_energies_kernel(
     with ExitStack() as ctx:
         lists = ctx.enter_context(tc.tile_pool(name="lists", bufs=1))
         keep = ctx.enter_context(tc.tile_pool(name="keep", bufs=1))
-        work = ctx.enter_context(tc.tile_pool(name="work", bufs=2))
         psum = ctx.enter_context(tc.psum_pool(name="psum", bufs=8))
 
         def held(name, shape, dtype):
@@ -40,7 +39,7 @@ def tile_list_crystal_laplace_energies_kernel(
         idx2 = lists.tile([P, S // 16], U16, name="idx2")
 
         wc_sb, coef_sb, wc_bf = {}, {}, {}
-        amp_sb = held("amp_sb", [P, 2, PACK], F32)
+        amp_sb = held("amp_sb", [P, 2, 8], F32)
 
         def load_words(name, words):
             dst = held(name, [P, words.shape[1]], I32)
@@ -60,7 +59,9 @@ def tile_list_crystal_laplace_energies_kernel(
 
         def load_coef(b):
             coef_sb[b] = held("coef_sb%d" % b, [P, PACK, N], F32)
-            nc.sync.dma_start(coef_sb[b][:], coef[b * KP : (b + 1) * KP, :].rearrange("(p j) n -> p j n", j=PACK))
+            rows = coef[b * KP : (b + 1) * KP, :].rearrange("(h t e) n -> t h e n", t=PACK, e=2)
+            for t in range(PACK):
+                nc.sync.dma_start(coef_sb[b][:, t, :], rows[t])
 
         tab_plane = held("tab_plane", [P, T // 4], I32)
         tab2_plane = held("tab2_plane", [P, T2 // 4], I32)
@@ -81,7 +82,8 @@ def tile_list_crystal_laplace_energies_kernel(
         load_plane(wp_plane, wp_scales, 0)
         tab2_sb = load_words("tab2_sb", tab2_words[0])
         load_wc(0, 1)
-        nc.sync.dma_start(amp_sb[:], amp.rearrange("(b p t) -> p b t", b=2, t=PACK))
+        for e in range(2):
+            nc.sync.dma_start(amp_sb[e:P:2, :, 0:7], amp.rearrange("(b h x) -> h b x", b=2, x=8)[:, :, e : e + 7])
         load_wc(1, 1)
         load_coef(0)
         load_coef(1)
@@ -101,12 +103,13 @@ def tile_list_crystal_laplace_energies_kernel(
 
         def round_wc(a, b, on_scalar):
             wc_bf[a, b] = held("wc_bf%d%d" % (a, b), [P, PACK, P, PACK], BF16)
-            dst = wc_bf[a, b][:].rearrange("p t m j -> p m j t")
-            src = wc_sb[a, b][:].rearrange("p j (m t) -> p m j t", t=PACK)
-            if on_scalar:
-                nc.scalar.activation(dst, src, ACT.Copy, scale=-1.0)
-            else:
-                nc.vector.tensor_scalar(dst, src, -1.0, None, ALU.mult)
+            dst = wc_bf[a, b][:].rearrange("p t (h e) j -> p t h j e", e=2)
+            src = wc_sb[a, b][:].rearrange("p j (h t e) -> p t h j e", t=PACK, e=2)
+            for t in range(PACK):
+                if on_scalar:
+                    nc.scalar.activation(dst[:, t], src[:, t], ACT.Copy, scale=-1.0)
+                else:
+                    nc.vector.tensor_scalar(dst[:, t], src[:, t], -1.0, None, ALU.mult)
 
         def quantize(codes, scales, grouped):
             nc.vector.quantize_mx(out=codes.bitcast(FP8X4), scales=scales, in_=grouped)
@@ -125,12 +128,12 @@ def tile_list_crystal_laplace_energies_kernel(
         quantize_wc(1, 0)
         gather(v_codes[1, 0], tab_sb1, U32, idx, 0)
         nc.vector.tensor_copy(
-            wp_codes[:].bitcast(U16).rearrange("p (b t m) -> p b m t", b=2, t=PACK),
-            wp_sb[:].bitcast(U16).rearrange("p (b m t) -> p b m t", b=2, t=PACK),
+            wp_codes[:].bitcast(I32).rearrange("p (b t h) -> p b t h", b=2, t=PACK),
+            wp_sb[:].rearrange("p (b h t) -> p b t h", b=2, t=PACK),
         )
         nc.vector.tensor_copy(
-            wp_perm_scales[:].rearrange("p (b t m) -> p b m t", b=2, t=PACK),
-            wp_plane[:].bitcast(U8).rearrange("p (b m t) -> p b m t", b=2, t=PACK),
+            wp_perm_scales[:].bitcast(U16).rearrange("p (b t h) -> p b t h", b=2, t=PACK),
+            wp_plane[:].bitcast(U16).rearrange("p (b h t) -> p b t h", b=2, t=PACK),
         )
         gather(v2_scales[0], tab2_plane, U8, idx2, 0)
         gather(v2_codes[0], tab2_sb, U32, idx2, 0)
@@ -168,28 +171,24 @@ def tile_list_crystal_laplace_energies_kernel(
             return psum.tile([P, HALF], F32, name="bank", tag="bank")
 
         chunks = [(b, s) for b in range(2) for s in range(2)]
-        dist, kern = {}, {}
+        kern = {c: held("kern%d%d" % c, [P, PACK, HALF], F32) for c in chunks}
         h_bf = {c: held("h_bf%d%d" % c, [P, HALF, PACK], BF16) for c in chunks}
         h_codes = {c: held("h_codes%d%d" % c, [P, HALF], U32) for c in chunks}
         h_scales = {c: held("h_scales%d%d" % c, [P, HALF], U8) for c in chunks}
 
-        def new_work(c):
-            dist[c] = work.tile([P, PACK, HALF], F32, name="dist", align_bytes=64)
-            kern[c] = work.tile([P, PACK, HALF], F32, name="kern", align_bytes=64)
-
         def take_abs(c, banks, cols):
             for t in range(PACK):
-                nc.scalar.activation(dist[c][:, t, cols], banks[t][:, cols], ACT.Abs)
+                nc.scalar.activation(kern[c][:, t, cols], banks[t][:, cols], ACT.Abs)
 
         def take_exp(c, cols):
-            nc.scalar.activation(kern[c][:, :, cols], dist[c][:, :, cols], ACT.Exp, scale=-1.0)
+            nc.scalar.activation(kern[c][:, :, cols], kern[c][:, :, cols], ACT.Exp, scale=-1.0)
 
         def weigh(c, cols):
-            runs = (cols.stop - cols.start) // 4
-            weights = amp_sb[:, c[0], :].unsqueeze(1).unsqueeze(3).to_broadcast([P, runs, PACK, 4])
+            runs = (cols.stop - cols.start) // 2
+            weights = amp_sb[:, c[0], 0:7:2].unsqueeze(1).unsqueeze(3).to_broadcast([P, runs, PACK, 2])
             nc.vector.tensor_tensor(
-                h_bf[c][:, cols, :].rearrange("p (u i) t -> p u t i", i=4),
-                kern[c][:, :, cols].rearrange("p t (u i) -> p u t i", i=4),
+                h_bf[c][:, cols, :].rearrange("p (u i) t -> p u t i", i=2),
+                kern[c][:, :, cols].rearrange("p t (u i) -> p u t i", i=2),
                 weights,
                 ALU.mult,
             )
@@ -203,8 +202,8 @@ def tile_list_crystal_laplace_energies_kernel(
 
         def round_coef(b):
             nc.vector.tensor_copy(
-                coef_bf[b][:].rearrange("p (u i) t -> p u t i", i=4),
-                coef_sb[b][:].rearrange("p t (u i) -> p u t i", i=4),
+                coef_bf[b][:].rearrange("p (u i) t -> p u t i", i=2),
+                coef_sb[b][:].rearrange("p t (u i) -> p u t i", i=2),
             )
 
         def quantize_coef(b):
@@ -245,7 +244,6 @@ def tile_list_crystal_laplace_energies_kernel(
                 pass_b(banks[b, s][t], b, t, s)
 
         def laplace(c):
-            new_work(c)
             take_abs(c, banks[c], whole)
             for cols in halves:
                 take_exp(c, cols)
@@ -274,7 +272,6 @@ def tile_list_crystal_laplace_energies_kernel(
         finish_h((1, 0))
 
         last = (1, 1)
-        new_work(last)
         first_out = []
         for n_tile in range(N // P):
             bank = new_bank()

@@ -17,10 +17,12 @@ ACT = mybir.ActivationFunctionType
 ALU = mybir.AluOpType
 
 P = 128
-PACK = 4
-KP = P * PACK
+SLOTS = 4
+PASS = P * SLOTS
 HALF = 512
 LIST_COLS = HALF // 16
+TAB_ROW = 4
+PAIR = 2
 
 
 def tile_list_crystal_laplace_energies_kernel(
@@ -30,38 +32,13 @@ def tile_list_crystal_laplace_energies_kernel(
     with ExitStack() as ctx:
         lists = ctx.enter_context(tc.tile_pool(name="lists", bufs=1))
         keep = ctx.enter_context(tc.tile_pool(name="keep", bufs=1))
-        psum = ctx.enter_context(tc.psum_pool(name="psum", bufs=8))
+        psum = ctx.enter_context(tc.psum_pool(name="psum", bufs=1))
 
-        def held(name, shape, dtype):
-            return keep.tile(shape, dtype, name=name, align_bytes=64)
+        def held(name, shape, dtype, tag=None):
+            return keep.tile(shape, dtype, name=name, tag=tag or name, align_bytes=64)
 
         idx = lists.tile([P, S // 16], U16, name="idx")
         idx2 = lists.tile([P, S // 16], U16, name="idx2")
-
-        wc_sb, coef_sb, wc_bf = {}, {}, {}
-        amp_sb = held("amp_sb", [P, 2, 8], F32)
-
-        def load_words(name, words):
-            dst = held(name, [P, words.shape[1]], I32)
-            nc.sync.dma_start(dst[:], words.rearrange("p t i -> p (t i)").bitcast(I32))
-            return dst
-
-        def load_wc(a, b):
-            wc_sb[a, b] = held("wc_sb%d%d" % (a, b), [P, PACK, KP], F32)
-            rows = wc[a * KP : (a + 1) * KP, b * KP : (b + 1) * KP]
-            nc.sync.dma_start(wc_sb[a, b][:], rows.rearrange("(p j) c -> p j c", j=PACK))
-
-        def load_plane(plane, scales, first):
-            passes, rows, width = scales.shape
-            for q in range(4):
-                start = 32 * q + first
-                nc.sync.dma_start(plane[start : start + 4 * passes, :], scales[:, 4 * q : 4 * q + 4, :].bitcast(I32))
-
-        def load_coef(b):
-            coef_sb[b] = held("coef_sb%d" % b, [P, PACK, N], F32)
-            rows = coef[b * KP : (b + 1) * KP, :].rearrange("(h t e) n -> t h e n", t=PACK, e=2)
-            for t in range(PACK):
-                nc.sync.dma_start(coef_sb[b][:, t, :], rows[t])
 
         tab_plane = held("tab_plane", [P, T // 4], I32)
         tab2_plane = held("tab2_plane", [P, T2 // 4], I32)
@@ -69,12 +46,37 @@ def tile_list_crystal_laplace_energies_kernel(
         for plane in (tab_plane, tab2_plane, wp_plane):
             nc.vector.memset(plane[:], 0)
 
+        def load_plane(plane, scales, first_row):
+            rows = 4 * scales.shape[0]
+            for quadrant in range(4):
+                start = 32 * quadrant + first_row
+                source = scales[:, 4 * quadrant : 4 * quadrant + 4, :]
+                nc.sync.dma_start(plane[start : start + rows, :], source.bitcast(I32))
+
+        def load_words(name, words):
+            table = held(name, [P, words.shape[1]], I32)
+            nc.sync.dma_start(table[:], words.rearrange("p t i -> p (t i)").bitcast(I32))
+            return table
+
+        wc_sb, coef_sb = {}, {}
+
+        def load_wc(a, b):
+            wc_sb[a, b] = held("wc_sb%d%d" % (a, b), [P, SLOTS, PASS], F32)
+            rows = wc[a * PASS : (a + 1) * PASS, b * PASS : (b + 1) * PASS]
+            nc.sync.dma_start(wc_sb[a, b][:], rows.rearrange("(p j) c -> p j c", j=SLOTS))
+
+        def load_coef(b):
+            coef_sb[b] = held("coef_sb%d" % b, [P, SLOTS, N], F32)
+            rows = coef[b * PASS : (b + 1) * PASS, :].rearrange("(u t e) n -> t u e n", t=SLOTS, e=2)
+            for t in range(SLOTS):
+                nc.sync.dma_start(coef_sb[b][:, t, :], rows[t])
+
         nc.sync.dma_start(idx[:], offs)
-        tab_sb0 = load_words("tab_sb0", tab_words[0])
-        load_plane(tab_plane, tab_scales, 4)
+        load_plane(tab_plane, tab_scales, TAB_ROW)
         nc.sync.dma_start(idx2[:], offs2)
-        load_wc(0, 0)
+        tab_sb0 = load_words("tab_sb0", tab_words[0])
         load_plane(tab2_plane, tab2_scales, 0)
+        load_wc(0, 0)
         tab_sb1 = load_words("tab_sb1", tab_words[1])
         load_wc(1, 0)
         wp_sb = held("wp_sb", [P, H // 2], I32)
@@ -82,138 +84,160 @@ def tile_list_crystal_laplace_energies_kernel(
         load_plane(wp_plane, wp_scales, 0)
         tab2_sb = load_words("tab2_sb", tab2_words[0])
         load_wc(0, 1)
-        for e in range(2):
-            nc.sync.dma_start(amp_sb[e:P:2, :, 0:7], amp.rearrange("(b h x) -> h b x", b=2, x=8)[:, :, e : e + 7])
         load_wc(1, 1)
+        amp_sb = held("amp_sb", [P, 2, 8], F32)
+        for e in range(2):
+            nc.sync.dma_start(amp_sb[e:P:2, :, 0:7], amp.rearrange("(b u x) -> u b x", b=2, x=8)[:, :, e : e + 7])
         load_coef(0)
         load_coef(1)
 
-        v_codes = {(a, s): held("v_codes%d%d" % (a, s), [P, HALF], U32) for a in range(2) for s in range(2)}
-        v_scales = [held("v_scales%d" % s, [P, HALF], U8) for s in range(2)]
-        v2_codes = [held("v2_codes%d" % s, [P, HALF], U32) for s in range(2)]
-        v2_scales = [held("v2_scales%d" % s, [P, HALF], U8) for s in range(2)]
-
-        def gather(dst, table, dtype, offsets, s):
+        def gather(name, table, dtype, offsets, s, tag=None):
+            picked = held(name, [P, HALF], dtype, tag)
             window = table[:].bitcast(dtype)
-            nc.vector.tensor_copy(dst[:], window.indirect(offsets[:, s * LIST_COLS : (s + 1) * LIST_COLS]))
-
-        blocks = [(a, b) for a in range(2) for b in range(2)]
-        wc_codes = {key: held("wc_codes%d%d" % key, [P, KP], U32) for key in blocks}
-        wc_scales = {key: held("wc_scales%d%d" % key, [P, KP], U8) for key in blocks}
-
-        def round_wc(a, b, on_scalar):
-            wc_bf[a, b] = held("wc_bf%d%d" % (a, b), [P, PACK, P, PACK], BF16)
-            dst = wc_bf[a, b][:].rearrange("p t (h e) j -> p t h j e", e=2)
-            src = wc_sb[a, b][:].rearrange("p j (h t e) -> p t h j e", t=PACK, e=2)
-            for t in range(PACK):
-                if on_scalar:
-                    nc.scalar.activation(dst[:, t], src[:, t], ACT.Copy, scale=-1.0)
-                else:
-                    nc.vector.tensor_scalar(dst[:, t], src[:, t], -1.0, None, ALU.mult)
+            nc.vector.tensor_copy(picked[:], window.indirect(offsets[:, s * LIST_COLS : (s + 1) * LIST_COLS]))
+            return picked
 
         def quantize(codes, scales, grouped):
             nc.vector.quantize_mx(out=codes.bitcast(FP8X4), scales=scales, in_=grouped)
 
+        wc_bf, wc_codes, wc_scales = {}, {}, {}
+
+        def round_wc(a, b, on_scalar):
+            wc_bf[a, b] = held("wc_bf%d%d" % (a, b), [P, SLOTS, P, SLOTS], BF16)
+            rounded = wc_bf[a, b][:].rearrange("p t (u e) j -> p t u j e", e=2)
+            loaded = wc_sb[a, b][:].rearrange("p j (u t e) -> p t u j e", t=SLOTS, e=2)
+            for t in range(SLOTS):
+                if on_scalar:
+                    nc.scalar.activation(rounded[:, t], loaded[:, t], ACT.Copy, scale=-1.0)
+                else:
+                    nc.vector.tensor_scalar(rounded[:, t], loaded[:, t], -1.0, None, ALU.mult)
+
         def quantize_wc(a, b):
+            wc_codes[a, b] = held("wc_codes%d%d" % (a, b), [P, PASS], U32)
+            wc_scales[a, b] = held("wc_scales%d%d" % (a, b), [P, PASS], U8)
             quantize(wc_codes[a, b][:], wc_scales[a, b][:], wc_bf[a, b][:].rearrange("p t m j -> p (t m j)"))
 
-        wp_codes = held("wp_codes", [P, 2 * H], U8)
-        wp_perm_scales = held("wp_perm_scales", [P, H], U8)
-
-        gather(v_scales[0], tab_plane, U8, idx, 0)
-        gather(v_codes[0, 0], tab_sb0, U32, idx, 0)
+        v_codes, v_scales, v2_codes, v2_scales = {}, {}, {}, {}
+        v_scales[0] = gather("v_scales0", tab_plane, U8, idx, 0)
+        v_codes[0, 0] = gather("v_codes00", tab_sb0, U32, idx, 0)
         round_wc(0, 0, True)
         quantize_wc(0, 0)
         round_wc(1, 0, True)
         quantize_wc(1, 0)
-        gather(v_codes[1, 0], tab_sb1, U32, idx, 0)
+        v_codes[1, 0] = gather("v_codes10", tab_sb1, U32, idx, 0)
+
+        wp_codes = held("wp_codes", [P, 2 * H], U8)
+        wp_sorted_scales = held("wp_sorted_scales", [P, H], U8)
         nc.vector.tensor_copy(
-            wp_codes[:].bitcast(I32).rearrange("p (b t h) -> p b t h", b=2, t=PACK),
-            wp_sb[:].rearrange("p (b h t) -> p b t h", b=2, t=PACK),
+            wp_codes[:].bitcast(I32).rearrange("p (b t u) -> p b t u", b=2, t=SLOTS),
+            wp_sb[:].rearrange("p (b u t) -> p b t u", b=2, t=SLOTS),
         )
         nc.vector.tensor_copy(
-            wp_perm_scales[:].bitcast(U16).rearrange("p (b t h) -> p b t h", b=2, t=PACK),
-            wp_plane[:].bitcast(U16).rearrange("p (b h t) -> p b t h", b=2, t=PACK),
+            wp_sorted_scales[:].bitcast(U16).rearrange("p (b t u) -> p b t u", b=2, t=SLOTS),
+            wp_plane[:].bitcast(U16).rearrange("p (b u t) -> p b t u", b=2, t=SLOTS),
         )
-        gather(v2_scales[0], tab2_plane, U8, idx2, 0)
-        gather(v2_codes[0], tab2_sb, U32, idx2, 0)
-        gather(v_scales[1], tab_plane, U8, idx, 1)
-        gather(v_codes[0, 1], tab_sb0, U32, idx, 1)
-        gather(v_codes[1, 1], tab_sb1, U32, idx, 1)
-        gather(v2_scales[1], tab2_plane, U8, idx2, 1)
-        gather(v2_codes[1], tab2_sb, U32, idx2, 1)
 
-        def pass_a(bank, a, b, t, s):
-            cols = slice(t * P, (t + 1) * P)
-            nc.tensor.matmul_mx(
-                out=bank[:],
-                lhsT=wc_codes[a, b][:, cols].bitcast(FP8X4),
-                lhsT_scale=wc_scales[a, b][:, cols],
-                rhs=v_codes[a, s][:].bitcast(FP8X4),
-                rhs_scale=v_scales[s][4 * (a + 1) : P, :],
-                start=(a == 0),
-                stop=False,
-            )
+        v2_scales[0] = gather("v2_scales0", tab2_plane, U8, idx2, 0)
+        v2_codes[0] = gather("v2_codes0", tab2_sb, U32, idx2, 0)
+        round_wc(0, 1, False)
+        round_wc(1, 1, False)
+        quantize_wc(0, 1)
+        quantize_wc(1, 1)
+        v_scales[1] = gather("v_scales1", tab_plane, U8, idx, 1)
+        v_codes[0, 1] = gather("v_codes01", tab_sb0, U32, idx, 1)
+        v_codes[1, 1] = gather("v_codes11", tab_sb1, U32, idx, 1)
+        v2_scales[1] = gather("v2_scales1", tab2_plane, U8, idx2, 1, tag="wc_sb01")
+        v2_codes[1] = gather("v2_codes1", tab2_sb, U32, idx2, 1)
 
-        def pass_b(bank, b, t, s):
-            first = b * KP + t * P
-            nc.tensor.matmul_mx(
-                out=bank[:],
-                lhsT=wp_codes[:, 2 * first : 2 * (first + P)].bitcast(FP4X4),
-                lhsT_scale=wp_perm_scales[:, first : first + P],
-                rhs=v2_codes[s][:].bitcast(FP8X4),
-                rhs_scale=v2_scales[s][:],
-                start=False,
-                stop=True,
-            )
+        def bank_tile(index):
+            return psum.tile([P, HALF], F32, name="bank%d" % index, tag="bank%d" % index)
 
-        def new_bank():
-            return psum.tile([P, HALF], F32, name="bank", tag="bank")
+        banks, kern, h_bf, h_codes, h_scales = {}, {}, {}, {}, {}
 
-        chunks = [(b, s) for b in range(2) for s in range(2)]
-        kern = {c: held("kern%d%d" % c, [P, PACK, HALF], F32) for c in chunks}
-        h_bf = {c: held("h_bf%d%d" % c, [P, HALF, PACK], BF16) for c in chunks}
-        h_codes = {c: held("h_codes%d%d" % c, [P, HALF], U32) for c in chunks}
-        h_scales = {c: held("h_scales%d%d" % c, [P, HALF], U8) for c in chunks}
+        def project(b, s, first_bank):
+            banks[b, s] = [bank_tile(first_bank + t) for t in range(SLOTS)]
+            for t in range(SLOTS):
+                cols = slice(t * P, (t + 1) * P)
+                for a in range(2):
+                    nc.tensor.matmul_mx(
+                        out=banks[b, s][t][:],
+                        lhsT=wc_codes[a, b][:, cols].bitcast(FP8X4),
+                        lhsT_scale=wc_scales[a, b][:, cols],
+                        rhs=v_codes[a, s][:].bitcast(FP8X4),
+                        rhs_scale=v_scales[s][TAB_ROW * (a + 1) : P, :],
+                        start=(a == 0),
+                        stop=False,
+                    )
+                first = b * PASS + t * P
+                nc.tensor.matmul_mx(
+                    out=banks[b, s][t][:],
+                    lhsT=wp_codes[:, 2 * first : 2 * (first + P)].bitcast(FP4X4),
+                    lhsT_scale=wp_sorted_scales[:, first : first + P],
+                    rhs=v2_codes[s][:].bitcast(FP8X4),
+                    rhs_scale=v2_scales[s][:],
+                    start=False,
+                    stop=True,
+                )
 
-        def take_abs(c, banks, cols):
-            for t in range(PACK):
-                nc.scalar.activation(kern[c][:, t, cols], banks[t][:, cols], ACT.Abs)
+        def take_abs(chunk):
+            kern[chunk] = held("kern%d%d" % chunk, [P, SLOTS, HALF], F32)
+            h_bf[chunk] = held("h_bf%d%d" % chunk, [P, HALF, SLOTS], BF16)
+            h_codes[chunk] = held("h_codes%d%d" % chunk, [P, HALF], U32)
+            h_scales[chunk] = held("h_scales%d%d" % chunk, [P, HALF], U8)
+            for t in range(SLOTS):
+                nc.scalar.activation(kern[chunk][:, t, :], banks[chunk][t][:], ACT.Abs)
 
-        def take_exp(c, cols):
-            nc.scalar.activation(kern[c][:, :, cols], kern[c][:, :, cols], ACT.Exp, scale=-1.0)
+        def take_exp(chunk, cols):
+            nc.scalar.activation(kern[chunk][:, :, cols], kern[chunk][:, :, cols], ACT.Exp, scale=-1.0)
 
-        def weigh(c, cols):
-            runs = (cols.stop - cols.start) // 2
-            weights = amp_sb[:, c[0], 0:7:2].unsqueeze(1).unsqueeze(3).to_broadcast([P, runs, PACK, 2])
+        def weigh(chunk, cols):
+            pairs = (cols.stop - cols.start) // PAIR
+            factors = amp_sb[:, chunk[0], 0:7:2].unsqueeze(1).unsqueeze(3).to_broadcast([P, pairs, SLOTS, PAIR])
             nc.vector.tensor_tensor(
-                h_bf[c][:, cols, :].rearrange("p (u i) t -> p u t i", i=2),
-                kern[c][:, :, cols].rearrange("p t (u i) -> p u t i", i=2),
-                weights,
+                h_bf[chunk][:, cols, :].rearrange("p (c i) t -> p c t i", i=PAIR),
+                kern[chunk][:, :, cols].rearrange("p t (c i) -> p c t i", i=PAIR),
+                factors,
                 ALU.mult,
             )
 
-        def quantize_h(c, cols):
-            quantize(h_codes[c][:, cols], h_scales[c][:, cols], h_bf[c][:, cols, :].rearrange("p j t -> p (j t)"))
+        def quantize_h(chunk, cols):
+            grouped = h_bf[chunk][:, cols, :].rearrange("p j t -> p (j t)")
+            quantize(h_codes[chunk][:, cols], h_scales[chunk][:, cols], grouped)
 
-        coef_bf = [held("coef_bf%d" % b, [P, N, PACK], BF16) for b in range(2)]
-        coef_codes = [held("coef_codes%d" % b, [P, N], U32) for b in range(2)]
-        coef_scales = [held("coef_scales%d" % b, [P, N], U8) for b in range(2)]
+        def pieces(count):
+            width = HALF // count
+            return [slice(i * width, (i + 1) * width) for i in range(count)]
+
+        def laplace(chunk):
+            take_abs(chunk)
+            for cols in pieces(2):
+                take_exp(chunk, cols)
+
+        def finish_h(chunk):
+            for cols in pieces(2):
+                weigh(chunk, cols)
+            for cols in pieces(2):
+                quantize_h(chunk, cols)
+
+        coef_bf, coef_codes, coef_scales = {}, {}, {}
 
         def round_coef(b):
+            coef_bf[b] = held("coef_bf%d" % b, [P, N, SLOTS], BF16)
             nc.vector.tensor_copy(
-                coef_bf[b][:].rearrange("p (u i) t -> p u t i", i=2),
-                coef_sb[b][:].rearrange("p t (u i) -> p u t i", i=2),
+                coef_bf[b][:].rearrange("p (c i) t -> p c t i", i=PAIR),
+                coef_sb[b][:].rearrange("p t (c i) -> p c t i", i=PAIR),
             )
 
         def quantize_coef(b):
+            coef_codes[b] = held("coef_codes%d" % b, [P, N], U32)
+            coef_scales[b] = held("coef_scales%d" % b, [P, N], U8)
             quantize(coef_codes[b][:], coef_scales[b][:], coef_bf[b][:].rearrange("p n t -> p (n t)"))
 
-        def readout(dst, n_tile, s, cols):
+        def readout(sums, n_tile, s, cols):
             rows = slice(n_tile * P, (n_tile + 1) * P)
             for b in range(2):
                 nc.tensor.matmul_mx(
-                    out=dst,
+                    out=sums,
                     lhsT=coef_codes[b][:, rows].bitcast(FP8X4),
                     lhsT_scale=coef_scales[b][:, rows],
                     rhs=h_codes[b, s][:, cols].bitcast(FP8X4),
@@ -222,81 +246,45 @@ def tile_list_crystal_laplace_energies_kernel(
                     stop=(b == 1),
                 )
 
-        whole = slice(0, HALF)
-        halves = [slice(0, 256), slice(256, 512)]
-        quarters = [slice(128 * q, 128 * (q + 1)) for q in range(4)]
+        def store(name, bank, target, copy):
+            staged = held(name, [P, HALF], F32)
+            copy(staged[:], bank[:])
+            nc.sync.dma_start(target, staged[:].rearrange("p (a j) -> p a j", a=target.shape[1]))
 
-        banks = {}
-        for s in range(2):
-            banks[0, s] = [new_bank() for t in range(PACK)]
-        for s in range(2):
-            for a in range(2):
-                for t in range(PACK):
-                    pass_a(banks[0, s][t], a, 0, t, s)
-            for t in range(PACK):
-                pass_b(banks[0, s][t], 0, t, s)
-
-        def project(b, s):
-            banks[b, s] = [new_bank() for t in range(PACK)]
-            for t in range(PACK):
-                for a in range(2):
-                    pass_a(banks[b, s][t], a, b, t, s)
-                pass_b(banks[b, s][t], b, t, s)
-
-        def laplace(c):
-            take_abs(c, banks[c], whole)
-            for cols in halves:
-                take_exp(c, cols)
-
-        def finish_h(c):
-            for cols in halves:
-                weigh(c, cols)
-            for cols in halves:
-                quantize_h(c, cols)
-
-        round_wc(0, 1, False)
+        project(0, 0, 0)
+        project(1, 0, SLOTS)
         laplace((0, 0))
-        round_wc(1, 1, False)
-        quantize_wc(0, 1)
-        quantize_wc(1, 1)
-        laplace((0, 1))
-        project(1, 0)
+        laplace((1, 0))
+        project(0, 1, 0)
         finish_h((0, 0))
         round_coef(0)
-        laplace((1, 0))
-        project(1, 1)
-        finish_h((0, 1))
         round_coef(1)
         quantize_coef(0)
-        quantize_coef(1)
         finish_h((1, 0))
+        quantize_coef(1)
+        laplace((0, 1))
+        project(1, 1, SLOTS)
+        first_out = [bank_tile(n_tile) for n_tile in range(N // P)]
+        for n_tile in range(N // P):
+            readout(first_out[n_tile][:], n_tile, 0, slice(0, HALF))
+        finish_h((0, 1))
 
         last = (1, 1)
-        first_out = []
-        for n_tile in range(N // P):
-            bank = new_bank()
-            readout(bank[:], n_tile, 0, whole)
-            first_out.append(bank)
+        quarters = pieces(4)
+        take_abs(last)
         for q, cols in enumerate(quarters):
-            take_abs(last, banks[last], cols)
             take_exp(last, cols)
             weigh(last, cols)
             if q > 0:
                 quantize_h(last, quarters[q - 1])
-            staged = held("staged%d" % q, [P, HALF], F32)
-            nc.scalar.copy(staged[:], first_out[q][:])
-            nc.sync.dma_start(out[q * P : (q + 1) * P, 0:HALF], staged[:])
-        quantize_h(last, quarters[3])
+        quantize_h(last, quarters[-1])
+
+        out_tiles = out.rearrange("(a p) j -> p a j", p=P)
+        for n_tile in range(N // P):
+            store("first%d" % n_tile, first_out[n_tile], out_tiles[:, n_tile : n_tile + 1, 0:HALF], nc.scalar.copy)
         for q, cols in enumerate(quarters):
-            bank = new_bank()
+            bank = bank_tile(SLOTS + q)
             for n_tile in range(N // P):
                 readout(bank[:, n_tile * P : (n_tile + 1) * P], n_tile, 1, cols)
-            staged = held("staged_last%d" % q, [P, HALF], F32)
-            if q == 2:
-                nc.vector.tensor_copy(staged[:], bank[:])
-            else:
-                nc.scalar.copy(staged[:], bank[:])
-            nc.sync.dma_start(
-                out[:, HALF + cols.start : HALF + cols.stop].rearrange("(a p) j -> p a j", p=P),
-                staged[:].rearrange("p (a j) -> p a j", j=P),
-            )
+            copy = nc.vector.tensor_copy if q == len(quarters) - 2 else nc.scalar.copy
+            store("last%d" % q, bank, out_tiles[:, :, HALF + cols.start : HALF + cols.stop], copy)

@@ -43,8 +43,9 @@ def tile_list_crystal_laplace_energies_kernel(
         tab_plane = held("tab_plane", [P, T // 4], I32)
         tab2_plane = held("tab2_plane", [P, T2 // 4], I32)
         wp_plane = held("wp_plane", [P, H // 4], I32)
-        for plane in (tab_plane, tab2_plane, wp_plane):
-            nc.vector.memset(plane[:], 0)
+        nc.gpsimd.memset(tab_plane[:], 0)
+        nc.vector.memset(tab2_plane[:], 0)
+        nc.vector.memset(wp_plane[:], 0)
 
         def load_plane(plane, scales, first_row):
             rows = 4 * scales.shape[0]
@@ -72,24 +73,24 @@ def tile_list_crystal_laplace_energies_kernel(
                 nc.sync.dma_start(coef_sb[b][:, t, :], rows[t])
 
         nc.sync.dma_start(idx[:], offs)
-        load_plane(tab_plane, tab_scales, TAB_ROW)
-        nc.sync.dma_start(idx2[:], offs2)
-        tab_sb0 = load_words("tab_sb0", tab_words[0])
         load_plane(tab2_plane, tab2_scales, 0)
-        load_wc(0, 0)
-        tab_sb1 = load_words("tab_sb1", tab_words[1])
-        load_wc(1, 0)
         wp_sb = held("wp_sb", [P, H // 2], I32)
         nc.sync.dma_start(wp_sb[:], wp_words[0].bitcast(I32))
+        nc.sync.dma_start(idx2[:], offs2)
+        tab_sb0 = load_words("tab_sb0", tab_words[0])
+        load_plane(tab_plane, tab_scales, TAB_ROW)
+        load_wc(0, 0)
         load_plane(wp_plane, wp_scales, 0)
+        tab_sb1 = load_words("tab_sb1", tab_words[1])
+        load_wc(1, 0)
         tab2_sb = load_words("tab2_sb", tab2_words[0])
         load_wc(0, 1)
         load_wc(1, 1)
+        load_coef(1)
         amp_sb = held("amp_sb", [P, 2, 8], F32)
         for e in range(2):
             nc.sync.dma_start(amp_sb[e:P:2, :, 0:7], amp.rearrange("(b u x) -> u b x", b=2, x=8)[:, :, e : e + 7])
         load_coef(0)
-        load_coef(1)
 
         def gather(name, table, dtype, offsets, s, tag=None):
             picked = held(name, [P, HALF], dtype, tag)
@@ -145,8 +146,8 @@ def tile_list_crystal_laplace_energies_kernel(
         quantize_wc(1, 1)
         v_scales[1] = gather("v_scales1", tab_plane, U8, idx, 1)
         v_codes[0, 1] = gather("v_codes01", tab_sb0, U32, idx, 1)
-        v_codes[1, 1] = gather("v_codes11", tab_sb1, U32, idx, 1)
-        v2_scales[1] = gather("v2_scales1", tab2_plane, U8, idx2, 1, tag="wc_sb01")
+        v_codes[1, 1] = gather("v_codes11", tab_sb1, U32, idx, 1, tag="wc_sb01")
+        v2_scales[1] = gather("v2_scales1", tab2_plane, U8, idx2, 1)
         v2_codes[1] = gather("v2_codes1", tab2_sb, U32, idx2, 1)
 
         def bank_tile(index):
@@ -246,9 +247,9 @@ def tile_list_crystal_laplace_energies_kernel(
                     stop=(b == 1),
                 )
 
-        def store(name, bank, target, copy):
+        def store(name, bank, target):
             staged = held(name, [P, HALF], F32)
-            copy(staged[:], bank[:])
+            nc.scalar.copy(staged[:], bank[:])
             nc.sync.dma_start(target, staged[:].rearrange("p (a j) -> p a j", a=target.shape[1]))
 
         project(0, 0, 0)
@@ -281,10 +282,9 @@ def tile_list_crystal_laplace_energies_kernel(
 
         out_tiles = out.rearrange("(a p) j -> p a j", p=P)
         for n_tile in range(N // P):
-            store("first%d" % n_tile, first_out[n_tile], out_tiles[:, n_tile : n_tile + 1, 0:HALF], nc.scalar.copy)
+            store("first%d" % n_tile, first_out[n_tile], out_tiles[:, n_tile : n_tile + 1, 0:HALF])
         for q, cols in enumerate(quarters):
             bank = bank_tile(SLOTS + q)
             for n_tile in range(N // P):
                 readout(bank[:, n_tile * P : (n_tile + 1) * P], n_tile, 1, cols)
-            copy = nc.vector.tensor_copy if q == len(quarters) - 2 else nc.scalar.copy
-            store("last%d" % q, bank, out_tiles[:, :, HALF + cols.start : HALF + cols.stop], copy)
+            store("last%d" % q, bank, out_tiles[:, :, HALF + cols.start : HALF + cols.stop])

@@ -1,3 +1,4 @@
+import math
 from contextlib import ExitStack
 
 import concourse.mybir as mybir
@@ -22,6 +23,7 @@ PASS = P * SLOTS
 HALF = 512
 LIST_COLS = HALF // 16
 TAB_ROW = 4
+RUN = 4
 PAIR = 2
 
 
@@ -43,8 +45,8 @@ def tile_list_crystal_laplace_energies_kernel(
         tab_plane = held("tab_plane", [P, T // 4], I32)
         tab2_plane = held("tab2_plane", [P, T2 // 4], I32)
         wp_plane = held("wp_plane", [P, H // 4], I32)
-        nc.gpsimd.memset(tab_plane[:], 0)
-        nc.vector.memset(tab2_plane[:], 0)
+        nc.vector.memset(tab_plane[:], 0)
+        nc.gpsimd.memset(tab2_plane[:], 0)
         nc.vector.memset(wp_plane[:], 0)
 
         def load_plane(plane, scales, first_row):
@@ -72,25 +74,43 @@ def tile_list_crystal_laplace_energies_kernel(
             for t in range(SLOTS):
                 nc.sync.dma_start(coef_sb[b][:, t, :], rows[t])
 
+        amp_sb = held("amp_sb", [P, 2, 8], F32)
+
+        def load_amp(e):
+            nc.sync.dma_start(amp_sb[e:P:2, :, 0:7], amp.rearrange("(b u x) -> u b x", b=2, x=8)[:, :, e : e + 7])
+
         nc.sync.dma_start(idx[:], offs)
+        load_amp(0)
+        load_amp(1)
+        load_plane(tab_plane, tab_scales, TAB_ROW)
+        tab_sb0 = load_words("tab_sb0", tab_words[0])
+        tab_sb1 = load_words("tab_sb1", tab_words[1])
+        nc.sync.dma_start(idx2[:], offs2)
         load_plane(tab2_plane, tab2_scales, 0)
+        tab2_sb = load_words("tab2_sb", tab2_words[0])
         wp_sb = held("wp_sb", [P, H // 2], I32)
         nc.sync.dma_start(wp_sb[:], wp_words[0].bitcast(I32))
-        nc.sync.dma_start(idx2[:], offs2)
-        tab_sb0 = load_words("tab_sb0", tab_words[0])
-        load_plane(tab_plane, tab_scales, TAB_ROW)
-        load_wc(0, 0)
         load_plane(wp_plane, wp_scales, 0)
-        tab_sb1 = load_words("tab_sb1", tab_words[1])
+        load_wc(0, 0)
         load_wc(1, 0)
-        tab2_sb = load_words("tab2_sb", tab2_words[0])
         load_wc(0, 1)
         load_wc(1, 1)
-        load_coef(1)
-        amp_sb = held("amp_sb", [P, 2, 8], F32)
-        for e in range(2):
-            nc.sync.dma_start(amp_sb[e:P:2, :, 0:7], amp.rearrange("(b u x) -> u b x", b=2, x=8)[:, :, e : e + 7])
         load_coef(0)
+        load_coef(1)
+
+        amp_bits = amp_sb[:].bitcast(I32)[:, :, 0:7:2]
+        biased_exponent = held("biased_exponent", [P, 2, SLOTS], I32)
+        mantissa = held("mantissa", [P, 2, SLOTS], I32)
+        log_power = held("log_power", [P, 2, SLOTS], F32)
+        log_mantissa = held("log_mantissa", [P, 2, SLOTS], F32)
+        log_amp = held("log_amp", [P, 2, SLOTS], F32)
+        nc.vector.tensor_scalar(biased_exponent[:], amp_bits, 23, None, ALU.logical_shift_right)
+        nc.vector.tensor_scalar(mantissa[:], amp_bits, 0x007FFFFF, 0x3F800000, ALU.bitwise_and, ALU.bitwise_or)
+        nc.vector.tensor_scalar(log_power[:], biased_exponent[:], -127.0, math.log(2.0), ALU.add, ALU.mult)
+        nc.scalar.activation(log_mantissa[:], mantissa[:].bitcast(F32), ACT.Ln)
+        nc.gpsimd.tensor_tensor(log_amp[:], log_mantissa[:], log_power[:], ALU.add)
+        exp_warm_up = held("exp_warm_up", [P, 1], F32)
+        nc.scalar.activation(exp_warm_up[:], log_mantissa[:, 0, 0:1], ACT.Exp)
 
         def gather(name, table, dtype, offsets, s, tag=None):
             picked = held(name, [P, HALF], dtype, tag)
@@ -103,29 +123,42 @@ def tile_list_crystal_laplace_energies_kernel(
 
         wc_bf, wc_codes, wc_scales = {}, {}, {}
 
-        def round_wc(a, b, on_scalar):
+        def wc_tiles(a, b):
             wc_bf[a, b] = held("wc_bf%d%d" % (a, b), [P, SLOTS, P, SLOTS], BF16)
-            rounded = wc_bf[a, b][:].rearrange("p t (u e) j -> p t u j e", e=2)
-            loaded = wc_sb[a, b][:].rearrange("p j (u t e) -> p t u j e", t=SLOTS, e=2)
-            for t in range(SLOTS):
-                if on_scalar:
-                    nc.scalar.activation(rounded[:, t], loaded[:, t], ACT.Copy, scale=-1.0)
-                else:
-                    nc.vector.tensor_scalar(rounded[:, t], loaded[:, t], -1.0, None, ALU.mult)
-
-        def quantize_wc(a, b):
             wc_codes[a, b] = held("wc_codes%d%d" % (a, b), [P, PASS], U32)
             wc_scales[a, b] = held("wc_scales%d%d" % (a, b), [P, PASS], U8)
-            quantize(wc_codes[a, b][:], wc_scales[a, b][:], wc_bf[a, b][:].rearrange("p t m j -> p (t m j)"))
+
+        def round_wc(a, b, t, on_scalar):
+            rounded = wc_bf[a, b][:].rearrange("p t (u e) j -> p t u j e", e=2)
+            loaded = wc_sb[a, b][:].rearrange("p j (u t e) -> p t u j e", t=SLOTS, e=2)
+            if on_scalar:
+                nc.scalar.activation(rounded[:, t], loaded[:, t], ACT.Copy, scale=-1.0)
+            else:
+                nc.vector.tensor_scalar(rounded[:, t], loaded[:, t], -1.0, None, ALU.mult)
+
+        def quantize_wc(a, b, first, last):
+            cols = slice(first * P, last * P)
+            grouped = wc_bf[a, b][:, first:last].rearrange("p t m j -> p (t m j)")
+            quantize(wc_codes[a, b][:, cols], wc_scales[a, b][:, cols], grouped)
+
+        def prepare_wc(a, b, scalar_slots, width):
+            wc_tiles(a, b)
+            for t in range(SLOTS):
+                round_wc(a, b, t, t in scalar_slots)
+            for first in range(0, SLOTS, width):
+                quantize_wc(a, b, first, first + width)
 
         v_codes, v_scales, v2_codes, v2_scales = {}, {}, {}, {}
-        v_scales[0] = gather("v_scales0", tab_plane, U8, idx, 0)
-        v_codes[0, 0] = gather("v_codes00", tab_sb0, U32, idx, 0)
-        round_wc(0, 0, True)
-        quantize_wc(0, 0)
-        round_wc(1, 0, True)
-        quantize_wc(1, 0)
-        v_codes[1, 0] = gather("v_codes10", tab_sb1, U32, idx, 0)
+        for s in range(2):
+            v_scales[s] = gather("v_scales%d" % s, tab_plane, U8, idx, s)
+        for s in range(2):
+            v_codes[0, s] = gather("v_codes0%d" % s, tab_sb0, U32, idx, s)
+        for s in range(2):
+            v_codes[1, s] = gather("v_codes1%d" % s, tab_sb1, U32, idx, s)
+        for s in range(2):
+            v2_scales[s] = gather("v2_scales%d" % s, tab2_plane, U8, idx2, s)
+        for s in range(2):
+            v2_codes[s] = gather("v2_codes%d" % s, tab2_sb, U32, idx2, s)
 
         wp_codes = held("wp_codes", [P, 2 * H], U8)
         wp_sorted_scales = held("wp_sorted_scales", [P, H], U8)
@@ -138,87 +171,118 @@ def tile_list_crystal_laplace_energies_kernel(
             wp_plane[:].bitcast(U16).rearrange("p (b u t) -> p b t u", b=2, t=SLOTS),
         )
 
-        v2_scales[0] = gather("v2_scales0", tab2_plane, U8, idx2, 0)
-        v2_codes[0] = gather("v2_codes0", tab2_sb, U32, idx2, 0)
-        round_wc(0, 1, False)
-        round_wc(1, 1, False)
-        quantize_wc(0, 1)
-        quantize_wc(1, 1)
-        v_scales[1] = gather("v_scales1", tab_plane, U8, idx, 1)
-        v_codes[0, 1] = gather("v_codes01", tab_sb0, U32, idx, 1)
-        v_codes[1, 1] = gather("v_codes11", tab_sb1, U32, idx, 1, tag="wc_sb01")
-        v2_scales[1] = gather("v2_scales1", tab2_plane, U8, idx2, 1)
-        v2_codes[1] = gather("v2_codes1", tab2_sb, U32, idx2, 1)
+        prepare_wc(0, 0, range(SLOTS), 1)
+        wc_tiles(1, 0)
+        for t in range(SLOTS):
+            round_wc(1, 0, t, t >= 2)
+            if t > 0:
+                quantize_wc(1, 0, t - 1, t)
+        quantize_wc(1, 0, SLOTS - 1, SLOTS)
+        prepare_wc(0, 1, (), SLOTS)
+        wc_tiles(1, 1)
+        for t in range(SLOTS):
+            round_wc(1, 1, t, False)
+            if t > 0:
+                quantize_wc(1, 1, t - 1, t)
+        quantize_wc(1, 1, SLOTS - 1, SLOTS)
 
         def bank_tile(index):
             return psum.tile([P, HALF], F32, name="bank%d" % index, tag="bank%d" % index)
 
-        banks, kern, h_bf, h_codes, h_scales = {}, {}, {}, {}, {}
+        h_codes = {(b, s): held("h_codes%d%d" % (b, s), [P, HALF], U32) for b in range(2) for s in range(2)}
+        h_scales = {(b, s): held("h_scales%d%d" % (b, s), [P, HALF], U8) for b in range(2) for s in range(2)}
 
-        def project(b, s, first_bank):
-            banks[b, s] = [bank_tile(first_bank + t) for t in range(SLOTS)]
-            for t in range(SLOTS):
-                cols = slice(t * P, (t + 1) * P)
-                for a in range(2):
-                    nc.tensor.matmul_mx(
-                        out=banks[b, s][t][:],
-                        lhsT=wc_codes[a, b][:, cols].bitcast(FP8X4),
-                        lhsT_scale=wc_scales[a, b][:, cols],
-                        rhs=v_codes[a, s][:].bitcast(FP8X4),
-                        rhs_scale=v_scales[s][TAB_ROW * (a + 1) : P, :],
-                        start=(a == 0),
-                        stop=False,
-                    )
-                first = b * PASS + t * P
-                nc.tensor.matmul_mx(
-                    out=banks[b, s][t][:],
-                    lhsT=wp_codes[:, 2 * first : 2 * (first + P)].bitcast(FP4X4),
-                    lhsT_scale=wp_sorted_scales[:, first : first + P],
-                    rhs=v2_codes[s][:].bitcast(FP8X4),
-                    rhs_scale=v2_scales[s][:],
-                    start=False,
-                    stop=True,
-                )
+        def pieces(cols, width):
+            return [slice(first, first + width) for first in range(cols.start, cols.stop, width)]
 
-        def take_abs(chunk):
-            kern[chunk] = held("kern%d%d" % chunk, [P, SLOTS, HALF], F32)
-            h_bf[chunk] = held("h_bf%d%d" % chunk, [P, HALF, SLOTS], BF16)
-            h_codes[chunk] = held("h_codes%d%d" % chunk, [P, HALF], U32)
-            h_scales[chunk] = held("h_scales%d%d" % chunk, [P, HALF], U8)
-            for t in range(SLOTS):
-                nc.scalar.activation(kern[chunk][:, t, :], banks[chunk][t][:], ACT.Abs)
-
-        def take_exp(chunk, cols):
-            nc.scalar.activation(kern[chunk][:, :, cols], kern[chunk][:, :, cols], ACT.Exp, scale=-1.0)
-
-        def weigh(chunk, cols):
-            pairs = (cols.stop - cols.start) // PAIR
-            factors = amp_sb[:, chunk[0], 0:7:2].unsqueeze(1).unsqueeze(3).to_broadcast([P, pairs, SLOTS, PAIR])
-            nc.vector.tensor_tensor(
-                h_bf[chunk][:, cols, :].rearrange("p (c i) t -> p c t i", i=PAIR),
-                kern[chunk][:, :, cols].rearrange("p t (c i) -> p c t i", i=PAIR),
-                factors,
-                ALU.mult,
+        def crystal_pass(sums, b, s, t, a, cols, start, stop):
+            rows = slice(t * P, (t + 1) * P)
+            nc.tensor.matmul_mx(
+                out=sums,
+                lhsT=wc_codes[a, b][:, rows].bitcast(FP8X4),
+                lhsT_scale=wc_scales[a, b][:, rows],
+                rhs=v_codes[a, s][:, cols].bitcast(FP8X4),
+                rhs_scale=v_scales[s][TAB_ROW * (a + 1) : P, cols],
+                start=start,
+                stop=stop,
             )
 
-        def quantize_h(chunk, cols):
-            grouped = h_bf[chunk][:, cols, :].rearrange("p j t -> p (j t)")
-            quantize(h_codes[chunk][:, cols], h_scales[chunk][:, cols], grouped)
+        def prototype_pass(sums, b, s, t, cols, start, stop):
+            first = b * PASS + t * P
+            nc.tensor.matmul_mx(
+                out=sums,
+                lhsT=wp_codes[:, 2 * first : 2 * (first + P)].bitcast(FP4X4),
+                lhsT_scale=wp_sorted_scales[:, first : first + P],
+                rhs=v2_codes[s][:, cols].bitcast(FP8X4),
+                rhs_scale=v2_scales[s][:, cols],
+                start=start,
+                stop=stop,
+            )
 
-        def pieces(count):
-            width = HALF // count
-            return [slice(i * width, (i + 1) * width) for i in range(count)]
+        def project_wide(b, s):
+            banks = [bank_tile(t) for t in range(SLOTS)]
+            for t in range(SLOTS):
+                prototype_pass(banks[t][:], b, s, t, whole, True, False)
+                for a in range(2):
+                    crystal_pass(banks[t][:], b, s, t, a, whole, False, a == 1)
+            return banks
 
-        def laplace(chunk):
-            take_abs(chunk)
-            for cols in pieces(2):
-                take_exp(chunk, cols)
+        def project_narrow(b, s, cols):
+            banks = [bank_tile(2 * b + pair) for pair in range(2)]
+            width = cols.stop - cols.start
+            for t in range(SLOTS):
+                first = (t % 2) * width
+                for a in range(2):
+                    crystal_pass(banks[t // 2][:, first : first + width], b, s, t, a, cols, a == 0, False)
+                parts = pieces(cols, P)
+                for i, part in enumerate(parts):
+                    sums = banks[t // 2][:, first + i * P : first + (i + 1) * P]
+                    prototype_pass(sums, b, s, t, part, False, i == len(parts) - 1)
+            return banks
 
-        def finish_h(chunk):
-            for cols in pieces(2):
-                weigh(chunk, cols)
-            for cols in pieces(2):
-                quantize_h(chunk, cols)
+        def chunk_tiles(name, width, tag=None):
+            dist = held("dist" + name, [P, SLOTS * width], F32)
+            h_slots = held("h_slots" + name, [P, SLOTS, width], BF16)
+            h_bf = held("h_bf" + name, [P, width, SLOTS], BF16, tag)
+            return dist, h_slots, h_bf
+
+        def take_abs(tiles, banks, i):
+            nc.scalar.activation(tiles[0][:, i * HALF : (i + 1) * HALF], banks[i][:], ACT.Abs)
+
+        def take_exp(tiles, b, t, cols):
+            dist = tiles[0][:].rearrange("p (t j) -> p t j", t=SLOTS)
+            nc.scalar.activation(tiles[1][:, t, cols], dist[:, t, cols], ACT.Exp, bias=log_amp[:, b, t : t + 1], scale=-1.0)
+
+        def interleave(tiles, cols):
+            nc.vector.tensor_copy(
+                tiles[2][:, cols, :].rearrange("p (c i) t -> p c t i", i=RUN),
+                tiles[1][:, :, cols].rearrange("p t (c i) -> p c t i", i=RUN),
+            )
+
+        def quantize_h(tiles, cols, b, s, first):
+            target = slice(first + cols.start, first + cols.stop)
+            grouped = tiles[2][:, cols, :].rearrange("p j t -> p (j t)")
+            quantize(h_codes[b, s][:, target], h_scales[b, s][:, target], grouped)
+
+        def laplace(tiles, banks, b):
+            width = tiles[1].shape[2]
+            slots_a_bank = SLOTS // len(banks)
+            for i in range(len(banks) + 1):
+                if i < len(banks):
+                    take_abs(tiles, banks, i)
+                if i > 0:
+                    for t in range((i - 1) * slots_a_bank, i * slots_a_bank):
+                        take_exp(tiles, b, t, slice(0, width))
+
+        def finish_h(tiles, b, s, first):
+            width = tiles[1].shape[2]
+            halves = pieces(slice(0, width), HALF // 2)
+            for cols in halves:
+                interleave(tiles, cols)
+            for cols in halves:
+                quantize_h(tiles, cols, b, s, first)
+
+        whole = slice(0, HALF)
 
         coef_bf, coef_codes, coef_scales = {}, {}, {}
 
@@ -234,57 +298,91 @@ def tile_list_crystal_laplace_energies_kernel(
             coef_scales[b] = held("coef_scales%d" % b, [P, N], U8)
             quantize(coef_codes[b][:], coef_scales[b][:], coef_bf[b][:].rearrange("p n t -> p (n t)"))
 
-        def readout(sums, n_tile, s, cols):
+        def readout_pass(sums, n_tile, b, s, cols):
             rows = slice(n_tile * P, (n_tile + 1) * P)
-            for b in range(2):
-                nc.tensor.matmul_mx(
-                    out=sums,
-                    lhsT=coef_codes[b][:, rows].bitcast(FP8X4),
-                    lhsT_scale=coef_scales[b][:, rows],
-                    rhs=h_codes[b, s][:, cols].bitcast(FP8X4),
-                    rhs_scale=h_scales[b, s][:, cols],
-                    start=(b == 0),
-                    stop=(b == 1),
-                )
+            nc.tensor.matmul_mx(
+                out=sums,
+                lhsT=coef_codes[b][:, rows].bitcast(FP8X4),
+                lhsT_scale=coef_scales[b][:, rows],
+                rhs=h_codes[b, s][:, cols].bitcast(FP8X4),
+                rhs_scale=h_scales[b, s][:, cols],
+                start=(b == 0),
+                stop=(b == 1),
+            )
 
-        def store(name, bank, target):
+        def copy_out(target, source, on_scalar):
+            if on_scalar:
+                nc.scalar.copy(target, source)
+            else:
+                nc.vector.tensor_copy(target, source)
+
+        def store(name, bank, target, on_scalar):
             staged = held(name, [P, HALF], F32)
-            nc.scalar.copy(staged[:], bank[:])
+            copy_out(staged[:], bank[:], on_scalar)
             nc.sync.dma_start(target, staged[:].rearrange("p (a j) -> p a j", a=target.shape[1]))
 
-        project(0, 0, 0)
-        project(1, 0, SLOTS)
-        laplace((0, 0))
-        laplace((1, 0))
-        project(0, 1, 0)
-        finish_h((0, 0))
+        out_tiles = out.rearrange("(a p) j -> p a j", p=P)
+        n_tiles = range(N // P)
+
+        wide = [chunk_tiles("00", HALF, "wc_bf11"), chunk_tiles("10", HALF)]
+        for b in range(2):
+            laplace(wide[b], project_wide(b, 0), b)
+        finish_h(wide[0], 0, 0, 0)
         round_coef(0)
         round_coef(1)
         quantize_coef(0)
-        finish_h((1, 0))
         quantize_coef(1)
-        laplace((0, 1))
-        project(1, 1, SLOTS)
-        first_out = [bank_tile(n_tile) for n_tile in range(N // P)]
-        for n_tile in range(N // P):
-            readout(first_out[n_tile][:], n_tile, 0, slice(0, HALF))
-        finish_h((0, 1))
+        finish_h(wide[1], 1, 0, 0)
+        first_out = [bank_tile(SLOTS + n_tile) for n_tile in n_tiles]
+        for n_tile in n_tiles:
+            for b in range(2):
+                readout_pass(first_out[n_tile][:], n_tile, b, 0, whole)
 
-        last = (1, 1)
-        quarters = pieces(4)
-        take_abs(last)
-        for q, cols in enumerate(quarters):
-            take_exp(last, cols)
-            weigh(last, cols)
-            if q > 0:
-                quantize_h(last, quarters[q - 1])
-        quantize_h(last, quarters[-1])
+        early, late = pieces(whole, HALF // 2)
+        narrow = {}
+        for b in range(2):
+            narrow[b] = chunk_tiles("e%d" % b, HALF // 2)
+            laplace(narrow[b], project_narrow(b, 1, early), b)
+        finish_h(narrow[0], 0, 1, early.start)
+        for n_tile in n_tiles:
+            store("first%d" % n_tile, first_out[n_tile], out_tiles[:, n_tile : n_tile + 1, 0:HALF], False)
+        finish_h(narrow[1], 1, 1, early.start)
+        late_first = chunk_tiles("l0", HALF // 2)
+        laplace(late_first, project_narrow(0, 1, late), 0)
+        last = chunk_tiles("l1", HALF // 2)
+        last_banks = project_narrow(1, 1, late)
+        early_out = [bank_tile(SLOTS + pair) for pair in range(2)]
+        for n_tile in n_tiles:
+            for b in range(2):
+                first = (n_tile % 2) * (HALF // 2)
+                readout_pass(early_out[n_tile // 2][:, first : first + HALF // 2], n_tile, b, 1, early)
+        finish_h(late_first, 0, 1, late.start)
 
-        out_tiles = out.rearrange("(a p) j -> p a j", p=P)
-        for n_tile in range(N // P):
-            store("first%d" % n_tile, first_out[n_tile], out_tiles[:, n_tile : n_tile + 1, 0:HALF])
-        for q, cols in enumerate(quarters):
-            bank = bank_tile(SLOTS + q)
-            for n_tile in range(N // P):
-                readout(bank[:, n_tile * P : (n_tile + 1) * P], n_tile, 1, cols)
-            store("last%d" % q, bank, out_tiles[:, :, HALF + cols.start : HALF + cols.stop])
+        for i in range(2):
+            take_abs(last, last_banks, i)
+        ends = pieces(slice(0, HALF // 2), P)
+        final_cols = slice(HALF - P, HALF)
+        final_out = [bank_tile(index) for index in (0, 1, 7, 2)]
+        for n_tile in n_tiles:
+            readout_pass(final_out[n_tile][:, 0:P], n_tile, 0, 1, final_cols)
+        for t in range(SLOTS):
+            take_exp(last, 1, t, ends[0])
+        interleave(last, ends[0])
+        quantize_h(last, ends[0], 1, 1, late.start)
+        for t in range(SLOTS):
+            take_exp(last, 1, t, ends[1])
+        interleave(last, ends[1])
+        quantize_h(last, ends[1], 1, 1, late.start)
+        store("early0", early_out[0], out_tiles[:, 0:2, HALF + early.start : HALF + early.stop], True)
+        store("early1", early_out[1], out_tiles[:, 2:4, HALF + early.start : HALF + early.stop], True)
+
+        bank = bank_tile(6)
+        for n_tile in n_tiles:
+            for b in range(2):
+                readout_pass(bank[:, n_tile * P : (n_tile + 1) * P], n_tile, b, 1, slice(late.start, late.start + P))
+        store("late", bank, out_tiles[:, :, HALF + late.start : HALF + late.start + P], True)
+        final_staged = held("final_staged", [P, N // P, P], F32)
+        for n_tile in n_tiles:
+            readout_pass(final_out[n_tile][:, 0:P], n_tile, 1, 1, final_cols)
+            copy_out(final_staged[:, n_tile, :], final_out[n_tile][:, 0:P], n_tile % 2 == 1)
+        nc.sync.dma_start(out_tiles[:, :, S - P : S], final_staged[:])

@@ -46,15 +46,18 @@ def tile_list_crystal_laplace_energies_kernel(
         tab2_plane = held("tab2_plane", [P, T2 // 4], I32)
         wp_plane = held("wp_plane", [P, H // 4], I32)
         nc.vector.memset(tab_plane[:], 0)
-        nc.gpsimd.memset(tab2_plane[:], 0)
+        nc.vector.memset(tab2_plane[:], 0)
         nc.vector.memset(wp_plane[:], 0)
 
-        def load_plane(plane, scales, first_row):
-            rows = 4 * scales.shape[0]
+        def load_plane(queue, plane, scales):
+            for r in range(4):
+                queue.dma_start(plane[r:P:32, :], scales[0, r:16:4, :].bitcast(I32))
+
+        def load_tab_plane():
             for quadrant in range(4):
-                start = 32 * quadrant + first_row
-                source = scales[:, 4 * quadrant : 4 * quadrant + 4, :]
-                nc.sync.dma_start(plane[start : start + rows, :], source.bitcast(I32))
+                start = 32 * quadrant + TAB_ROW
+                source = tab_scales[:, 4 * quadrant : 4 * quadrant + 4, :]
+                nc.gpsimd.dma_start(tab_plane[start : start + 8, :], source.bitcast(I32))
 
         def load_words(name, words):
             table = held(name, [P, words.shape[1]], I32)
@@ -79,20 +82,20 @@ def tile_list_crystal_laplace_energies_kernel(
         def load_amp(e):
             nc.sync.dma_start(amp_sb[e:P:2, :, 0:7], amp.rearrange("(b u x) -> u b x", b=2, x=8)[:, :, e : e + 7])
 
+        load_tab_plane()
+        load_plane(nc.gpsimd, tab2_plane, tab2_scales)
+        load_plane(nc.gpsimd, wp_plane, wp_scales)
         nc.sync.dma_start(idx[:], offs)
         load_amp(0)
         load_amp(1)
-        load_plane(tab_plane, tab_scales, TAB_ROW)
         tab_sb0 = load_words("tab_sb0", tab_words[0])
+        load_wc(0, 0)
         tab_sb1 = load_words("tab_sb1", tab_words[1])
         nc.sync.dma_start(idx2[:], offs2)
-        load_plane(tab2_plane, tab2_scales, 0)
-        tab2_sb = load_words("tab2_sb", tab2_words[0])
         wp_sb = held("wp_sb", [P, H // 2], I32)
         nc.sync.dma_start(wp_sb[:], wp_words[0].bitcast(I32))
-        load_plane(wp_plane, wp_scales, 0)
-        load_wc(0, 0)
         load_wc(1, 0)
+        tab2_sb = load_words("tab2_sb", tab2_words[0])
         load_wc(0, 1)
         load_wc(1, 1)
         load_coef(0)
@@ -108,7 +111,7 @@ def tile_list_crystal_laplace_energies_kernel(
         nc.vector.tensor_scalar(mantissa[:], amp_bits, 0x007FFFFF, 0x3F800000, ALU.bitwise_and, ALU.bitwise_or)
         nc.vector.tensor_scalar(log_power[:], biased_exponent[:], -127.0, math.log(2.0), ALU.add, ALU.mult)
         nc.scalar.activation(log_mantissa[:], mantissa[:].bitcast(F32), ACT.Ln)
-        nc.gpsimd.tensor_tensor(log_amp[:], log_mantissa[:], log_power[:], ALU.add)
+        nc.vector.tensor_tensor(log_amp[:], log_mantissa[:], log_power[:], ALU.add)
         exp_warm_up = held("exp_warm_up", [P, 1], F32)
         nc.scalar.activation(exp_warm_up[:], log_mantissa[:, 0, 0:1], ACT.Exp)
 
@@ -116,6 +119,11 @@ def tile_list_crystal_laplace_energies_kernel(
             picked = held(name, [P, HALF], dtype, tag)
             window = table[:].bitcast(dtype)
             nc.vector.tensor_copy(picked[:], window.indirect(offsets[:, s * LIST_COLS : (s + 1) * LIST_COLS]))
+            return picked
+
+        def gather_plane(name, plane, offsets, tag=None):
+            picked = held(name, [P, 2, HALF], U8, tag)
+            nc.vector.tensor_copy(picked[:].rearrange("p s j -> p (s j)"), plane[:].bitcast(U8).indirect(offsets[:]))
             return picked
 
         def quantize(codes, scales, grouped):
@@ -148,17 +156,14 @@ def tile_list_crystal_laplace_energies_kernel(
             for first in range(0, SLOTS, width):
                 quantize_wc(a, b, first, first + width)
 
-        v_codes, v_scales, v2_codes, v2_scales = {}, {}, {}, {}
-        for s in range(2):
-            v_scales[s] = gather("v_scales%d" % s, tab_plane, U8, idx, s)
+        v_codes, v2_codes = {}, {}
         for s in range(2):
             v_codes[0, s] = gather("v_codes0%d" % s, tab_sb0, U32, idx, s)
+        v_scales = gather_plane("v_scales", tab_plane, idx, "tab_sb0")
+        prepare_wc(0, 0, range(SLOTS), SLOTS)
         for s in range(2):
             v_codes[1, s] = gather("v_codes1%d" % s, tab_sb1, U32, idx, s)
-        for s in range(2):
-            v2_scales[s] = gather("v2_scales%d" % s, tab2_plane, U8, idx2, s)
-        for s in range(2):
-            v2_codes[s] = gather("v2_codes%d" % s, tab2_sb, U32, idx2, s)
+        v2_scales = gather_plane("v2_scales", tab2_plane, idx2)
 
         wp_codes = held("wp_codes", [P, 2 * H], U8)
         wp_sorted_scales = held("wp_sorted_scales", [P, H], U8)
@@ -171,13 +176,9 @@ def tile_list_crystal_laplace_energies_kernel(
             wp_plane[:].bitcast(U16).rearrange("p (b u t) -> p b t u", b=2, t=SLOTS),
         )
 
-        prepare_wc(0, 0, range(SLOTS), 1)
-        wc_tiles(1, 0)
-        for t in range(SLOTS):
-            round_wc(1, 0, t, t >= 2)
-            if t > 0:
-                quantize_wc(1, 0, t - 1, t)
-        quantize_wc(1, 0, SLOTS - 1, SLOTS)
+        prepare_wc(1, 0, range(SLOTS), SLOTS)
+        for s in range(2):
+            v2_codes[s] = gather("v2_codes%d" % s, tab2_sb, U32, idx2, s)
         prepare_wc(0, 1, (), SLOTS)
         wc_tiles(1, 1)
         for t in range(SLOTS):
@@ -202,7 +203,7 @@ def tile_list_crystal_laplace_energies_kernel(
                 lhsT=wc_codes[a, b][:, rows].bitcast(FP8X4),
                 lhsT_scale=wc_scales[a, b][:, rows],
                 rhs=v_codes[a, s][:, cols].bitcast(FP8X4),
-                rhs_scale=v_scales[s][TAB_ROW * (a + 1) : P, cols],
+                rhs_scale=v_scales[TAB_ROW * (a + 1) : P, s, cols],
                 start=start,
                 stop=stop,
             )
@@ -214,17 +215,20 @@ def tile_list_crystal_laplace_energies_kernel(
                 lhsT=wp_codes[:, 2 * first : 2 * (first + P)].bitcast(FP4X4),
                 lhsT_scale=wp_sorted_scales[:, first : first + P],
                 rhs=v2_codes[s][:, cols].bitcast(FP8X4),
-                rhs_scale=v2_scales[s][:, cols],
+                rhs_scale=v2_scales[:, s, cols],
                 start=start,
                 stop=stop,
             )
 
         def project_wide(b, s):
-            banks = [bank_tile(t) for t in range(SLOTS)]
+            banks = [bank_tile(SLOTS * b + t) for t in range(SLOTS)]
             for t in range(SLOTS):
-                prototype_pass(banks[t][:], b, s, t, whole, True, False)
+                if b == 1:
+                    prototype_pass(banks[t][:], b, s, t, whole, True, False)
                 for a in range(2):
-                    crystal_pass(banks[t][:], b, s, t, a, whole, False, a == 1)
+                    crystal_pass(banks[t][:], b, s, t, a, whole, b == 0 and a == 0, b == 1 and a == 1)
+                if b == 0:
+                    prototype_pass(banks[t][:], b, s, t, whole, False, True)
             return banks
 
         def project_narrow(b, s, cols):

@@ -53,11 +53,11 @@ def tile_list_crystal_laplace_energies_kernel(
             for r in range(4):
                 queue.dma_start(plane[r:P:32, :], scales[0, r:16:4, :].bitcast(I32))
 
-        def load_tab_plane():
+        def load_tab_plane(queue):
             for quadrant in range(4):
                 start = 32 * quadrant + TAB_ROW
                 source = tab_scales[:, 4 * quadrant : 4 * quadrant + 4, :]
-                nc.gpsimd.dma_start(tab_plane[start : start + 8, :], source.bitcast(I32))
+                queue.dma_start(tab_plane[start : start + 8, :], source.bitcast(I32))
 
         def load_words(name, words):
             table = held(name, [P, words.shape[1]], I32)
@@ -82,18 +82,18 @@ def tile_list_crystal_laplace_energies_kernel(
         def load_amp(e):
             nc.sync.dma_start(amp_sb[e:P:2, :, 0:7], amp.rearrange("(b u x) -> u b x", b=2, x=8)[:, :, e : e + 7])
 
-        load_tab_plane()
-        load_plane(nc.gpsimd, tab2_plane, tab2_scales)
-        load_plane(nc.gpsimd, wp_plane, wp_scales)
+        load_tab_plane(nc.gpsimd)
         nc.sync.dma_start(idx[:], offs)
         load_amp(0)
         load_amp(1)
         tab_sb0 = load_words("tab_sb0", tab_words[0])
+        nc.sync.dma_start(idx2[:], offs2)
+        load_plane(nc.sync, tab2_plane, tab2_scales)
         load_wc(0, 0)
         tab_sb1 = load_words("tab_sb1", tab_words[1])
-        nc.sync.dma_start(idx2[:], offs2)
         wp_sb = held("wp_sb", [P, H // 2], I32)
         nc.sync.dma_start(wp_sb[:], wp_words[0].bitcast(I32))
+        load_plane(nc.sync, wp_plane, wp_scales)
         load_wc(1, 0)
         tab2_sb = load_words("tab2_sb", tab2_words[0])
         load_wc(0, 1)
@@ -159,11 +159,11 @@ def tile_list_crystal_laplace_energies_kernel(
         v_codes, v2_codes = {}, {}
         for s in range(2):
             v_codes[0, s] = gather("v_codes0%d" % s, tab_sb0, U32, idx, s)
-        v_scales = gather_plane("v_scales", tab_plane, idx, "tab_sb0")
+        v2_scales = gather_plane("v2_scales", tab2_plane, idx2, "tab_sb0")
+        v_scales = gather_plane("v_scales", tab_plane, idx, "tab2_plane")
         prepare_wc(0, 0, range(SLOTS), SLOTS)
         for s in range(2):
             v_codes[1, s] = gather("v_codes1%d" % s, tab_sb1, U32, idx, s)
-        v2_scales = gather_plane("v2_scales", tab2_plane, idx2)
 
         wp_codes = held("wp_codes", [P, 2 * H], U8)
         wp_sorted_scales = held("wp_sorted_scales", [P, H], U8)

@@ -23,6 +23,7 @@ PASS = P * SLOTS
 HALF = 512
 LIST_COLS = HALF // 16
 TAB_ROW = 4
+TERMS = 6
 RUN = 4
 PAIR = 2
 
@@ -101,19 +102,28 @@ def tile_list_crystal_laplace_energies_kernel(
         load_coef(0)
         load_coef(1)
 
+        def per_slot(name, dtype):
+            return held(name, [P, 2, SLOTS], dtype)
+
         amp_bits = amp_sb[:].bitcast(I32)[:, :, 0:7:2]
-        biased_exponent = held("biased_exponent", [P, 2, SLOTS], I32)
-        mantissa = held("mantissa", [P, 2, SLOTS], I32)
-        log_power = held("log_power", [P, 2, SLOTS], F32)
-        log_mantissa = held("log_mantissa", [P, 2, SLOTS], F32)
-        log_amp = held("log_amp", [P, 2, SLOTS], F32)
+        biased_exponent, mantissa_bits = per_slot("biased_exponent", I32), per_slot("mantissa_bits", I32)
+        log_power, shifted, inverse = per_slot("log_power", F32), per_slot("shifted", F32), per_slot("inverse", F32)
+        ratio, square, log_amp = per_slot("ratio", F32), per_slot("square", F32), per_slot("log_amp", F32)
+        nc.vector.tensor_scalar(mantissa_bits[:], amp_bits, 0x007FFFFF, 0x3F800000, ALU.bitwise_and, ALU.bitwise_or)
         nc.vector.tensor_scalar(biased_exponent[:], amp_bits, 23, None, ALU.logical_shift_right)
-        nc.vector.tensor_scalar(mantissa[:], amp_bits, 0x007FFFFF, 0x3F800000, ALU.bitwise_and, ALU.bitwise_or)
+        mantissa = mantissa_bits[:].bitcast(F32)
+        nc.vector.tensor_scalar(shifted[:], mantissa, 1.5, None, ALU.add)
         nc.vector.tensor_scalar(log_power[:], biased_exponent[:], -127.0, math.log(2.0), ALU.add, ALU.mult)
-        nc.scalar.activation(log_mantissa[:], mantissa[:].bitcast(F32), ACT.Ln)
-        nc.vector.tensor_tensor(log_amp[:], log_mantissa[:], log_power[:], ALU.add)
-        exp_warm_up = held("exp_warm_up", [P, 1], F32)
-        nc.scalar.activation(exp_warm_up[:], log_mantissa[:, 0, 0:1], ACT.Exp)
+        nc.vector.reciprocal(inverse[:], shifted[:])
+        nc.vector.scalar_tensor_tensor(ratio[:], mantissa, -1.5, inverse[:], ALU.add, ALU.mult)
+        nc.vector.tensor_tensor(square[:], ratio[:], ratio[:], ALU.mult)
+        series = per_slot("series%d" % TERMS, F32)
+        nc.vector.tensor_scalar(series[:], square[:], 2.0 / (2 * TERMS - 1), None, ALU.mult)
+        for k in range(TERMS - 2, -1, -1):
+            inner, series = series, per_slot("series%d" % k, F32)
+            factor = square if k > 0 else ratio
+            nc.vector.scalar_tensor_tensor(series[:], inner[:], 2.0 / (2 * k + 1), factor[:], ALU.add, ALU.mult)
+        nc.vector.scalar_tensor_tensor(log_amp[:], series[:], math.log(1.5), log_power[:], ALU.add, ALU.add)
 
         def gather(name, table, dtype, offsets, s, tag=None):
             picked = held(name, [P, HALF], dtype, tag)
@@ -348,14 +358,14 @@ def tile_list_crystal_laplace_energies_kernel(
             narrow[b] = chunk_tiles("e%d" % b, HALF // 2)
             laplace(narrow[b], project_narrow(b, 1, early), b)
         finish_h(narrow[0], 0, 1, early.start)
+        finish_h(narrow[1], 1, 1, early.start)
         for n_tile in n_tiles:
             store("first%d" % n_tile, first_out[n_tile], out_tiles[:, n_tile : n_tile + 1, 0:HALF], False)
-        finish_h(narrow[1], 1, 1, early.start)
         late_first = chunk_tiles("l0", HALF // 2)
         laplace(late_first, project_narrow(0, 1, late), 0)
         last = chunk_tiles("l1", HALF // 2)
         last_banks = project_narrow(1, 1, late)
-        early_out = [bank_tile(SLOTS + pair) for pair in range(2)]
+        early_out = [bank_tile(5 + pair) for pair in range(2)]
         for n_tile in n_tiles:
             for b in range(2):
                 first = (n_tile % 2) * (HALF // 2)
@@ -366,7 +376,7 @@ def tile_list_crystal_laplace_energies_kernel(
             take_abs(last, last_banks, i)
         ends = pieces(slice(0, HALF // 2), P)
         final_cols = slice(HALF - P, HALF)
-        final_out = [bank_tile(index) for index in (0, 1, 7, 2)]
+        final_out = [bank_tile(index) for index in (0, 1, 4, 7)]
         for n_tile in n_tiles:
             readout_pass(final_out[n_tile][:, 0:P], n_tile, 0, 1, final_cols)
         for t in range(SLOTS):
@@ -380,7 +390,7 @@ def tile_list_crystal_laplace_energies_kernel(
         store("early0", early_out[0], out_tiles[:, 0:2, HALF + early.start : HALF + early.stop], True)
         store("early1", early_out[1], out_tiles[:, 2:4, HALF + early.start : HALF + early.stop], True)
 
-        bank = bank_tile(6)
+        bank = bank_tile(2)
         for n_tile in n_tiles:
             for b in range(2):
                 readout_pass(bank[:, n_tile * P : (n_tile + 1) * P], n_tile, b, 1, slice(late.start, late.start + P))

@@ -170,10 +170,10 @@ def tile_list_crystal_laplace_energies_kernel(
         for s in range(2):
             v_codes[0, s] = gather("v_codes0%d" % s, tab_sb0, U32, idx, s)
         v2_scales = gather_plane("v2_scales", tab2_plane, idx2, "tab_sb0")
-        v_scales = gather_plane("v_scales", tab_plane, idx, "tab2_plane")
         prepare_wc(0, 0, range(SLOTS), SLOTS)
         for s in range(2):
             v_codes[1, s] = gather("v_codes1%d" % s, tab_sb1, U32, idx, s)
+        v_scales = {0: gather("v_scales0", tab_plane, U8, idx, 0, "wc_bf00")}
 
         wp_codes = held("wp_codes", [P, 2 * H], U8)
         wp_sorted_scales = held("wp_sorted_scales", [P, H], U8)
@@ -186,6 +186,7 @@ def tile_list_crystal_laplace_energies_kernel(
             wp_plane[:].bitcast(U16).rearrange("p (b u t) -> p b t u", b=2, t=SLOTS),
         )
 
+        v_scales[1] = gather("v_scales1", tab_plane, U8, idx, 1, "wp_plane")
         prepare_wc(1, 0, range(SLOTS), SLOTS)
         for s in range(2):
             v2_codes[s] = gather("v2_codes%d" % s, tab2_sb, U32, idx2, s)
@@ -213,7 +214,7 @@ def tile_list_crystal_laplace_energies_kernel(
                 lhsT=wc_codes[a, b][:, rows].bitcast(FP8X4),
                 lhsT_scale=wc_scales[a, b][:, rows],
                 rhs=v_codes[a, s][:, cols].bitcast(FP8X4),
-                rhs_scale=v_scales[TAB_ROW * (a + 1) : P, s, cols],
+                rhs_scale=v_scales[s][TAB_ROW * (a + 1) : P, cols],
                 start=start,
                 stop=stop,
             )

@@ -313,7 +313,7 @@ def tile_list_crystal_laplace_energies_kernel(
             coef_scales[b] = held("coef_scales%d" % b, [P, N], U8)
             quantize(coef_codes[b][:], coef_scales[b][:], coef_bf[b][:].rearrange("p n t -> p (n t)"))
 
-        def readout_pass(sums, n_tile, b, s, cols):
+        def readout_pass(sums, n_tile, b, s, cols, closes=True):
             rows = slice(n_tile * P, (n_tile + 1) * P)
             nc.tensor.matmul_mx(
                 out=sums,
@@ -322,7 +322,7 @@ def tile_list_crystal_laplace_energies_kernel(
                 rhs=h_codes[b, s][:, cols].bitcast(FP8X4),
                 rhs_scale=h_scales[b, s][:, cols],
                 start=(b == 0),
-                stop=(b == 1),
+                stop=(closes and b == 1),
             )
 
         def copy_out(target, source, on_scalar):
@@ -376,10 +376,9 @@ def tile_list_crystal_laplace_energies_kernel(
         for i in range(2):
             take_abs(last, last_banks, i)
         ends = pieces(slice(0, HALF // 2), P)
-        final_cols = slice(HALF - P, HALF)
-        final_out = [bank_tile(index) for index in (0, 1, 4, 7)]
+        late_out = [bank_tile(index) for index in (0, 1, 4, 7)]
         for n_tile in n_tiles:
-            readout_pass(final_out[n_tile][:, 0:P], n_tile, 0, 1, final_cols)
+            readout_pass(late_out[n_tile][:, 0 : HALF // 2], n_tile, 0, 1, late)
         for t in range(SLOTS):
             take_exp(last, 1, t, ends[0])
         interleave(last, ends[0])
@@ -391,13 +390,10 @@ def tile_list_crystal_laplace_energies_kernel(
         store("early0", early_out[0], out_tiles[:, 0:2, HALF + early.start : HALF + early.stop], True)
         store("early1", early_out[1], out_tiles[:, 2:4, HALF + early.start : HALF + early.stop], True)
 
-        bank = bank_tile(2)
         for n_tile in n_tiles:
-            for b in range(2):
-                readout_pass(bank[:, n_tile * P : (n_tile + 1) * P], n_tile, b, 1, slice(late.start, late.start + P))
-        store("late", bank, out_tiles[:, :, HALF + late.start : HALF + late.start + P], True)
-        final_staged = held("final_staged", [P, N // P, P], F32)
+            readout_pass(late_out[n_tile][:, 0:P], n_tile, 1, 1, slice(late.start, late.start + P), False)
         for n_tile in n_tiles:
-            readout_pass(final_out[n_tile][:, 0:P], n_tile, 1, 1, final_cols)
-            copy_out(final_staged[:, n_tile, :], final_out[n_tile][:, 0:P], n_tile % 2 == 1)
-        nc.sync.dma_start(out_tiles[:, :, S - P : S], final_staged[:])
+            staged = held("late%d" % n_tile, [P, HALF // 2], F32)
+            readout_pass(late_out[n_tile][:, P : 2 * P], n_tile, 1, 1, slice(late.start + P, late.stop))
+            copy_out(staged[:], late_out[n_tile][:, 0 : HALF // 2], n_tile % 2 == 0)
+            nc.sync.dma_start(out_tiles[:, n_tile, HALF + late.start : HALF + late.stop], staged[:])

@@ -23,7 +23,8 @@ PASS = P * SLOTS
 HALF = 512
 LIST_COLS = HALF // 16
 TAB_ROW = 4
-TERMS = 6
+TERMS = 18
+SPREAD = P // 16
 RUN = 4
 PAIR = 2
 
@@ -44,15 +45,11 @@ def tile_list_crystal_laplace_energies_kernel(
         idx2 = lists.tile([P, S // 16], U16, name="idx2")
 
         tab_plane = held("tab_plane", [P, T // 4], I32)
-        tab2_plane = held("tab2_plane", [P, T2 // 4], I32)
-        wp_plane = held("wp_plane", [P, H // 4], I32)
+        tab2_rows = held("tab2_rows", [P, T2 // 4], I32)
+        wp_rows = held("wp_rows", [P, H // 4], I32)
         nc.vector.memset(tab_plane[:], 0)
-        nc.vector.memset(tab2_plane[:], 0)
-        nc.vector.memset(wp_plane[:], 0)
-
-        def load_plane(queue, plane, scales):
-            for r in range(4):
-                queue.dma_start(plane[r:P:32, :], scales[0, r:16:4, :].bitcast(I32))
+        nc.vector.memset(tab2_rows[:], 0)
+        nc.vector.memset(wp_rows[:], 0)
 
         def load_tab_plane(queue):
             for quadrant in range(4):
@@ -81,49 +78,59 @@ def tile_list_crystal_laplace_energies_kernel(
         amp_sb = held("amp_sb", [P, 2, 8], F32)
 
         def load_amp(e):
-            nc.sync.dma_start(amp_sb[e:P:2, :, 0:7], amp.rearrange("(b u x) -> u b x", b=2, x=8)[:, :, e : e + 7])
+            nc.scalar.dma_start(amp_sb[e:P:2, :, 0:7], amp.rearrange("(b u x) -> u b x", b=2, x=8)[:, :, e : e + 7])
 
+        counts = held("counts", [P, 2, TERMS], F32)
+        nc.gpsimd.iota(counts[:, 0, :], [[1, TERMS]], base=-TERMS, channel_multiplier=0, allow_small_or_imprecise_dtypes=True)
         load_tab_plane(nc.gpsimd)
-        nc.sync.dma_start(idx[:], offs)
         load_amp(0)
         load_amp(1)
-        tab_sb0 = load_words("tab_sb0", tab_words[0])
         nc.sync.dma_start(idx2[:], offs2)
-        load_plane(nc.sync, tab2_plane, tab2_scales)
-        load_wc(0, 0)
-        tab_sb1 = load_words("tab_sb1", tab_words[1])
+        nc.scalar.dma_start(tab2_rows[0:P:SPREAD, :], tab2_scales[0].bitcast(I32))
+        nc.scalar.dma_start(wp_rows[0:P:SPREAD, :], wp_scales[0].bitcast(I32))
+        tab_sb0 = load_words("tab_sb0", tab_words[0])
+        nc.sync.dma_start(idx[:], offs)
         wp_sb = held("wp_sb", [P, H // 2], I32)
         nc.sync.dma_start(wp_sb[:], wp_words[0].bitcast(I32))
-        load_plane(nc.sync, wp_plane, wp_scales)
-        load_wc(1, 0)
+        load_wc(0, 0)
         tab2_sb = load_words("tab2_sb", tab2_words[0])
+        tab_sb1 = load_words("tab_sb1", tab_words[1])
+        load_wc(1, 0)
         load_wc(0, 1)
         load_wc(1, 1)
         load_coef(0)
         load_coef(1)
 
-        def per_slot(name, dtype):
-            return held(name, [P, 2, SLOTS], dtype)
+        def per_value(name, dtype, width):
+            return held(name, [P, 2, SLOTS, width], dtype)
 
+        addends = per_value("addends", F32, TERMS + 1)
+        factors, horner = per_value("factors", F32, TERMS + 1), per_value("horner", F32, TERMS + 1)
+        nc.vector.memset(factors[:], 0.0)
+        nc.vector.reciprocal(counts[:, 1, :], counts[:, 0, :])
+        runs = addends[:].rearrange("p b t k -> p (b t) k")
+        nc.vector.tensor_copy(runs[:, :, 0:TERMS], counts[:, 1:2, :].to_broadcast([P, 2 * SLOTS, TERMS]))
         amp_bits = amp_sb[:].bitcast(I32)[:, :, 0:7:2]
-        biased_exponent, mantissa_bits = per_slot("biased_exponent", I32), per_slot("mantissa_bits", I32)
-        log_power, shifted, inverse = per_slot("log_power", F32), per_slot("shifted", F32), per_slot("inverse", F32)
-        ratio, square, log_amp = per_slot("ratio", F32), per_slot("square", F32), per_slot("log_amp", F32)
-        nc.vector.tensor_scalar(mantissa_bits[:], amp_bits, 0x007FFFFF, 0x3F800000, ALU.bitwise_and, ALU.bitwise_or)
+        biased_exponent, mantissa_bits = held("biased_exponent", [P, 2, SLOTS], I32), held("mantissa_bits", [P, 2 * SLOTS, 1], I32)
+        nc.vector.tensor_scalar(
+            mantissa_bits[:].rearrange("p (b t) o -> p b (t o)", b=2), amp_bits, 0x007FFFFF, 0x3F800000, ALU.bitwise_and, ALU.bitwise_or
+        )
         nc.vector.tensor_scalar(biased_exponent[:], amp_bits, 23, None, ALU.logical_shift_right)
-        mantissa = mantissa_bits[:].bitcast(F32)
-        nc.vector.tensor_scalar(shifted[:], mantissa, 1.5, None, ALU.add)
-        nc.vector.tensor_scalar(log_power[:], biased_exponent[:], -127.0, math.log(2.0), ALU.add, ALU.mult)
-        nc.vector.reciprocal(inverse[:], shifted[:])
-        nc.vector.scalar_tensor_tensor(ratio[:], mantissa, -1.5, inverse[:], ALU.add, ALU.mult)
-        nc.vector.tensor_tensor(square[:], ratio[:], ratio[:], ALU.mult)
-        series = per_slot("series%d" % TERMS, F32)
-        nc.vector.tensor_scalar(series[:], square[:], 2.0 / (2 * TERMS - 1), None, ALU.mult)
-        for k in range(TERMS - 2, -1, -1):
-            inner, series = series, per_slot("series%d" % k, F32)
-            factor = square if k > 0 else ratio
-            nc.vector.scalar_tensor_tensor(series[:], inner[:], 2.0 / (2 * k + 1), factor[:], ALU.add, ALU.mult)
-        nc.vector.scalar_tensor_tensor(log_amp[:], series[:], math.log(1.5), log_power[:], ALU.add, ALU.add)
+        nc.vector.tensor_scalar(
+            factors[:].rearrange("p b t k -> p (b t) k")[:, :, 1 : TERMS + 1],
+            mantissa_bits[:].bitcast(F32).to_broadcast([P, 2 * SLOTS, TERMS]),
+            -1.0 / 1.5,
+            1.0,
+            ALU.mult,
+            ALU.add,
+        )
+        nc.vector.tensor_scalar(
+            addends[:, :, :, TERMS], biased_exponent[:], math.log(2.0), math.log(1.5) - 127.0 * math.log(2.0), ALU.mult, ALU.add
+        )
+        flat = "p b t k -> p (b t k)"
+        nc.vector.tensor_tensor_scan(
+            horner[:].rearrange(flat), factors[:].rearrange(flat), addends[:].rearrange(flat), 0.0, ALU.mult, ALU.add
+        )
 
         def gather(name, table, dtype, offsets, s, tag=None):
             picked = held(name, [P, HALF], dtype, tag)
@@ -166,30 +173,33 @@ def tile_list_crystal_laplace_energies_kernel(
             for first in range(0, SLOTS, width):
                 quantize_wc(a, b, first, first + width)
 
-        v_codes, v2_codes = {}, {}
+        v_codes, v2_codes, v_scales = {}, {}, {}
+        planes = held("planes", [P, (S + H) // 4], I32)
+        v2_rows = gather_plane("v2_rows", tab2_rows, idx2)
+        nc.vector.tensor_copy(
+            planes[:, S // 4 :].bitcast(U16).rearrange("p (b t u) -> p b t u", b=2, t=SLOTS),
+            wp_rows[:].bitcast(U16).rearrange("p (b u t) -> p b t u", b=2, t=SLOTS),
+        )
+        nc.vector.tensor_copy(planes[:, 0 : S // 4], v2_rows[:].rearrange("p s j -> p (s j)").bitcast(I32))
+        for r in range(1, 4):
+            nc.gpsimd.dma_start(planes[r:P:32, :], planes[SPREAD * r : P : 32, :])
+        v2_scales = planes[:, 0 : S // 4].bitcast(U8).rearrange("p (s j) -> p s j", s=2)
+        wp_sorted_scales = planes[:, S // 4 :].bitcast(U8)
         for s in range(2):
             v_codes[0, s] = gather("v_codes0%d" % s, tab_sb0, U32, idx, s)
-        v2_scales = gather_plane("v2_scales", tab2_plane, idx2, "tab_sb0")
-        prepare_wc(0, 0, range(SLOTS), SLOTS)
-        for s in range(2):
-            v_codes[1, s] = gather("v_codes1%d" % s, tab_sb1, U32, idx, s)
-        v_scales = {0: gather("v_scales0", tab_plane, U8, idx, 0, "wc_bf00")}
-
         wp_codes = held("wp_codes", [P, 2 * H], U8)
-        wp_sorted_scales = held("wp_sorted_scales", [P, H], U8)
         nc.vector.tensor_copy(
             wp_codes[:].bitcast(I32).rearrange("p (b t u) -> p b t u", b=2, t=SLOTS),
             wp_sb[:].rearrange("p (b u t) -> p b t u", b=2, t=SLOTS),
         )
-        nc.vector.tensor_copy(
-            wp_sorted_scales[:].bitcast(U16).rearrange("p (b t u) -> p b t u", b=2, t=SLOTS),
-            wp_plane[:].bitcast(U16).rearrange("p (b u t) -> p b t u", b=2, t=SLOTS),
-        )
-
-        v_scales[1] = gather("v_scales1", tab_plane, U8, idx, 1, "wp_plane")
-        prepare_wc(1, 0, range(SLOTS), SLOTS)
+        v_scales[0] = gather("v_scales0", tab_plane, U8, idx, 0, "tab_sb0")
+        v_scales[1] = gather("v_scales1", tab_plane, U8, idx, 1, "wp_sb")
+        prepare_wc(0, 0, range(SLOTS), SLOTS)
         for s in range(2):
             v2_codes[s] = gather("v2_codes%d" % s, tab2_sb, U32, idx2, s)
+        for s in range(2):
+            v_codes[1, s] = gather("v_codes1%d" % s, tab_sb1, U32, idx, s)
+        prepare_wc(1, 0, (2, 3), 1)
         prepare_wc(0, 1, (), SLOTS)
         wc_tiles(1, 1)
         for t in range(SLOTS):
@@ -231,28 +241,23 @@ def tile_list_crystal_laplace_energies_kernel(
                 stop=stop,
             )
 
-        def project_wide(b, s):
-            banks = [bank_tile(SLOTS * b + t) for t in range(SLOTS)]
+        def project_wide(b, s, indices):
+            banks = [bank_tile(index) for index in indices]
             for t in range(SLOTS):
-                if b == 1:
-                    prototype_pass(banks[t][:], b, s, t, whole, True, False)
+                prototype_pass(banks[t][:], b, s, t, whole, True, False)
                 for a in range(2):
-                    crystal_pass(banks[t][:], b, s, t, a, whole, b == 0 and a == 0, b == 1 and a == 1)
-                if b == 0:
-                    prototype_pass(banks[t][:], b, s, t, whole, False, True)
+                    crystal_pass(banks[t][:], b, s, t, a, whole, False, a == 1)
             return banks
 
-        def project_narrow(b, s, cols):
-            banks = [bank_tile(2 * b + pair) for pair in range(2)]
+        def project_narrow(b, s, cols, indices):
+            banks = [bank_tile(index) for index in indices]
             width = cols.stop - cols.start
             for t in range(SLOTS):
-                first = (t % 2) * width
-                for a in range(2):
-                    crystal_pass(banks[t // 2][:, first : first + width], b, s, t, a, cols, a == 0, False)
-                parts = pieces(cols, P)
-                for i, part in enumerate(parts):
-                    sums = banks[t // 2][:, first + i * P : first + (i + 1) * P]
-                    prototype_pass(sums, b, s, t, part, False, i == len(parts) - 1)
+                bank, first = banks[t * width // HALF], t * width % HALF
+                crystal_pass(bank[:, first : first + width], b, s, t, 0, cols, True, False)
+                for i, part in enumerate(pieces(cols, P)):
+                    prototype_pass(bank[:, first + i * P : first + (i + 1) * P], b, s, t, part, False, False)
+                crystal_pass(bank[:, first : first + width], b, s, t, 1, cols, False, True)
             return banks
 
         def chunk_tiles(name, width, tag=None):
@@ -266,7 +271,7 @@ def tile_list_crystal_laplace_energies_kernel(
 
         def take_exp(tiles, b, t, cols):
             dist = tiles[0][:].rearrange("p (t j) -> p t j", t=SLOTS)
-            nc.scalar.activation(tiles[1][:, t, cols], dist[:, t, cols], ACT.Exp, bias=log_amp[:, b, t : t + 1], scale=-1.0)
+            nc.scalar.activation(tiles[1][:, t, cols], dist[:, t, cols], ACT.Exp, bias=horner[:, b, t, TERMS : TERMS + 1], scale=-1.0)
 
         def interleave(tiles, cols):
             nc.vector.tensor_copy(
@@ -291,7 +296,7 @@ def tile_list_crystal_laplace_energies_kernel(
 
         def finish_h(tiles, b, s, first):
             width = tiles[1].shape[2]
-            halves = pieces(slice(0, width), HALF // 2)
+            halves = pieces(slice(0, width), min(width, HALF // 2))
             for cols in halves:
                 interleave(tiles, cols)
             for cols in halves:
@@ -339,61 +344,61 @@ def tile_list_crystal_laplace_energies_kernel(
         out_tiles = out.rearrange("(a p) j -> p a j", p=P)
         n_tiles = range(N // P)
 
-        wide = [chunk_tiles("00", HALF, "wc_bf11"), chunk_tiles("10", HALF)]
-        for b in range(2):
-            laplace(wide[b], project_wide(b, 0), b)
+        early, late = pieces(whole, HALF // 2)
+
+        def laplace_wide(tiles, banks, b):
+            for cols in (early, late):
+                for t in range(SLOTS):
+                    dist = tiles[0][:, t * HALF : (t + 1) * HALF]
+                    nc.scalar.activation(dist[:, cols], banks[t][:, cols], ACT.Abs)
+                for t in range(SLOTS):
+                    take_exp(tiles, b, t, cols)
+
+        wide = [chunk_tiles("00", HALF, "wc_bf00"), chunk_tiles("10", HALF)]
+        narrow = [chunk_tiles("e%d" % b, HALF // 2) for b in range(2)]
+        laplace_wide(wide[0], project_wide(0, 0, (0, 1, 2, 3)), 0)
+        laplace(narrow[0], project_narrow(0, 1, early, (4, 5)), 0)
+        laplace_wide(wide[1], project_wide(1, 0, (6, 7, 0, 1)), 1)
+        laplace(narrow[1], project_narrow(1, 1, early, (2, 3)), 1)
         finish_h(wide[0], 0, 0, 0)
         round_coef(0)
-        round_coef(1)
-        quantize_coef(0)
-        quantize_coef(1)
-        finish_h(wide[1], 1, 0, 0)
-        first_out = [bank_tile(SLOTS + n_tile) for n_tile in n_tiles]
-        for n_tile in n_tiles:
-            for b in range(2):
-                readout_pass(first_out[n_tile][:], n_tile, b, 0, whole)
-
-        early, late = pieces(whole, HALF // 2)
-        narrow = {}
-        for b in range(2):
-            narrow[b] = chunk_tiles("e%d" % b, HALF // 2)
-            laplace(narrow[b], project_narrow(b, 1, early), b)
         finish_h(narrow[0], 0, 1, early.start)
+        quantize_coef(0)
+        round_coef(1)
+        interleave(wide[1], early)
+        quantize_coef(1)
+        quantize_h(wide[1], early, 1, 0, 0)
+        interleave(wide[1], late)
+        quantize_h(wide[1], late, 1, 0, 0)
+        late_first = chunk_tiles("l0", HALF // 2)
+        laplace(late_first, project_narrow(0, 1, late, (4, 5)), 0)
+        first_out = [bank_tile(index) for index in n_tiles]
+        for b in range(2):
+            for n_tile in n_tiles:
+                readout_pass(first_out[n_tile][:], n_tile, b, 0, whole)
+        ends = pieces(late, P)
+        last = [chunk_tiles("l1%d" % i, P) for i in range(2)]
+        for i in range(2):
+            laplace(last[i], project_narrow(1, 1, ends[i], (6 + i,)), 1)
         finish_h(narrow[1], 1, 1, early.start)
         for n_tile in n_tiles:
             store("first%d" % n_tile, first_out[n_tile], out_tiles[:, n_tile : n_tile + 1, 0:HALF], False)
-        late_first = chunk_tiles("l0", HALF // 2)
-        laplace(late_first, project_narrow(0, 1, late), 0)
-        last = chunk_tiles("l1", HALF // 2)
-        last_banks = project_narrow(1, 1, late)
-        early_out = [bank_tile(5 + pair) for pair in range(2)]
+        early_out = [bank_tile(4 + pair) for pair in range(2)]
         for n_tile in n_tiles:
             for b in range(2):
                 first = (n_tile % 2) * (HALF // 2)
                 readout_pass(early_out[n_tile // 2][:, first : first + HALF // 2], n_tile, b, 1, early)
         finish_h(late_first, 0, 1, late.start)
-
-        for i in range(2):
-            take_abs(last, last_banks, i)
-        ends = pieces(slice(0, HALF // 2), P)
-        late_out = [bank_tile(index) for index in (0, 1, 4, 7)]
+        store("early0", early_out[0], out_tiles[:, 0:2, HALF + early.start : HALF + early.stop], True)
+        late_out = [bank_tile(index) for index in n_tiles]
         for n_tile in n_tiles:
             readout_pass(late_out[n_tile][:, 0 : HALF // 2], n_tile, 0, 1, late)
-        for t in range(SLOTS):
-            take_exp(last, 1, t, ends[0])
-        interleave(last, ends[0])
-        quantize_h(last, ends[0], 1, 1, late.start)
-        for t in range(SLOTS):
-            take_exp(last, 1, t, ends[1])
-        interleave(last, ends[1])
-        quantize_h(last, ends[1], 1, 1, late.start)
-        store("early0", early_out[0], out_tiles[:, 0:2, HALF + early.start : HALF + early.stop], True)
         store("early1", early_out[1], out_tiles[:, 2:4, HALF + early.start : HALF + early.stop], True)
-
-        for n_tile in n_tiles:
-            readout_pass(late_out[n_tile][:, 0:P], n_tile, 1, 1, slice(late.start, late.start + P), False)
+        for i in range(2):
+            finish_h(last[i], 1, 1, ends[i].start)
+            for n_tile in n_tiles:
+                readout_pass(late_out[n_tile][:, i * P : (i + 1) * P], n_tile, 1, 1, ends[i], i == 1)
         for n_tile in n_tiles:
             staged = held("late%d" % n_tile, [P, HALF // 2], F32)
-            readout_pass(late_out[n_tile][:, P : 2 * P], n_tile, 1, 1, slice(late.start + P, late.stop))
             copy_out(staged[:], late_out[n_tile][:, 0 : HALF // 2], n_tile % 2 == 0)
             nc.sync.dma_start(out_tiles[:, n_tile, HALF + late.start : HALF + late.stop], staged[:])

@@ -44,18 +44,12 @@ def tile_list_crystal_laplace_energies_kernel(
         idx = lists.tile([P, S // 16], U16, name="idx")
         idx2 = lists.tile([P, S // 16], U16, name="idx2")
 
-        tab_plane = held("tab_plane", [P, T // 4], I32)
+        tab_rows = held("tab_rows", [P, T // 4], I32)
         tab2_rows = held("tab2_rows", [P, T2 // 4], I32)
-        wp_rows = held("wp_rows", [P, H // 4], I32)
-        nc.vector.memset(tab_plane[:], 0)
+        wp_plane = held("wp_plane", [P, H // 4], I32)
         nc.vector.memset(tab2_rows[:], 0)
-        nc.vector.memset(wp_rows[:], 0)
-
-        def load_tab_plane(queue):
-            for quadrant in range(4):
-                start = 32 * quadrant + TAB_ROW
-                source = tab_scales[:, 4 * quadrant : 4 * quadrant + 4, :]
-                queue.dma_start(tab_plane[start : start + 8, :], source.bitcast(I32))
+        nc.vector.memset(tab_rows[:], 0)
+        nc.vector.memset(wp_plane[:], 0)
 
         def load_words(name, words):
             table = held(name, [P, words.shape[1]], I32)
@@ -82,24 +76,19 @@ def tile_list_crystal_laplace_energies_kernel(
 
         counts = held("counts", [P, 2, TERMS], F32)
         nc.gpsimd.iota(counts[:, 0, :], [[1, TERMS]], base=-TERMS, channel_multiplier=0, allow_small_or_imprecise_dtypes=True)
-        load_tab_plane(nc.gpsimd)
         load_amp(0)
         load_amp(1)
         nc.sync.dma_start(idx2[:], offs2)
         nc.scalar.dma_start(tab2_rows[0:P:SPREAD, :], tab2_scales[0].bitcast(I32))
-        nc.scalar.dma_start(wp_rows[0:P:SPREAD, :], wp_scales[0].bitcast(I32))
-        tab_sb0 = load_words("tab_sb0", tab_words[0])
+        nc.scalar.dma_start(tab_rows[0 : P : SPREAD // 2, :], tab_scales.rearrange("a q t -> q a t").bitcast(I32))
+        for r in range(4):
+            nc.scalar.dma_start(wp_plane[r:P:32, :], wp_scales[0, r:16:4, :].bitcast(I32))
         nc.sync.dma_start(idx[:], offs)
+        load_wc(0, 0)
         wp_sb = held("wp_sb", [P, H // 2], I32)
         nc.sync.dma_start(wp_sb[:], wp_words[0].bitcast(I32))
-        load_wc(0, 0)
-        tab2_sb = load_words("tab2_sb", tab2_words[0])
         tab_sb1 = load_words("tab_sb1", tab_words[1])
-        load_wc(1, 0)
-        load_wc(0, 1)
-        load_wc(1, 1)
-        load_coef(0)
-        load_coef(1)
+        tab2_sb = load_words("tab2_sb", tab2_words[0])
 
         def per_value(name, dtype, width):
             return held(name, [P, 2, SLOTS, width], dtype)
@@ -124,23 +113,19 @@ def tile_list_crystal_laplace_energies_kernel(
             ALU.mult,
             ALU.add,
         )
-        nc.vector.tensor_scalar(
-            addends[:, :, :, TERMS], biased_exponent[:], math.log(2.0), math.log(1.5) - 127.0 * math.log(2.0), ALU.mult, ALU.add
-        )
+        nc.vector.tensor_scalar(addends[:, :, :, TERMS], biased_exponent[:], -127.0, math.log(2.0), ALU.add, ALU.mult)
         flat = "p b t k -> p (b t k)"
         nc.vector.tensor_tensor_scan(
             horner[:].rearrange(flat), factors[:].rearrange(flat), addends[:].rearrange(flat), 0.0, ALU.mult, ALU.add
         )
 
+        log_amp = held("log_amp", [P, 2, SLOTS], F32)
+        nc.scalar.activation(log_amp[:], horner[:, :, :, TERMS], ACT.Copy, bias=math.log(1.5))
+
         def gather(name, table, dtype, offsets, s, tag=None):
             picked = held(name, [P, HALF], dtype, tag)
             window = table[:].bitcast(dtype)
             nc.vector.tensor_copy(picked[:], window.indirect(offsets[:, s * LIST_COLS : (s + 1) * LIST_COLS]))
-            return picked
-
-        def gather_plane(name, plane, offsets, tag=None):
-            picked = held(name, [P, 2, HALF], U8, tag)
-            nc.vector.tensor_copy(picked[:].rearrange("p s j -> p (s j)"), plane[:].bitcast(U8).indirect(offsets[:]))
             return picked
 
         def quantize(codes, scales, grouped):
@@ -173,32 +158,43 @@ def tile_list_crystal_laplace_energies_kernel(
             for first in range(0, SLOTS, width):
                 quantize_wc(a, b, first, first + width)
 
-        v_codes, v2_codes, v_scales = {}, {}, {}
-        planes = held("planes", [P, (S + H) // 4], I32)
-        v2_rows = gather_plane("v2_rows", tab2_rows, idx2)
-        nc.vector.tensor_copy(
-            planes[:, S // 4 :].bitcast(U16).rearrange("p (b t u) -> p b t u", b=2, t=SLOTS),
-            wp_rows[:].bitcast(U16).rearrange("p (b u t) -> p b t u", b=2, t=SLOTS),
-        )
-        nc.vector.tensor_copy(planes[:, 0 : S // 4], v2_rows[:].rearrange("p s j -> p (s j)").bitcast(I32))
+        v_codes, v2_codes = {}, {}
+        picked_rows = held("picked_rows", [P, 2 * S], U8)
+        planes = held("planes", [P, 2 * S // 4], I32)
+        nc.vector.tensor_copy(picked_rows[:, S : 2 * S], tab2_rows[:].bitcast(U8).indirect(idx2[:]))
+        nc.vector.tensor_copy(picked_rows[:, 0:S], tab_rows[:].bitcast(U8).indirect(idx[:]))
+        spread = picked_rows[:].bitcast(I32)
+        nc.vector.tensor_copy(planes[:], spread)
+        v_cols, v2_cols = slice(0, S // 4), slice(S // 4, S // 2)
         for r in range(1, 4):
-            nc.gpsimd.dma_start(planes[r:P:32, :], planes[SPREAD * r : P : 32, :])
-        v2_scales = planes[:, 0 : S // 4].bitcast(U8).rearrange("p (s j) -> p s j", s=2)
-        wp_sorted_scales = planes[:, S // 4 :].bitcast(U8)
+            nc.sync.dma_start(planes[r:P:32, :], spread[SPREAD * r : P : 32, :])
+        for r in range(1, 4):
+            nc.sync.dma_start(planes[TAB_ROW + r : P : 32, v_cols], spread[TAB_ROW + SPREAD * r : P : 32, v_cols])
+        tab_sb0 = load_words("tab_sb0", tab_words[0])
+        load_wc(1, 0)
+        load_wc(0, 1)
+        load_wc(1, 1)
+        load_coef(0)
+        load_coef(1)
+        v_scales = planes[:, v_cols].bitcast(U8).rearrange("p (s j) -> p s j", s=2)
+        v2_scales = planes[:, v2_cols].bitcast(U8).rearrange("p (s j) -> p s j", s=2)
         for s in range(2):
-            v_codes[0, s] = gather("v_codes0%d" % s, tab_sb0, U32, idx, s)
+            v_codes[1, s] = gather("v_codes1%d" % s, tab_sb1, U32, idx, s)
         wp_codes = held("wp_codes", [P, 2 * H], U8)
+        wp_sorted_scales = held("wp_sorted_scales", [P, H], U8)
         nc.vector.tensor_copy(
             wp_codes[:].bitcast(I32).rearrange("p (b t u) -> p b t u", b=2, t=SLOTS),
             wp_sb[:].rearrange("p (b u t) -> p b t u", b=2, t=SLOTS),
         )
-        v_scales[0] = gather("v_scales0", tab_plane, U8, idx, 0, "tab_sb0")
-        v_scales[1] = gather("v_scales1", tab_plane, U8, idx, 1, "wp_sb")
+        nc.vector.tensor_copy(
+            wp_sorted_scales[:].bitcast(U16).rearrange("p (b t u) -> p b t u", b=2, t=SLOTS),
+            wp_plane[:].bitcast(U16).rearrange("p (b u t) -> p b t u", b=2, t=SLOTS),
+        )
         prepare_wc(0, 0, range(SLOTS), SLOTS)
         for s in range(2):
             v2_codes[s] = gather("v2_codes%d" % s, tab2_sb, U32, idx2, s)
         for s in range(2):
-            v_codes[1, s] = gather("v_codes1%d" % s, tab_sb1, U32, idx, s)
+            v_codes[0, s] = gather("v_codes0%d" % s, tab_sb0, U32, idx, s)
         prepare_wc(1, 0, (2, 3), 1)
         prepare_wc(0, 1, (), SLOTS)
         wc_tiles(1, 1)
@@ -224,7 +220,7 @@ def tile_list_crystal_laplace_energies_kernel(
                 lhsT=wc_codes[a, b][:, rows].bitcast(FP8X4),
                 lhsT_scale=wc_scales[a, b][:, rows],
                 rhs=v_codes[a, s][:, cols].bitcast(FP8X4),
-                rhs_scale=v_scales[s][TAB_ROW * (a + 1) : P, cols],
+                rhs_scale=v_scales[TAB_ROW * a : P, s, cols],
                 start=start,
                 stop=stop,
             )
@@ -244,9 +240,12 @@ def tile_list_crystal_laplace_energies_kernel(
         def project_wide(b, s, indices):
             banks = [bank_tile(index) for index in indices]
             for t in range(SLOTS):
-                prototype_pass(banks[t][:], b, s, t, whole, True, False)
-                for a in range(2):
-                    crystal_pass(banks[t][:], b, s, t, a, whole, False, a == 1)
+                if b == 0:
+                    prototype_pass(banks[t][:], b, s, t, whole, True, False)
+                crystal_pass(banks[t][:], b, s, t, 0, whole, b == 1, False)
+                if b == 1:
+                    prototype_pass(banks[t][:], b, s, t, whole, False, False)
+                crystal_pass(banks[t][:], b, s, t, 1, whole, False, True)
             return banks
 
         def project_narrow(b, s, cols, indices):
@@ -260,8 +259,8 @@ def tile_list_crystal_laplace_energies_kernel(
                 crystal_pass(bank[:, first : first + width], b, s, t, 1, cols, False, True)
             return banks
 
-        def chunk_tiles(name, width, tag=None):
-            dist = held("dist" + name, [P, SLOTS * width], F32)
+        def chunk_tiles(name, width, tag=None, dist_tag=None):
+            dist = held("dist" + name, [P, SLOTS * width], F32, dist_tag)
             h_slots = held("h_slots" + name, [P, SLOTS, width], BF16)
             h_bf = held("h_bf" + name, [P, width, SLOTS], BF16, tag)
             return dist, h_slots, h_bf
@@ -271,7 +270,7 @@ def tile_list_crystal_laplace_energies_kernel(
 
         def take_exp(tiles, b, t, cols):
             dist = tiles[0][:].rearrange("p (t j) -> p t j", t=SLOTS)
-            nc.scalar.activation(tiles[1][:, t, cols], dist[:, t, cols], ACT.Exp, bias=horner[:, b, t, TERMS : TERMS + 1], scale=-1.0)
+            nc.scalar.activation(tiles[1][:, t, cols], dist[:, t, cols], ACT.Exp, bias=log_amp[:, b, t : t + 1], scale=-1.0)
 
         def interleave(tiles, cols):
             nc.vector.tensor_copy(
@@ -354,7 +353,7 @@ def tile_list_crystal_laplace_energies_kernel(
                 for t in range(SLOTS):
                     take_exp(tiles, b, t, cols)
 
-        wide = [chunk_tiles("00", HALF, "wc_bf00"), chunk_tiles("10", HALF)]
+        wide = [chunk_tiles("00", HALF, "wc_bf00"), chunk_tiles("10", HALF, None, "tab_sb1")]
         narrow = [chunk_tiles("e%d" % b, HALF // 2) for b in range(2)]
         laplace_wide(wide[0], project_wide(0, 0, (0, 1, 2, 3)), 0)
         laplace(narrow[0], project_narrow(0, 1, early, (4, 5)), 0)

@@ -23,8 +23,8 @@ PASS = P * SLOTS
 HALF = 512
 LIST_COLS = HALF // 16
 TAB_ROW = 4
-TERMS = 18
 SPREAD = P // 16
+TERMS = 18
 RUN = 4
 PAIR = 2
 
@@ -46,10 +46,10 @@ def tile_list_crystal_laplace_energies_kernel(
 
         tab_rows = held("tab_rows", [P, T // 4], I32)
         tab2_rows = held("tab2_rows", [P, T2 // 4], I32)
-        wp_plane = held("wp_plane", [P, H // 4], I32)
-        nc.vector.memset(tab2_rows[:], 0)
+        wp_rows = held("wp_rows", [P, H // 4], I32)
         nc.vector.memset(tab_rows[:], 0)
-        nc.vector.memset(wp_plane[:], 0)
+        nc.vector.memset(tab2_rows[:], 0)
+        nc.vector.memset(wp_rows[:], 0)
 
         def load_words(name, words):
             table = held(name, [P, words.shape[1]], I32)
@@ -72,19 +72,16 @@ def tile_list_crystal_laplace_energies_kernel(
         amp_sb = held("amp_sb", [P, 2, 8], F32)
 
         def load_amp(e):
-            nc.scalar.dma_start(amp_sb[e:P:2, :, 0:7], amp.rearrange("(b u x) -> u b x", b=2, x=8)[:, :, e : e + 7])
+            nc.sync.dma_start(amp_sb[e:P:2, :, 0:7], amp.rearrange("(b u x) -> u b x", b=2, x=8)[:, :, e : e + 7])
 
-        counts = held("counts", [P, 2, TERMS], F32)
-        nc.gpsimd.iota(counts[:, 0, :], [[1, TERMS]], base=-TERMS, channel_multiplier=0, allow_small_or_imprecise_dtypes=True)
         load_amp(0)
         load_amp(1)
-        nc.sync.dma_start(idx2[:], offs2)
-        nc.scalar.dma_start(tab2_rows[0:P:SPREAD, :], tab2_scales[0].bitcast(I32))
-        nc.scalar.dma_start(tab_rows[0 : P : SPREAD // 2, :], tab_scales.rearrange("a q t -> q a t").bitcast(I32))
-        for r in range(4):
-            nc.scalar.dma_start(wp_plane[r:P:32, :], wp_scales[0, r:16:4, :].bitcast(I32))
         nc.sync.dma_start(idx[:], offs)
+        nc.sync.dma_start(tab_rows[0 : P : SPREAD // 2, :], tab_scales.rearrange("a q t -> q a t").bitcast(I32))
         load_wc(0, 0)
+        nc.sync.dma_start(idx2[:], offs2)
+        nc.sync.dma_start(tab2_rows[0:P:SPREAD, :], tab2_scales[0].bitcast(I32))
+        nc.sync.dma_start(wp_rows[0:P:SPREAD, :], wp_scales[0].bitcast(I32))
         wp_sb = held("wp_sb", [P, H // 2], I32)
         nc.sync.dma_start(wp_sb[:], wp_words[0].bitcast(I32))
         tab_sb1 = load_words("tab_sb1", tab_words[1])
@@ -95,10 +92,13 @@ def tile_list_crystal_laplace_energies_kernel(
 
         addends = per_value("addends", F32, TERMS + 1)
         factors, horner = per_value("factors", F32, TERMS + 1), per_value("horner", F32, TERMS + 1)
+        ones, counts, inverses = held("ones", [P, TERMS], F32), held("counts", [P, TERMS], F32), held("inverses", [P, 1, TERMS], F32)
+        nc.vector.memset(ones[:], 1.0)
         nc.vector.memset(factors[:], 0.0)
-        nc.vector.reciprocal(counts[:, 1, :], counts[:, 0, :])
+        nc.vector.tensor_tensor_scan(counts[:], ones[:], ones[:], -1.0 - TERMS, ALU.mult, ALU.add)
+        nc.vector.reciprocal(inverses[:, 0, :], counts[:])
         runs = addends[:].rearrange("p b t k -> p (b t) k")
-        nc.vector.tensor_copy(runs[:, :, 0:TERMS], counts[:, 1:2, :].to_broadcast([P, 2 * SLOTS, TERMS]))
+        nc.scalar.activation(runs[:, :, 0:TERMS], inverses[:].to_broadcast([P, 2 * SLOTS, TERMS]), ACT.Copy)
         amp_bits = amp_sb[:].bitcast(I32)[:, :, 0:7:2]
         biased_exponent, mantissa_bits = held("biased_exponent", [P, 2, SLOTS], I32), held("mantissa_bits", [P, 2 * SLOTS, 1], I32)
         nc.vector.tensor_scalar(
@@ -113,14 +113,14 @@ def tile_list_crystal_laplace_energies_kernel(
             ALU.mult,
             ALU.add,
         )
-        nc.vector.tensor_scalar(addends[:, :, :, TERMS], biased_exponent[:], -127.0, math.log(2.0), ALU.add, ALU.mult)
+        nc.vector.tensor_scalar(
+            addends[:, :, :, TERMS], biased_exponent[:], math.log(2.0), math.log(1.5) - 127.0 * math.log(2.0), ALU.mult, ALU.add
+        )
         flat = "p b t k -> p (b t k)"
         nc.vector.tensor_tensor_scan(
             horner[:].rearrange(flat), factors[:].rearrange(flat), addends[:].rearrange(flat), 0.0, ALU.mult, ALU.add
         )
 
-        log_amp = held("log_amp", [P, 2, SLOTS], F32)
-        nc.scalar.activation(log_amp[:], horner[:, :, :, TERMS], ACT.Copy, bias=math.log(1.5))
 
         def gather(name, table, dtype, offsets, s, tag=None):
             picked = held(name, [P, HALF], dtype, tag)
@@ -160,16 +160,21 @@ def tile_list_crystal_laplace_energies_kernel(
 
         v_codes, v2_codes = {}, {}
         picked_rows = held("picked_rows", [P, 2 * S], U8)
-        planes = held("planes", [P, 2 * S // 4], I32)
-        nc.vector.tensor_copy(picked_rows[:, S : 2 * S], tab2_rows[:].bitcast(U8).indirect(idx2[:]))
+        planes = held("planes", [P, (2 * S + H) // 4], I32)
         nc.vector.tensor_copy(picked_rows[:, 0:S], tab_rows[:].bitcast(U8).indirect(idx[:]))
+        nc.vector.tensor_copy(picked_rows[:, S : 2 * S], tab2_rows[:].bitcast(U8).indirect(idx2[:]))
         spread = picked_rows[:].bitcast(I32)
-        nc.vector.tensor_copy(planes[:], spread)
-        v_cols, v2_cols = slice(0, S // 4), slice(S // 4, S // 2)
+        v_cols, v2_cols, wp_cols = slice(0, S // 4), slice(S // 4, S // 2), slice(S // 2, S // 2 + H // 4)
+        nc.vector.tensor_copy(planes[:, v_cols], spread[:, v_cols])
+        nc.vector.tensor_copy(
+            planes[:, wp_cols].bitcast(U16).rearrange("p (b t u) -> p b t u", b=2, t=SLOTS),
+            wp_rows[:].bitcast(U16).rearrange("p (b u t) -> p b t u", b=2, t=SLOTS),
+        )
+        nc.vector.tensor_copy(planes[:, v2_cols], spread[:, v2_cols])
         for r in range(1, 4):
-            nc.sync.dma_start(planes[r:P:32, :], spread[SPREAD * r : P : 32, :])
+            nc.sync.dma_start(planes[r:P:32, :], planes[SPREAD * r : P : 32, :])
         for r in range(1, 4):
-            nc.sync.dma_start(planes[TAB_ROW + r : P : 32, v_cols], spread[TAB_ROW + SPREAD * r : P : 32, v_cols])
+            nc.sync.dma_start(planes[TAB_ROW + r : P : 32, v_cols], planes[TAB_ROW + SPREAD * r : P : 32, v_cols])
         tab_sb0 = load_words("tab_sb0", tab_words[0])
         load_wc(1, 0)
         load_wc(0, 1)
@@ -181,14 +186,10 @@ def tile_list_crystal_laplace_energies_kernel(
         for s in range(2):
             v_codes[1, s] = gather("v_codes1%d" % s, tab_sb1, U32, idx, s)
         wp_codes = held("wp_codes", [P, 2 * H], U8)
-        wp_sorted_scales = held("wp_sorted_scales", [P, H], U8)
+        wp_sorted_scales = planes[:, wp_cols].bitcast(U8)
         nc.vector.tensor_copy(
             wp_codes[:].bitcast(I32).rearrange("p (b t u) -> p b t u", b=2, t=SLOTS),
             wp_sb[:].rearrange("p (b u t) -> p b t u", b=2, t=SLOTS),
-        )
-        nc.vector.tensor_copy(
-            wp_sorted_scales[:].bitcast(U16).rearrange("p (b t u) -> p b t u", b=2, t=SLOTS),
-            wp_plane[:].bitcast(U16).rearrange("p (b u t) -> p b t u", b=2, t=SLOTS),
         )
         prepare_wc(0, 0, range(SLOTS), SLOTS)
         for s in range(2):
@@ -270,7 +271,7 @@ def tile_list_crystal_laplace_energies_kernel(
 
         def take_exp(tiles, b, t, cols):
             dist = tiles[0][:].rearrange("p (t j) -> p t j", t=SLOTS)
-            nc.scalar.activation(tiles[1][:, t, cols], dist[:, t, cols], ACT.Exp, bias=log_amp[:, b, t : t + 1], scale=-1.0)
+            nc.scalar.activation(tiles[1][:, t, cols], dist[:, t, cols], ACT.Exp, bias=horner[:, b, t, TERMS : TERMS + 1], scale=-1.0)
 
         def interleave(tiles, cols):
             nc.vector.tensor_copy(
@@ -389,15 +390,25 @@ def tile_list_crystal_laplace_energies_kernel(
                 readout_pass(early_out[n_tile // 2][:, first : first + HALF // 2], n_tile, b, 1, early)
         finish_h(late_first, 0, 1, late.start)
         store("early0", early_out[0], out_tiles[:, 0:2, HALF + early.start : HALF + early.stop], True)
-        late_out = [bank_tile(index) for index in n_tiles]
-        for n_tile in n_tiles:
-            readout_pass(late_out[n_tile][:, 0 : HALF // 2], n_tile, 0, 1, late)
         store("early1", early_out[1], out_tiles[:, 2:4, HALF + early.start : HALF + early.stop], True)
-        for i in range(2):
-            finish_h(last[i], 1, 1, ends[i].start)
-            for n_tile in n_tiles:
-                readout_pass(late_out[n_tile][:, i * P : (i + 1) * P], n_tile, 1, 1, ends[i], i == 1)
+        near_out = [bank_tile(6 + pair) for pair in range(2)]
+        late_out = [bank_tile(index) for index in n_tiles]
+        finish_h(last[0], 1, 1, ends[0].start)
         for n_tile in n_tiles:
-            staged = held("late%d" % n_tile, [P, HALF // 2], F32)
-            copy_out(staged[:], late_out[n_tile][:, 0 : HALF // 2], n_tile % 2 == 0)
-            nc.sync.dma_start(out_tiles[:, n_tile, HALF + late.start : HALF + late.stop], staged[:])
+            for b in range(2):
+                first = (n_tile % 2) * P
+                readout_pass(near_out[n_tile // 2][:, first : first + P], n_tile, b, 1, ends[0])
+        for n_tile in n_tiles:
+            readout_pass(late_out[n_tile][:, 0:P], n_tile, 0, 1, ends[1])
+        finish_h(last[1], 1, 1, ends[1].start)
+        near = held("near", [P, N // P, P], F32)
+        for pair in range(2):
+            copy_out(near[:, 2 * pair : 2 * pair + 2, :].rearrange("p a j -> p (a j)"), near_out[pair][:, 0 : 2 * P], pair == 0)
+        nc.sync.dma_start(out_tiles[:, :, HALF + ends[0].start : HALF + ends[0].stop], near[:])
+        for n_tile in n_tiles:
+            readout_pass(late_out[n_tile][:, 0:P], n_tile, 1, 1, ends[1])
+        for pair in range(2):
+            staged = held("late%d" % pair, [P, 2, P], F32)
+            for i in range(2):
+                copy_out(staged[:, i, :], late_out[2 * i + pair][:, 0:P], pair == 0)
+            nc.sync.dma_start(out_tiles[:, pair:4:2, HALF + ends[1].start : HALF + ends[1].stop], staged[:])

@@ -65,17 +65,13 @@ def tile_list_crystal_laplace_energies_kernel(
 
         def load_coef(b):
             coef_sb[b] = held("coef_sb%d" % b, [P, SLOTS, N], F32)
-            rows = coef[b * PASS : (b + 1) * PASS, :].rearrange("(u t e) n -> t u e n", t=SLOTS, e=2)
+            rows = coef[b * PASS : (b + 1) * PASS, :].rearrange("(u t e) n -> t u e n", t=SLOTS, e=RUN)
             for t in range(SLOTS):
                 nc.sync.dma_start(coef_sb[b][:, t, :], rows[t])
 
-        amp_sb = held("amp_sb", [P, 2, 8], F32)
-
-        def load_amp(e):
-            nc.sync.dma_start(amp_sb[e:P:2, :, 0:7], amp.rearrange("(b u x) -> u b x", b=2, x=8)[:, :, e : e + 7])
-
-        load_amp(0)
-        load_amp(1)
+        amp_sb = held("amp_sb", [P, 2, 16], F32)
+        for e in range(RUN):
+            nc.sync.dma_start(amp_sb[e:P:RUN, :, 0:13], amp.rearrange("(b u x) -> u b x", b=2, x=16)[:, :, e : e + 13])
         nc.sync.dma_start(idx[:], offs)
         nc.sync.dma_start(tab_rows[0 : P : SPREAD // 2, :], tab_scales.rearrange("a q t -> q a t").bitcast(I32))
         load_wc(0, 0)
@@ -99,7 +95,7 @@ def tile_list_crystal_laplace_energies_kernel(
         nc.vector.reciprocal(inverses[:, 0, :], counts[:])
         runs = addends[:].rearrange("p b t k -> p (b t) k")
         nc.scalar.activation(runs[:, :, 0:TERMS], inverses[:].to_broadcast([P, 2 * SLOTS, TERMS]), ACT.Copy)
-        amp_bits = amp_sb[:].bitcast(I32)[:, :, 0:7:2]
+        amp_bits = amp_sb[:].bitcast(I32)[:, :, 0:13:RUN]
         biased_exponent, mantissa_bits = held("biased_exponent", [P, 2, SLOTS], I32), held("mantissa_bits", [P, 2 * SLOTS, 1], I32)
         nc.vector.tensor_scalar(
             mantissa_bits[:].rearrange("p (b t) o -> p b (t o)", b=2), amp_bits, 0x007FFFFF, 0x3F800000, ALU.bitwise_and, ALU.bitwise_or
@@ -139,8 +135,8 @@ def tile_list_crystal_laplace_energies_kernel(
             wc_scales[a, b] = held("wc_scales%d%d" % (a, b), [P, PASS], U8)
 
         def round_wc(a, b, t, on_scalar):
-            rounded = wc_bf[a, b][:].rearrange("p t (u e) j -> p t u j e", e=2)
-            loaded = wc_sb[a, b][:].rearrange("p j (u t e) -> p t u j e", t=SLOTS, e=2)
+            rounded = wc_bf[a, b][:].rearrange("p t (u e) j -> p t u j e", e=RUN)
+            loaded = wc_sb[a, b][:].rearrange("p j (u t e) -> p t u j e", t=SLOTS, e=RUN)
             if on_scalar:
                 nc.scalar.activation(rounded[:, t], loaded[:, t], ACT.Copy, scale=-1.0)
             else:
@@ -167,8 +163,8 @@ def tile_list_crystal_laplace_energies_kernel(
         v_cols, v2_cols, wp_cols = slice(0, S // 4), slice(S // 4, S // 2), slice(S // 2, S // 2 + H // 4)
         nc.vector.tensor_copy(planes[:, v_cols], spread[:, v_cols])
         nc.vector.tensor_copy(
-            planes[:, wp_cols].bitcast(U16).rearrange("p (b t u) -> p b t u", b=2, t=SLOTS),
-            wp_rows[:].bitcast(U16).rearrange("p (b u t) -> p b t u", b=2, t=SLOTS),
+            planes[:, wp_cols].rearrange("p (b t u) -> p b t u", b=2, t=SLOTS),
+            wp_rows[:].rearrange("p (b u t) -> p b t u", b=2, t=SLOTS),
         )
         nc.vector.tensor_copy(planes[:, v2_cols], spread[:, v2_cols])
         for r in range(1, 4):
@@ -188,8 +184,8 @@ def tile_list_crystal_laplace_energies_kernel(
         wp_codes = held("wp_codes", [P, 2 * H], U8)
         wp_sorted_scales = planes[:, wp_cols].bitcast(U8)
         nc.vector.tensor_copy(
-            wp_codes[:].bitcast(I32).rearrange("p (b t u) -> p b t u", b=2, t=SLOTS),
-            wp_sb[:].rearrange("p (b u t) -> p b t u", b=2, t=SLOTS),
+            wp_codes[:].bitcast(I32).rearrange("p (b t u w) -> p b t u w", b=2, t=SLOTS, w=2),
+            wp_sb[:].rearrange("p (b u t w) -> p b t u w", b=2, t=SLOTS, w=2),
         )
         prepare_wc(0, 0, range(SLOTS), SLOTS)
         for s in range(2):
@@ -309,8 +305,8 @@ def tile_list_crystal_laplace_energies_kernel(
         def round_coef(b):
             coef_bf[b] = held("coef_bf%d" % b, [P, N, SLOTS], BF16)
             nc.vector.tensor_copy(
-                coef_bf[b][:].rearrange("p (c i) t -> p c t i", i=PAIR),
-                coef_sb[b][:].rearrange("p t (c i) -> p c t i", i=PAIR),
+                coef_bf[b][:].rearrange("p (c i) t -> p c t i", i=RUN),
+                coef_sb[b][:].rearrange("p t (c i) -> p c t i", i=RUN),
             )
 
         def quantize_coef(b):

@@ -343,10 +343,9 @@ def tile_list_crystal_laplace_energies_kernel(
         early, late = pieces(whole, HALF // 2)
 
         def laplace_wide(tiles, banks, b):
+            for t in range(SLOTS):
+                take_abs(tiles, banks, t)
             for cols in (early, late):
-                for t in range(SLOTS):
-                    dist = tiles[0][:, t * HALF : (t + 1) * HALF]
-                    nc.scalar.activation(dist[:, cols], banks[t][:, cols], ACT.Abs)
                 for t in range(SLOTS):
                     take_exp(tiles, b, t, cols)
 
@@ -354,7 +353,7 @@ def tile_list_crystal_laplace_energies_kernel(
         narrow = [chunk_tiles("e%d" % b, HALF // 2) for b in range(2)]
         laplace_wide(wide[0], project_wide(0, 0, (0, 1, 2, 3)), 0)
         laplace(narrow[0], project_narrow(0, 1, early, (4, 5)), 0)
-        laplace_wide(wide[1], project_wide(1, 0, (6, 7, 0, 1)), 1)
+        laplace(wide[1], project_wide(1, 0, (6, 7, 0, 1)), 1)
         laplace(narrow[1], project_narrow(1, 1, early, (2, 3)), 1)
         finish_h(wide[0], 0, 0, 0)
         round_coef(0)
@@ -379,7 +378,7 @@ def tile_list_crystal_laplace_energies_kernel(
         finish_h(narrow[1], 1, 1, early.start)
         for n_tile in n_tiles:
             store("first%d" % n_tile, first_out[n_tile], out_tiles[:, n_tile : n_tile + 1, 0:HALF], False)
-        early_out = [bank_tile(4 + pair) for pair in range(2)]
+        early_out = [bank_tile(index) for index in (4, 7)]
         for n_tile in n_tiles:
             for b in range(2):
                 first = (n_tile % 2) * (HALF // 2)
@@ -387,7 +386,7 @@ def tile_list_crystal_laplace_energies_kernel(
         finish_h(late_first, 0, 1, late.start)
         store("early0", early_out[0], out_tiles[:, 0:2, HALF + early.start : HALF + early.stop], True)
         store("early1", early_out[1], out_tiles[:, 2:4, HALF + early.start : HALF + early.stop], True)
-        near_out = [bank_tile(6 + pair) for pair in range(2)]
+        near_out = [bank_tile(5 + pair) for pair in range(2)]
         late_out = [bank_tile(index) for index in n_tiles]
         finish_h(last[0], 1, 1, ends[0].start)
         for n_tile in n_tiles:

@@ -18,15 +18,17 @@ ACT = mybir.ActivationFunctionType
 ALU = mybir.AluOpType
 
 P = 128
+QUADRANT = 32
 SLOTS = 4
 PASS = P * SLOTS
-HALF = 512
+BANK = 512
+HALF = S // 2
+QUARTER = S // 4
 LIST_COLS = HALF // 16
-TAB_ROW = 4
 SPREAD = P // 16
+SECOND = 4
 TERMS = 18
 RUN = 4
-PAIR = 2
 
 
 def tile_list_crystal_laplace_energies_kernel(
@@ -61,7 +63,7 @@ def tile_list_crystal_laplace_energies_kernel(
         def load_wc(a, b):
             wc_sb[a, b] = held("wc_sb%d%d" % (a, b), [P, SLOTS, PASS], F32)
             rows = wc[a * PASS : (a + 1) * PASS, b * PASS : (b + 1) * PASS]
-            nc.sync.dma_start(wc_sb[a, b][:], rows.rearrange("(p j) c -> p j c", j=SLOTS))
+            nc.sync.dma_start(wc_sb[a, b][:], rows.rearrange("(p i) c -> p i c", i=SLOTS))
 
         def load_coef(b):
             coef_sb[b] = held("coef_sb%d" % b, [P, SLOTS, N], F32)
@@ -69,9 +71,11 @@ def tile_list_crystal_laplace_energies_kernel(
             for t in range(SLOTS):
                 nc.sync.dma_start(coef_sb[b][:, t, :], rows[t])
 
-        amp_sb = held("amp_sb", [P, 2, 16], F32)
+        reach = RUN * (SLOTS - 1) + 1
+        amp_sb = held("amp_sb", [P, 2, RUN * SLOTS], F32)
+        amp_runs = amp.rearrange("(b u x) -> u b x", b=2, x=RUN * SLOTS)
         for e in range(RUN):
-            nc.sync.dma_start(amp_sb[e:P:RUN, :, 0:13], amp.rearrange("(b u x) -> u b x", b=2, x=16)[:, :, e : e + 13])
+            nc.sync.dma_start(amp_sb[e:P:RUN, :, 0:reach], amp_runs[:, :, e : e + reach])
         nc.sync.dma_start(idx[:], offs)
         nc.sync.dma_start(tab_rows[0 : P : SPREAD // 2, :], tab_scales.rearrange("a q t -> q a t").bitcast(I32))
         load_wc(0, 0)
@@ -83,26 +87,31 @@ def tile_list_crystal_laplace_energies_kernel(
         tab_sb1 = load_words("tab_sb1", tab_words[1])
         tab2_sb = load_words("tab2_sb", tab2_words[0])
 
-        def per_value(name, dtype, width):
-            return held(name, [P, 2, SLOTS, width], dtype)
+        def runs_of(name):
+            return held(name, [P, 2 * SLOTS, TERMS + 1], F32)
 
-        addends = per_value("addends", F32, TERMS + 1)
-        factors, horner = per_value("factors", F32, TERMS + 1), per_value("horner", F32, TERMS + 1)
-        ones, counts, inverses = held("ones", [P, TERMS], F32), held("counts", [P, TERMS], F32), held("inverses", [P, 1, TERMS], F32)
+        addends, factors, horner = runs_of("addends"), runs_of("factors"), runs_of("horner")
+        ones, counts = held("ones", [P, TERMS], F32), held("counts", [P, TERMS], F32)
+        inverses = held("inverses", [P, 1, TERMS], F32)
         nc.vector.memset(ones[:], 1.0)
         nc.vector.memset(factors[:], 0.0)
         nc.vector.tensor_tensor_scan(counts[:], ones[:], ones[:], -1.0 - TERMS, ALU.mult, ALU.add)
         nc.vector.reciprocal(inverses[:, 0, :], counts[:])
-        runs = addends[:].rearrange("p b t k -> p (b t) k")
-        nc.scalar.activation(runs[:, :, 0:TERMS], inverses[:].to_broadcast([P, 2 * SLOTS, TERMS]), ACT.Copy)
-        amp_bits = amp_sb[:].bitcast(I32)[:, :, 0:13:RUN]
-        biased_exponent, mantissa_bits = held("biased_exponent", [P, 2, SLOTS], I32), held("mantissa_bits", [P, 2 * SLOTS, 1], I32)
+        nc.scalar.activation(addends[:, :, 0:TERMS], inverses[:].to_broadcast([P, 2 * SLOTS, TERMS]), ACT.Copy)
+        amp_bits = amp_sb[:].bitcast(I32)[:, :, 0:reach:RUN]
+        biased_exponent = held("biased_exponent", [P, 2, SLOTS], I32)
+        mantissa_bits = held("mantissa_bits", [P, 2 * SLOTS, 1], I32)
         nc.vector.tensor_scalar(
-            mantissa_bits[:].rearrange("p (b t) o -> p b (t o)", b=2), amp_bits, 0x007FFFFF, 0x3F800000, ALU.bitwise_and, ALU.bitwise_or
+            mantissa_bits[:].rearrange("p (b t) o -> p b (t o)", b=2),
+            amp_bits,
+            0x007FFFFF,
+            0x3F800000,
+            ALU.bitwise_and,
+            ALU.bitwise_or,
         )
         nc.vector.tensor_scalar(biased_exponent[:], amp_bits, 23, None, ALU.logical_shift_right)
         nc.vector.tensor_scalar(
-            factors[:].rearrange("p b t k -> p (b t) k")[:, :, 1 : TERMS + 1],
+            factors[:, :, 1 : TERMS + 1],
             mantissa_bits[:].bitcast(F32).to_broadcast([P, 2 * SLOTS, TERMS]),
             -1.0 / 1.5,
             1.0,
@@ -110,17 +119,53 @@ def tile_list_crystal_laplace_energies_kernel(
             ALU.add,
         )
         nc.vector.tensor_scalar(
-            addends[:, :, :, TERMS], biased_exponent[:], math.log(2.0), math.log(1.5) - 127.0 * math.log(2.0), ALU.mult, ALU.add
+            addends[:].rearrange("p (b t) k -> p b t k", b=2)[:, :, :, TERMS],
+            biased_exponent[:],
+            math.log(2.0),
+            math.log(1.5) - 127.0 * math.log(2.0),
+            ALU.mult,
+            ALU.add,
         )
-        flat = "p b t k -> p (b t k)"
+        flat = "p v k -> p (v k)"
         nc.vector.tensor_tensor_scan(
             horner[:].rearrange(flat), factors[:].rearrange(flat), addends[:].rearrange(flat), 0.0, ALU.mult, ALU.add
         )
 
+        def log_amp(b, t):
+            return horner[:, SLOTS * b + t, TERMS : TERMS + 1]
 
-        def gather(name, table, dtype, offsets, s, tag=None):
-            picked = held(name, [P, HALF], dtype, tag)
-            window = table[:].bitcast(dtype)
+        picked_rows = held("picked_rows", [P, 2 * S], U8)
+        planes = held("planes", [P, (2 * S + H) // 4], I32)
+        nc.vector.tensor_copy(picked_rows[:, 0:S], tab_rows[:].bitcast(U8).indirect(idx[:]))
+        nc.vector.tensor_copy(picked_rows[:, S : 2 * S], tab2_rows[:].bitcast(U8).indirect(idx2[:]))
+        picked_words = picked_rows[:].bitcast(I32)
+        v_cols, v2_cols, wp_cols = slice(0, S // 4), slice(S // 4, S // 2), slice(S // 2, S // 2 + H // 4)
+        nc.vector.tensor_copy(planes[:, v_cols], picked_words[:, v_cols])
+        nc.vector.tensor_copy(
+            planes[:, wp_cols].rearrange("p (b t u) -> p b t u", b=2, t=SLOTS),
+            wp_rows[:].rearrange("p (b u t) -> p b t u", b=2, t=SLOTS),
+        )
+        nc.vector.tensor_copy(planes[:, v2_cols], picked_words[:, v2_cols])
+        for r in range(1, 4):
+            nc.sync.dma_start(planes[r:P:QUADRANT, :], planes[SPREAD * r : P : QUADRANT, :])
+        for r in range(1, 4):
+            nc.sync.dma_start(
+                planes[SECOND + r : P : QUADRANT, v_cols], planes[SECOND + SPREAD * r : P : QUADRANT, v_cols]
+            )
+        v_scales = planes[:, v_cols].bitcast(U8).rearrange("p (s j) -> p s j", s=2)
+        v2_scales = planes[:, v2_cols].bitcast(U8).rearrange("p (s j) -> p s j", s=2)
+        wp_sorted_scales = planes[:, wp_cols].bitcast(U8)
+
+        tab_sb0 = load_words("tab_sb0", tab_words[0])
+        load_wc(1, 0)
+        load_wc(0, 1)
+        load_wc(1, 1)
+        load_coef(0)
+        load_coef(1)
+
+        def gather(name, table, offsets, s, tag=None):
+            picked = held(name, [P, HALF], U32, tag)
+            window = table[:].bitcast(U32)
             nc.vector.tensor_copy(picked[:], window.indirect(offsets[:, s * LIST_COLS : (s + 1) * LIST_COLS]))
             return picked
 
@@ -135,8 +180,8 @@ def tile_list_crystal_laplace_energies_kernel(
             wc_scales[a, b] = held("wc_scales%d%d" % (a, b), [P, PASS], U8)
 
         def round_wc(a, b, t, on_scalar):
-            rounded = wc_bf[a, b][:].rearrange("p t (u e) j -> p t u j e", e=RUN)
-            loaded = wc_sb[a, b][:].rearrange("p j (u t e) -> p t u j e", t=SLOTS, e=RUN)
+            rounded = wc_bf[a, b][:].rearrange("p t (u e) i -> p t u i e", e=RUN)
+            loaded = wc_sb[a, b][:].rearrange("p i (u t e) -> p t u i e", t=SLOTS, e=RUN)
             if on_scalar:
                 nc.scalar.activation(rounded[:, t], loaded[:, t], ACT.Copy, scale=-1.0)
             else:
@@ -144,7 +189,7 @@ def tile_list_crystal_laplace_energies_kernel(
 
         def quantize_wc(a, b, first, last):
             cols = slice(first * P, last * P)
-            grouped = wc_bf[a, b][:, first:last].rearrange("p t m j -> p (t m j)")
+            grouped = wc_bf[a, b][:, first:last].rearrange("p t m i -> p (t m i)")
             quantize(wc_codes[a, b][:, cols], wc_scales[a, b][:, cols], grouped)
 
         def prepare_wc(a, b, scalar_slots, width):
@@ -155,60 +200,38 @@ def tile_list_crystal_laplace_energies_kernel(
                 quantize_wc(a, b, first, first + width)
 
         v_codes, v2_codes = {}, {}
-        picked_rows = held("picked_rows", [P, 2 * S], U8)
-        planes = held("planes", [P, (2 * S + H) // 4], I32)
-        nc.vector.tensor_copy(picked_rows[:, 0:S], tab_rows[:].bitcast(U8).indirect(idx[:]))
-        nc.vector.tensor_copy(picked_rows[:, S : 2 * S], tab2_rows[:].bitcast(U8).indirect(idx2[:]))
-        spread = picked_rows[:].bitcast(I32)
-        v_cols, v2_cols, wp_cols = slice(0, S // 4), slice(S // 4, S // 2), slice(S // 2, S // 2 + H // 4)
-        nc.vector.tensor_copy(planes[:, v_cols], spread[:, v_cols])
-        nc.vector.tensor_copy(
-            planes[:, wp_cols].rearrange("p (b t u) -> p b t u", b=2, t=SLOTS),
-            wp_rows[:].rearrange("p (b u t) -> p b t u", b=2, t=SLOTS),
-        )
-        nc.vector.tensor_copy(planes[:, v2_cols], spread[:, v2_cols])
-        for r in range(1, 4):
-            nc.sync.dma_start(planes[r:P:32, :], planes[SPREAD * r : P : 32, :])
-        for r in range(1, 4):
-            nc.sync.dma_start(planes[TAB_ROW + r : P : 32, v_cols], planes[TAB_ROW + SPREAD * r : P : 32, v_cols])
-        tab_sb0 = load_words("tab_sb0", tab_words[0])
-        load_wc(1, 0)
-        load_wc(0, 1)
-        load_wc(1, 1)
-        load_coef(0)
-        load_coef(1)
-        v_scales = planes[:, v_cols].bitcast(U8).rearrange("p (s j) -> p s j", s=2)
-        v2_scales = planes[:, v2_cols].bitcast(U8).rearrange("p (s j) -> p s j", s=2)
         for s in range(2):
-            v_codes[1, s] = gather("v_codes1%d" % s, tab_sb1, U32, idx, s)
+            v_codes[1, s] = gather("v_codes1%d" % s, tab_sb1, idx, s)
         wp_codes = held("wp_codes", [P, 2 * H], U8)
-        wp_sorted_scales = planes[:, wp_cols].bitcast(U8)
         nc.vector.tensor_copy(
             wp_codes[:].bitcast(I32).rearrange("p (b t u w) -> p b t u w", b=2, t=SLOTS, w=2),
             wp_sb[:].rearrange("p (b u t w) -> p b t u w", b=2, t=SLOTS, w=2),
         )
         prepare_wc(0, 0, range(SLOTS), SLOTS)
         for s in range(2):
-            v2_codes[s] = gather("v2_codes%d" % s, tab2_sb, U32, idx2, s)
-        for s in range(2):
-            v_codes[0, s] = gather("v_codes0%d" % s, tab_sb0, U32, idx, s)
-        prepare_wc(1, 0, (2, 3), 1)
-        prepare_wc(0, 1, (), SLOTS)
-        wc_tiles(1, 1)
-        for t in range(SLOTS):
-            round_wc(1, 1, t, False)
-            if t > 0:
-                quantize_wc(1, 1, t - 1, t)
-        quantize_wc(1, 1, SLOTS - 1, SLOTS)
+            v2_codes[s] = gather("v2_codes%d" % s, tab2_sb, idx2, s)
+        v_codes[0, 0] = gather("v_codes00", tab_sb0, idx, 0)
+        prepare_wc(1, 0, range(SLOTS // 2, SLOTS), 1)
+        v_codes[0, 1] = gather("v_codes01", tab_sb0, idx, 1, "wc_sb10")
+        for a in range(2):
+            wc_tiles(a, 1)
+            for t in range(SLOTS):
+                round_wc(a, 1, t, False)
+                if t == SLOTS // 2:
+                    quantize_wc(a, 1, 0, SLOTS // 2)
+            quantize_wc(a, 1, SLOTS // 2, SLOTS)
 
         def bank_tile(index):
-            return psum.tile([P, HALF], F32, name="bank%d" % index, tag="bank%d" % index)
+            return psum.tile([P, BANK], F32, name="bank%d" % index, tag="bank%d" % index)
 
         h_codes = {(b, s): held("h_codes%d%d" % (b, s), [P, HALF], U32) for b in range(2) for s in range(2)}
         h_scales = {(b, s): held("h_scales%d%d" % (b, s), [P, HALF], U8) for b in range(2) for s in range(2)}
 
         def pieces(cols, width):
             return [slice(first, first + width) for first in range(cols.start, cols.stop, width)]
+
+        whole = slice(0, HALF)
+        early, late = pieces(whole, QUARTER)
 
         def crystal_pass(sums, b, s, t, a, cols, start, stop):
             rows = slice(t * P, (t + 1) * P)
@@ -217,12 +240,12 @@ def tile_list_crystal_laplace_energies_kernel(
                 lhsT=wc_codes[a, b][:, rows].bitcast(FP8X4),
                 lhsT_scale=wc_scales[a, b][:, rows],
                 rhs=v_codes[a, s][:, cols].bitcast(FP8X4),
-                rhs_scale=v_scales[TAB_ROW * a : P, s, cols],
+                rhs_scale=v_scales[SECOND * a : P, s, cols],
                 start=start,
                 stop=stop,
             )
 
-        def prototype_pass(sums, b, s, t, cols, start, stop):
+        def prototype_pass(sums, b, s, t, cols, start):
             first = b * PASS + t * P
             nc.tensor.matmul_mx(
                 out=sums,
@@ -231,43 +254,53 @@ def tile_list_crystal_laplace_energies_kernel(
                 rhs=v2_codes[s][:, cols].bitcast(FP8X4),
                 rhs_scale=v2_scales[:, s, cols],
                 start=start,
-                stop=stop,
+                stop=False,
             )
 
-        def project_wide(b, s, indices):
+        def project_wide(b, indices):
             banks = [bank_tile(index) for index in indices]
             for t in range(SLOTS):
                 if b == 0:
-                    prototype_pass(banks[t][:], b, s, t, whole, True, False)
-                crystal_pass(banks[t][:], b, s, t, 0, whole, b == 1, False)
+                    prototype_pass(banks[t][:], b, 0, t, whole, True)
+                crystal_pass(banks[t][:], b, 0, t, 0, whole, b == 1, False)
                 if b == 1:
-                    prototype_pass(banks[t][:], b, s, t, whole, False, False)
-                crystal_pass(banks[t][:], b, s, t, 1, whole, False, True)
+                    prototype_pass(banks[t][:], b, 0, t, whole, False)
+                crystal_pass(banks[t][:], b, 0, t, 1, whole, False, True)
             return banks
 
-        def project_narrow(b, s, cols, indices):
+        def project_narrow(b, cols, indices):
             banks = [bank_tile(index) for index in indices]
             width = cols.stop - cols.start
             for t in range(SLOTS):
-                bank, first = banks[t * width // HALF], t * width % HALF
-                crystal_pass(bank[:, first : first + width], b, s, t, 0, cols, True, False)
+                bank, first = banks[t * width // BANK], t * width % BANK
+                crystal_pass(bank[:, first : first + width], b, 1, t, 0, cols, True, False)
                 for i, part in enumerate(pieces(cols, P)):
-                    prototype_pass(bank[:, first + i * P : first + (i + 1) * P], b, s, t, part, False, False)
-                crystal_pass(bank[:, first : first + width], b, s, t, 1, cols, False, True)
+                    prototype_pass(bank[:, first + i * P : first + (i + 1) * P], b, 1, t, part, False)
+                crystal_pass(bank[:, first : first + width], b, 1, t, 1, cols, False, True)
             return banks
 
-        def chunk_tiles(name, width, tag=None, dist_tag=None):
+        def chunk_tiles(name, width, dist_tag=None, h_bf_tag=None):
             dist = held("dist" + name, [P, SLOTS * width], F32, dist_tag)
             h_slots = held("h_slots" + name, [P, SLOTS, width], BF16)
-            h_bf = held("h_bf" + name, [P, width, SLOTS], BF16, tag)
+            h_bf = held("h_bf" + name, [P, width, SLOTS], BF16, h_bf_tag)
             return dist, h_slots, h_bf
 
         def take_abs(tiles, banks, i):
-            nc.scalar.activation(tiles[0][:, i * HALF : (i + 1) * HALF], banks[i][:], ACT.Abs)
+            nc.scalar.activation(tiles[0][:, i * BANK : (i + 1) * BANK], banks[i][:], ACT.Abs)
 
         def take_exp(tiles, b, t, cols):
             dist = tiles[0][:].rearrange("p (t j) -> p t j", t=SLOTS)
-            nc.scalar.activation(tiles[1][:, t, cols], dist[:, t, cols], ACT.Exp, bias=horner[:, b, t, TERMS : TERMS + 1], scale=-1.0)
+            nc.scalar.activation(tiles[1][:, t, cols], dist[:, t, cols], ACT.Exp, bias=log_amp(b, t), scale=-1.0)
+
+        def laplace(tiles, banks, b):
+            width = tiles[1].shape[2]
+            slots_a_bank = SLOTS // len(banks)
+            for i in range(len(banks) + 1):
+                if i < len(banks):
+                    take_abs(tiles, banks, i)
+                if i > 0:
+                    for t in range((i - 1) * slots_a_bank, i * slots_a_bank):
+                        take_exp(tiles, b, t, slice(0, width))
 
         def interleave(tiles, cols):
             nc.vector.tensor_copy(
@@ -280,25 +313,13 @@ def tile_list_crystal_laplace_energies_kernel(
             grouped = tiles[2][:, cols, :].rearrange("p j t -> p (j t)")
             quantize(h_codes[b, s][:, target], h_scales[b, s][:, target], grouped)
 
-        def laplace(tiles, banks, b):
-            width = tiles[1].shape[2]
-            slots_a_bank = SLOTS // len(banks)
-            for i in range(len(banks) + 1):
-                if i < len(banks):
-                    take_abs(tiles, banks, i)
-                if i > 0:
-                    for t in range((i - 1) * slots_a_bank, i * slots_a_bank):
-                        take_exp(tiles, b, t, slice(0, width))
-
         def finish_h(tiles, b, s, first):
             width = tiles[1].shape[2]
-            halves = pieces(slice(0, width), min(width, HALF // 2))
-            for cols in halves:
+            parts = pieces(slice(0, width), min(width, QUARTER))
+            for cols in parts:
                 interleave(tiles, cols)
-            for cols in halves:
+            for cols in parts:
                 quantize_h(tiles, cols, b, s, first)
-
-        whole = slice(0, HALF)
 
         coef_bf, coef_codes, coef_scales = {}, {}, {}
 
@@ -314,7 +335,7 @@ def tile_list_crystal_laplace_energies_kernel(
             coef_scales[b] = held("coef_scales%d" % b, [P, N], U8)
             quantize(coef_codes[b][:], coef_scales[b][:], coef_bf[b][:].rearrange("p n t -> p (n t)"))
 
-        def readout_pass(sums, n_tile, b, s, cols, closes=True):
+        def readout_pass(sums, n_tile, b, s, cols):
             rows = slice(n_tile * P, (n_tile + 1) * P)
             nc.tensor.matmul_mx(
                 out=sums,
@@ -323,8 +344,17 @@ def tile_list_crystal_laplace_energies_kernel(
                 rhs=h_codes[b, s][:, cols].bitcast(FP8X4),
                 rhs_scale=h_scales[b, s][:, cols],
                 start=(b == 0),
-                stop=(closes and b == 1),
+                stop=(b == 1),
             )
+
+        def read_out_paired(indices, cols):
+            banks = [bank_tile(index) for index in indices]
+            width = cols.stop - cols.start
+            for n_tile in n_tiles:
+                for b in range(2):
+                    first = (n_tile % 2) * width
+                    readout_pass(banks[n_tile // 2][:, first : first + width], n_tile, b, 1, cols)
+            return banks
 
         def copy_out(target, source, on_scalar):
             if on_scalar:
@@ -333,28 +363,27 @@ def tile_list_crystal_laplace_energies_kernel(
                 nc.vector.tensor_copy(target, source)
 
         def store(name, bank, target, on_scalar):
-            staged = held(name, [P, HALF], F32)
+            staged = held(name, [P, BANK], F32)
             copy_out(staged[:], bank[:], on_scalar)
             nc.sync.dma_start(target, staged[:].rearrange("p (a j) -> p a j", a=target.shape[1]))
 
         out_tiles = out.rearrange("(a p) j -> p a j", p=P)
         n_tiles = range(N // P)
 
-        early, late = pieces(whole, HALF // 2)
+        def second_half(cols):
+            return slice(HALF + cols.start, HALF + cols.stop)
 
-        def laplace_wide(tiles, banks, b):
+        wide = [chunk_tiles("00", HALF, None, "wc_bf00"), chunk_tiles("10", HALF, "tab_sb1")]
+        narrow = [chunk_tiles("e%d" % b, QUARTER) for b in range(2)]
+        opening = project_wide(0, (0, 1, 2, 3))
+        for t in range(SLOTS):
+            take_abs(wide[0], opening, t)
+        for cols in (early, late):
             for t in range(SLOTS):
-                take_abs(tiles, banks, t)
-            for cols in (early, late):
-                for t in range(SLOTS):
-                    take_exp(tiles, b, t, cols)
-
-        wide = [chunk_tiles("00", HALF, "wc_bf00"), chunk_tiles("10", HALF, None, "tab_sb1")]
-        narrow = [chunk_tiles("e%d" % b, HALF // 2) for b in range(2)]
-        laplace_wide(wide[0], project_wide(0, 0, (0, 1, 2, 3)), 0)
-        laplace(narrow[0], project_narrow(0, 1, early, (4, 5)), 0)
-        laplace(wide[1], project_wide(1, 0, (6, 7, 0, 1)), 1)
-        laplace(narrow[1], project_narrow(1, 1, early, (2, 3)), 1)
+                take_exp(wide[0], 0, t, cols)
+        laplace(narrow[0], project_narrow(0, early, (4, 5)), 0)
+        laplace(wide[1], project_wide(1, (6, 7, 0, 1)), 1)
+        laplace(narrow[1], project_narrow(1, early, (2, 3)), 1)
         finish_h(wide[0], 0, 0, 0)
         round_coef(0)
         finish_h(narrow[0], 0, 1, early.start)
@@ -365,45 +394,41 @@ def tile_list_crystal_laplace_energies_kernel(
         quantize_h(wide[1], early, 1, 0, 0)
         interleave(wide[1], late)
         quantize_h(wide[1], late, 1, 0, 0)
-        late_first = chunk_tiles("l0", HALF // 2)
-        laplace(late_first, project_narrow(0, 1, late, (4, 5)), 0)
-        first_out = [bank_tile(index) for index in n_tiles]
+        late_first = chunk_tiles("l0", QUARTER)
+        laplace(late_first, project_narrow(0, late, (4, 5)), 0)
+
+        first_out = [bank_tile(n_tile) for n_tile in n_tiles]
         for b in range(2):
             for n_tile in n_tiles:
                 readout_pass(first_out[n_tile][:], n_tile, b, 0, whole)
         ends = pieces(late, P)
         last = [chunk_tiles("l1%d" % i, P) for i in range(2)]
         for i in range(2):
-            laplace(last[i], project_narrow(1, 1, ends[i], (6 + i,)), 1)
+            laplace(last[i], project_narrow(1, ends[i], (6 + i,)), 1)
         finish_h(narrow[1], 1, 1, early.start)
         for n_tile in n_tiles:
-            store("first%d" % n_tile, first_out[n_tile], out_tiles[:, n_tile : n_tile + 1, 0:HALF], False)
-        early_out = [bank_tile(index) for index in (4, 7)]
-        for n_tile in n_tiles:
-            for b in range(2):
-                first = (n_tile % 2) * (HALF // 2)
-                readout_pass(early_out[n_tile // 2][:, first : first + HALF // 2], n_tile, b, 1, early)
+            store("first%d" % n_tile, first_out[n_tile], out_tiles[:, n_tile : n_tile + 1, whole], False)
+
+        early_out = read_out_paired((4, 7), early)
         finish_h(late_first, 0, 1, late.start)
-        store("early0", early_out[0], out_tiles[:, 0:2, HALF + early.start : HALF + early.stop], True)
-        store("early1", early_out[1], out_tiles[:, 2:4, HALF + early.start : HALF + early.stop], True)
-        near_out = [bank_tile(5 + pair) for pair in range(2)]
-        late_out = [bank_tile(index) for index in n_tiles]
+        for pair in range(2):
+            store("early%d" % pair, early_out[pair], out_tiles[:, 2 * pair : 2 * pair + 2, second_half(early)], True)
+
         finish_h(last[0], 1, 1, ends[0].start)
+        near_out = read_out_paired((5, 6), ends[0])
+        end_out = [bank_tile(n_tile) for n_tile in n_tiles]
         for n_tile in n_tiles:
-            for b in range(2):
-                first = (n_tile % 2) * P
-                readout_pass(near_out[n_tile // 2][:, first : first + P], n_tile, b, 1, ends[0])
-        for n_tile in n_tiles:
-            readout_pass(late_out[n_tile][:, 0:P], n_tile, 0, 1, ends[1])
+            readout_pass(end_out[n_tile][:, 0:P], n_tile, 0, 1, ends[1])
         finish_h(last[1], 1, 1, ends[1].start)
         near = held("near", [P, N // P, P], F32)
         for pair in range(2):
-            copy_out(near[:, 2 * pair : 2 * pair + 2, :].rearrange("p a j -> p (a j)"), near_out[pair][:, 0 : 2 * P], pair == 0)
-        nc.sync.dma_start(out_tiles[:, :, HALF + ends[0].start : HALF + ends[0].stop], near[:])
+            target = near[:, 2 * pair : 2 * pair + 2, :].rearrange("p a j -> p (a j)")
+            copy_out(target, near_out[pair][:, 0 : 2 * P], pair == 0)
+        nc.sync.dma_start(out_tiles[:, :, second_half(ends[0])], near[:])
         for n_tile in n_tiles:
-            readout_pass(late_out[n_tile][:, 0:P], n_tile, 1, 1, ends[1])
-        for pair in range(2):
-            staged = held("late%d" % pair, [P, 2, P], F32)
+            readout_pass(end_out[n_tile][:, 0:P], n_tile, 1, 1, ends[1])
+        for parity in range(2):
+            staged = held("end%d" % parity, [P, 2, P], F32)
             for i in range(2):
-                copy_out(staged[:, i, :], late_out[2 * i + pair][:, 0:P], pair == 0)
-            nc.sync.dma_start(out_tiles[:, pair:4:2, HALF + ends[1].start : HALF + ends[1].stop], staged[:])
+                copy_out(staged[:, i, :], end_out[2 * i + parity][:, 0:P], parity == 0)
+            nc.sync.dma_start(out_tiles[:, parity : N // P : 2, second_half(ends[1])], staged[:])

@@ -24,10 +24,10 @@ PASS = P * SLOTS
 BANK = 512
 HALF = S // 2
 QUARTER = S // 4
-LIST_COLS = HALF // 16
 SPREAD = P // 16
 SECOND = 4
-TERMS = 18
+STEPS = 3
+CENTRE = 0.043
 RUN = 4
 
 
@@ -60,10 +60,10 @@ def tile_list_crystal_laplace_energies_kernel(
 
         wc_sb, coef_sb = {}, {}
 
-        def load_wc(a, b):
+        def load_wc(a, b, last=SLOTS):
             wc_sb[a, b] = held("wc_sb%d%d" % (a, b), [P, SLOTS, PASS], F32)
             rows = wc[a * PASS : (a + 1) * PASS, b * PASS : (b + 1) * PASS]
-            nc.sync.dma_start(wc_sb[a, b][:], rows.rearrange("(p i) c -> p i c", i=SLOTS))
+            nc.sync.dma_start(wc_sb[a, b][:, 0:last], rows.rearrange("(p i) c -> p i c", i=SLOTS)[:, 0:last])
 
         def load_coef(b):
             coef_sb[b] = held("coef_sb%d" % b, [P, SLOTS, N], F32)
@@ -74,65 +74,19 @@ def tile_list_crystal_laplace_energies_kernel(
         reach = RUN * (SLOTS - 1) + 1
         amp_sb = held("amp_sb", [P, 2, RUN * SLOTS], F32)
         amp_runs = amp.rearrange("(b u x) -> u b x", b=2, x=RUN * SLOTS)
-        for e in range(RUN):
-            nc.sync.dma_start(amp_sb[e:P:RUN, :, 0:reach], amp_runs[:, :, e : e + reach])
         nc.sync.dma_start(idx[:], offs)
+        load_wc(0, 0, 1)
         nc.sync.dma_start(tab_rows[0 : P : SPREAD // 2, :], tab_scales.rearrange("a q t -> q a t").bitcast(I32))
-        load_wc(0, 0)
+        nc.sync.dma_start(wc_sb[0, 0][:, 1:SLOTS], wc[0:PASS, 0:PASS].rearrange("(p i) c -> p i c", i=SLOTS)[:, 1:SLOTS])
         nc.sync.dma_start(idx2[:], offs2)
         nc.sync.dma_start(tab2_rows[0:P:SPREAD, :], tab2_scales[0].bitcast(I32))
         nc.sync.dma_start(wp_rows[0:P:SPREAD, :], wp_scales[0].bitcast(I32))
         wp_sb = held("wp_sb", [P, H // 2], I32)
         nc.sync.dma_start(wp_sb[:], wp_words[0].bitcast(I32))
         tab_sb1 = load_words("tab_sb1", tab_words[1])
+        for e in range(RUN):
+            nc.sync.dma_start(amp_sb[e:P:RUN, :, 0:reach], amp_runs[:, :, e : e + reach])
         tab2_sb = load_words("tab2_sb", tab2_words[0])
-
-        def runs_of(name):
-            return held(name, [P, 2 * SLOTS, TERMS + 1], F32)
-
-        addends, factors, horner = runs_of("addends"), runs_of("factors"), runs_of("horner")
-        ones, counts = held("ones", [P, TERMS], F32), held("counts", [P, TERMS], F32)
-        inverses = held("inverses", [P, 1, TERMS], F32)
-        nc.vector.memset(ones[:], 1.0)
-        nc.vector.memset(factors[:], 0.0)
-        nc.vector.tensor_tensor_scan(counts[:], ones[:], ones[:], -1.0 - TERMS, ALU.mult, ALU.add)
-        nc.vector.reciprocal(inverses[:, 0, :], counts[:])
-        nc.scalar.activation(addends[:, :, 0:TERMS], inverses[:].to_broadcast([P, 2 * SLOTS, TERMS]), ACT.Copy)
-        amp_bits = amp_sb[:].bitcast(I32)[:, :, 0:reach:RUN]
-        biased_exponent = held("biased_exponent", [P, 2, SLOTS], I32)
-        mantissa_bits = held("mantissa_bits", [P, 2 * SLOTS, 1], I32)
-        nc.vector.tensor_scalar(
-            mantissa_bits[:].rearrange("p (b t) o -> p b (t o)", b=2),
-            amp_bits,
-            0x007FFFFF,
-            0x3F800000,
-            ALU.bitwise_and,
-            ALU.bitwise_or,
-        )
-        nc.vector.tensor_scalar(biased_exponent[:], amp_bits, 23, None, ALU.logical_shift_right)
-        nc.vector.tensor_scalar(
-            factors[:, :, 1 : TERMS + 1],
-            mantissa_bits[:].bitcast(F32).to_broadcast([P, 2 * SLOTS, TERMS]),
-            -1.0 / 1.5,
-            1.0,
-            ALU.mult,
-            ALU.add,
-        )
-        nc.vector.tensor_scalar(
-            addends[:].rearrange("p (b t) k -> p b t k", b=2)[:, :, :, TERMS],
-            biased_exponent[:],
-            math.log(2.0),
-            math.log(1.5) - 127.0 * math.log(2.0),
-            ALU.mult,
-            ALU.add,
-        )
-        flat = "p v k -> p (v k)"
-        nc.vector.tensor_tensor_scan(
-            horner[:].rearrange(flat), factors[:].rearrange(flat), addends[:].rearrange(flat), 0.0, ALU.mult, ALU.add
-        )
-
-        def log_amp(b, t):
-            return horner[:, SLOTS * b + t, TERMS : TERMS + 1]
 
         picked_rows = held("picked_rows", [P, 2 * S], U8)
         planes = held("planes", [P, (2 * S + H) // 4], I32)
@@ -141,9 +95,9 @@ def tile_list_crystal_laplace_energies_kernel(
         picked_words = picked_rows[:].bitcast(I32)
         v_cols, v2_cols, wp_cols = slice(0, S // 4), slice(S // 4, S // 2), slice(S // 2, S // 2 + H // 4)
         nc.vector.tensor_copy(planes[:, v_cols], picked_words[:, v_cols])
-        nc.vector.tensor_copy(
-            planes[:, wp_cols].rearrange("p (b t u) -> p b t u", b=2, t=SLOTS),
-            wp_rows[:].rearrange("p (b u t) -> p b t u", b=2, t=SLOTS),
+        nc.scalar.copy(
+            planes[:, wp_cols].bitcast(U32).rearrange("p (b t u) -> p b t u", b=2, t=SLOTS),
+            wp_rows[:].bitcast(U32).rearrange("p (b u t) -> p b t u", b=2, t=SLOTS),
         )
         nc.vector.tensor_copy(planes[:, v2_cols], picked_words[:, v2_cols])
         for r in range(1, 4):
@@ -156,17 +110,19 @@ def tile_list_crystal_laplace_energies_kernel(
         v2_scales = planes[:, v2_cols].bitcast(U8).rearrange("p (s j) -> p s j", s=2)
         wp_sorted_scales = planes[:, wp_cols].bitcast(U8)
 
-        tab_sb0 = load_words("tab_sb0", tab_words[0])
         load_wc(1, 0)
+        tab_sb0 = load_words("tab_sb0", tab_words[0])
         load_wc(0, 1)
         load_wc(1, 1)
         load_coef(0)
         load_coef(1)
 
-        def gather(name, table, offsets, s, tag=None):
-            picked = held(name, [P, HALF], U32, tag)
+        def gather(name, table, offsets, s, width=HALF):
+            picked = held(name, [P, HALF], U32)
             window = table[:].bitcast(U32)
-            nc.vector.tensor_copy(picked[:], window.indirect(offsets[:, s * LIST_COLS : (s + 1) * LIST_COLS]))
+            for first in range(0, HALF, width):
+                entries = slice((s * HALF + first) // 16, (s * HALF + first + width) // 16)
+                nc.vector.tensor_copy(picked[:, first : first + width], window.indirect(offsets[:, entries]))
             return picked
 
         def quantize(codes, scales, grouped):
@@ -176,7 +132,7 @@ def tile_list_crystal_laplace_energies_kernel(
 
         def wc_tiles(a, b):
             wc_bf[a, b] = held("wc_bf%d%d" % (a, b), [P, SLOTS, P, SLOTS], BF16)
-            wc_codes[a, b] = held("wc_codes%d%d" % (a, b), [P, PASS], U32)
+            wc_codes[a, b] = held("wc_codes%d%d" % (a, b), [P, PASS], U32, None if a or b else "tab_sb1")
             wc_scales[a, b] = held("wc_scales%d%d" % (a, b), [P, PASS], U8)
 
         def round_wc(a, b, t, on_scalar):
@@ -203,16 +159,41 @@ def tile_list_crystal_laplace_energies_kernel(
         for s in range(2):
             v_codes[1, s] = gather("v_codes1%d" % s, tab_sb1, idx, s)
         wp_codes = held("wp_codes", [P, 2 * H], U8)
-        nc.vector.tensor_copy(
-            wp_codes[:].bitcast(I32).rearrange("p (b t u w) -> p b t u w", b=2, t=SLOTS, w=2),
-            wp_sb[:].rearrange("p (b u t w) -> p b t u w", b=2, t=SLOTS, w=2),
+        nc.scalar.copy(
+            wp_codes[:].bitcast(U32).rearrange("p (b t u w) -> p b t u w", b=2, t=SLOTS, w=2),
+            wp_sb[:].bitcast(U32).rearrange("p (b u t w) -> p b t u w", b=2, t=SLOTS, w=2),
         )
         prepare_wc(0, 0, range(SLOTS), SLOTS)
+
+        shifted = [held("shifted%d" % k, [P, 2, SLOTS], F32, None if k else "wc_sb00") for k in range(STEPS + 1)]
+        nc.scalar.activation(
+            shifted[0][:],
+            amp_sb[:].bitcast(U32)[:, :, 0:reach:RUN],
+            ACT.Copy,
+            scale=math.log(2.0) / 2.0**23,
+            bias=(CENTRE - 127.0) * math.log(2.0) - STEPS,
+        )
+        for k in range(STEPS):
+            decay = held("decay%d" % k, [P, 2, SLOTS], F32)
+            nc.scalar.activation(decay[:], shifted[k][:], ACT.Exp, scale=-1.0, bias=float(k - STEPS))
+            for b in range(2):
+                for t in range(SLOTS):
+                    nc.scalar.activation(
+                        shifted[k + 1][:, b, t : t + 1],
+                        decay[:, b, t : t + 1],
+                        ACT.Identity,
+                        scale=amp_sb[:, b, RUN * t : RUN * t + 1],
+                        bias=shifted[k][:, b, t : t + 1],
+                    )
+
+        def log_amp(b, t):
+            return shifted[STEPS][:, b, t : t + 1]
+
         for s in range(2):
             v2_codes[s] = gather("v2_codes%d" % s, tab2_sb, idx2, s)
-        v_codes[0, 0] = gather("v_codes00", tab_sb0, idx, 0)
-        prepare_wc(1, 0, range(SLOTS // 2, SLOTS), 1)
-        v_codes[0, 1] = gather("v_codes01", tab_sb0, idx, 1, "wc_sb10")
+        prepare_wc(1, 0, range(SLOTS // 2, SLOTS), SLOTS // 2)
+        v_codes[0, 0] = gather("v_codes00", tab_sb0, idx, 0, QUARTER)
+        v_codes[0, 1] = gather("v_codes01", tab_sb0, idx, 1)
         for a in range(2):
             wc_tiles(a, 1)
             for t in range(SLOTS):
@@ -257,26 +238,23 @@ def tile_list_crystal_laplace_energies_kernel(
                 stop=False,
             )
 
-        def project_wide(b, indices):
-            banks = [bank_tile(index) for index in indices]
-            for t in range(SLOTS):
-                if b == 0:
-                    prototype_pass(banks[t][:], b, 0, t, whole, True)
-                crystal_pass(banks[t][:], b, 0, t, 0, whole, b == 1, False)
-                if b == 1:
-                    prototype_pass(banks[t][:], b, 0, t, whole, False)
-                crystal_pass(banks[t][:], b, 0, t, 1, whole, False, True)
-            return banks
-
-        def project_narrow(b, cols, indices):
+        def project(b, s, cols, indices):
             banks = [bank_tile(index) for index in indices]
             width = cols.stop - cols.start
-            for t in range(SLOTS):
-                bank, first = banks[t * width // BANK], t * width % BANK
-                crystal_pass(bank[:, first : first + width], b, 1, t, 0, cols, True, False)
-                for i, part in enumerate(pieces(cols, P)):
-                    prototype_pass(bank[:, first + i * P : first + (i + 1) * P], b, 1, t, part, False)
-                crystal_pass(bank[:, first : first + width], b, 1, t, 1, cols, False, True)
+            slots_a_bank = SLOTS // len(banks)
+            opens = (b, s) == (0, 0)
+            for i, bank in enumerate(banks):
+                slots = range(i * slots_a_bank, (i + 1) * slots_a_bank)
+                for step in range(3):
+                    for t in slots:
+                        sums = bank[:, (t - slots[0]) * width : (t - slots[0] + 1) * width]
+                        start, stop = step == 0 and t == slots[0], step == 2 and t == slots[-1]
+                        if step == (0 if opens else 1):
+                            prototype_pass(sums, b, s, t, cols, start)
+                        elif opens:
+                            crystal_pass(sums, b, s, t, 2 - step, cols, start, stop)
+                        else:
+                            crystal_pass(sums, b, s, t, step // 2, cols, start, stop)
             return banks
 
         def chunk_tiles(name, width, dist_tag=None, h_bf_tag=None):
@@ -373,29 +351,27 @@ def tile_list_crystal_laplace_energies_kernel(
         def second_half(cols):
             return slice(HALF + cols.start, HALF + cols.stop)
 
-        wide = [chunk_tiles("00", HALF, None, "wc_bf00"), chunk_tiles("10", HALF, "tab_sb1")]
+        opening = [chunk_tiles("00", QUARTER, None, "wc_bf00"), chunk_tiles("01", QUARTER)]
+        wide = chunk_tiles("10", HALF, "tab2_sb")
         narrow = [chunk_tiles("e%d" % b, QUARTER) for b in range(2)]
-        opening = project_wide(0, (0, 1, 2, 3))
-        for t in range(SLOTS):
-            take_abs(wide[0], opening, t)
-        for cols in (early, late):
-            for t in range(SLOTS):
-                take_exp(wide[0], 0, t, cols)
-        laplace(narrow[0], project_narrow(0, early, (4, 5)), 0)
-        laplace(wide[1], project_wide(1, (6, 7, 0, 1)), 1)
-        laplace(narrow[1], project_narrow(1, early, (2, 3)), 1)
-        finish_h(wide[0], 0, 0, 0)
+        laplace(opening[0], project(0, 0, early, (0, 1)), 0)
+        laplace(opening[1], project(0, 0, late, (2, 3)), 0)
+        laplace(narrow[0], project(0, 1, early, (4, 5)), 0)
+        laplace(wide, project(1, 0, whole, (6, 7, 0, 1)), 1)
+        laplace(narrow[1], project(1, 1, early, (2, 3)), 1)
+        finish_h(opening[0], 0, 0, early.start)
+        finish_h(opening[1], 0, 0, late.start)
         round_coef(0)
         finish_h(narrow[0], 0, 1, early.start)
         quantize_coef(0)
         round_coef(1)
-        interleave(wide[1], early)
+        interleave(wide, early)
         quantize_coef(1)
-        quantize_h(wide[1], early, 1, 0, 0)
-        interleave(wide[1], late)
-        quantize_h(wide[1], late, 1, 0, 0)
+        quantize_h(wide, early, 1, 0, 0)
+        interleave(wide, late)
+        quantize_h(wide, late, 1, 0, 0)
         late_first = chunk_tiles("l0", QUARTER)
-        laplace(late_first, project_narrow(0, late, (4, 5)), 0)
+        laplace(late_first, project(0, 1, late, (4, 5)), 0)
 
         first_out = [bank_tile(n_tile) for n_tile in n_tiles]
         for b in range(2):
@@ -404,7 +380,7 @@ def tile_list_crystal_laplace_energies_kernel(
         ends = pieces(late, P)
         last = [chunk_tiles("l1%d" % i, P) for i in range(2)]
         for i in range(2):
-            laplace(last[i], project_narrow(1, ends[i], (6 + i,)), 1)
+            laplace(last[i], project(1, 1, ends[i], (6 + i,)), 1)
         finish_h(narrow[1], 1, 1, early.start)
         for n_tile in n_tiles:
             store("first%d" % n_tile, first_out[n_tile], out_tiles[:, n_tile : n_tile + 1, whole], False)

@@ -60,10 +60,10 @@ def tile_list_crystal_laplace_energies_kernel(
 
         wc_sb, coef_sb = {}, {}
 
-        def load_wc(a, b, last=SLOTS):
+        def load_wc(a, b):
             wc_sb[a, b] = held("wc_sb%d%d" % (a, b), [P, SLOTS, PASS], F32)
             rows = wc[a * PASS : (a + 1) * PASS, b * PASS : (b + 1) * PASS]
-            nc.sync.dma_start(wc_sb[a, b][:, 0:last], rows.rearrange("(p i) c -> p i c", i=SLOTS)[:, 0:last])
+            nc.sync.dma_start(wc_sb[a, b][:], rows.rearrange("(p i) c -> p i c", i=SLOTS))
 
         def load_coef(b):
             coef_sb[b] = held("coef_sb%d" % b, [P, SLOTS, N], F32)
@@ -71,21 +71,18 @@ def tile_list_crystal_laplace_energies_kernel(
             for t in range(SLOTS):
                 nc.sync.dma_start(coef_sb[b][:, t, :], rows[t])
 
-        reach = RUN * (SLOTS - 1) + 1
-        amp_sb = held("amp_sb", [P, 2, RUN * SLOTS], F32)
-        amp_runs = amp.rearrange("(b u x) -> u b x", b=2, x=RUN * SLOTS)
+        amp_rows = held("amp_rows", [P, P], F32)
+        nc.vector.memset(amp_rows[:], 0.0)
         nc.sync.dma_start(idx[:], offs)
-        load_wc(0, 0, 1)
+        wp_sb = held("wp_sb", [P, H // 2], I32)
+        nc.sync.dma_start(wp_sb[:], wp_words[0].bitcast(I32))
         nc.sync.dma_start(tab_rows[0 : P : SPREAD // 2, :], tab_scales.rearrange("a q t -> q a t").bitcast(I32))
-        nc.sync.dma_start(wc_sb[0, 0][:, 1:SLOTS], wc[0:PASS, 0:PASS].rearrange("(p i) c -> p i c", i=SLOTS)[:, 1:SLOTS])
+        load_wc(0, 0)
         nc.sync.dma_start(idx2[:], offs2)
         nc.sync.dma_start(tab2_rows[0:P:SPREAD, :], tab2_scales[0].bitcast(I32))
         nc.sync.dma_start(wp_rows[0:P:SPREAD, :], wp_scales[0].bitcast(I32))
-        wp_sb = held("wp_sb", [P, H // 2], I32)
-        nc.sync.dma_start(wp_sb[:], wp_words[0].bitcast(I32))
+        nc.sync.dma_start(amp_rows[0 : P : QUADRANT // 2, :], amp.rearrange("(b q x) -> q b x", b=2, x=P))
         tab_sb1 = load_words("tab_sb1", tab_words[1])
-        for e in range(RUN):
-            nc.sync.dma_start(amp_sb[e:P:RUN, :, 0:reach], amp_runs[:, :, e : e + reach])
         tab2_sb = load_words("tab2_sb", tab2_words[0])
 
         picked_rows = held("picked_rows", [P, 2 * S], U8)
@@ -109,6 +106,14 @@ def tile_list_crystal_laplace_energies_kernel(
         v_scales = planes[:, v_cols].bitcast(U8).rearrange("p (s j) -> p s j", s=2)
         v2_scales = planes[:, v2_cols].bitcast(U8).rearrange("p (s j) -> p s j", s=2)
         wp_sorted_scales = planes[:, wp_cols].bitcast(U8)
+
+        amp_sorted, amp_turned = held("amp_sorted", [P, P], F32), held("amp_turned", [P, P], F32)
+        nc.scalar.copy(
+            amp_sorted[:].rearrange("p (t u e) -> p t u e", t=SLOTS, e=RUN),
+            amp_rows[:].rearrange("p (u t e) -> p t u e", t=SLOTS, e=RUN),
+        )
+        nc.vector.transpose(amp_turned[:], amp_sorted[:])
+        amp_sb = amp_turned[:].rearrange("p (t b x) -> p b t x", t=SLOTS, b=2)
 
         load_wc(1, 0)
         tab_sb0 = load_words("tab_sb0", tab_words[0])
@@ -168,7 +173,7 @@ def tile_list_crystal_laplace_energies_kernel(
         shifted = [held("shifted%d" % k, [P, 2, SLOTS], F32, None if k else "wc_sb00") for k in range(STEPS + 1)]
         nc.scalar.activation(
             shifted[0][:],
-            amp_sb[:].bitcast(U32)[:, :, 0:reach:RUN],
+            amp_turned[:].bitcast(U32).rearrange("p (t b x) -> p b t x", t=SLOTS, b=2)[:, :, :, 0],
             ACT.Copy,
             scale=math.log(2.0) / 2.0**23,
             bias=(CENTRE - 127.0) * math.log(2.0) - STEPS,
@@ -182,7 +187,7 @@ def tile_list_crystal_laplace_energies_kernel(
                         shifted[k + 1][:, b, t : t + 1],
                         decay[:, b, t : t + 1],
                         ACT.Identity,
-                        scale=amp_sb[:, b, RUN * t : RUN * t + 1],
+                        scale=amp_sb[:, b, t, 0:1],
                         bias=shifted[k][:, b, t : t + 1],
                     )
 

@@ -28,6 +28,7 @@ SPREAD = P // 16
 SECOND = 4
 STEPS = 3
 CENTRE = 0.043
+MOVED_BY_DMA = ("tab", "wp_sb", "wc_sb", "coef_sb", "first", "early", "near", "end")
 RUN = 4
 
 
@@ -41,7 +42,8 @@ def tile_list_crystal_laplace_energies_kernel(
         psum = ctx.enter_context(tc.psum_pool(name="psum", bufs=1))
 
         def held(name, shape, dtype, tag=None):
-            return keep.tile(shape, dtype, name=name, tag=tag or name, align_bytes=64)
+            moved = (tag or name).startswith(MOVED_BY_DMA)
+            return keep.tile(shape, dtype, name=name, tag=tag or name, align_bytes=256 if moved else 64)
 
         idx = lists.tile([P, S // 16], U16, name="idx")
         idx2 = lists.tile([P, S // 16], U16, name="idx2")

@@ -69,9 +69,8 @@ def tile_list_crystal_laplace_energies_kernel(
 
         def load_coef(b):
             coef_sb[b] = held("coef_sb%d" % b, [P, SLOTS, N], F32)
-            rows = coef[b * PASS : (b + 1) * PASS, :].rearrange("(u t e) n -> t u e n", t=SLOTS, e=RUN)
-            for t in range(SLOTS):
-                nc.sync.dma_start(coef_sb[b][:, t, :], rows[t])
+            rows = coef[b * PASS : (b + 1) * PASS, :]
+            nc.sync.dma_start(coef_sb[b][:], rows.rearrange("(p t) n -> p t n", t=SLOTS))
 
         amp_rows = held("amp_rows", [P, P], F32)
         nc.vector.memset(amp_rows[:], 0.0)
@@ -94,9 +93,9 @@ def tile_list_crystal_laplace_energies_kernel(
         picked_words = picked_rows[:].bitcast(I32)
         v_cols, v2_cols, wp_cols = slice(0, S // 4), slice(S // 4, S // 2), slice(S // 2, S // 2 + H // 4)
         nc.vector.tensor_copy(planes[:, v_cols], picked_words[:, v_cols])
-        nc.scalar.copy(
-            planes[:, wp_cols].bitcast(U32).rearrange("p (b t u) -> p b t u", b=2, t=SLOTS),
-            wp_rows[:].bitcast(U32).rearrange("p (b u t) -> p b t u", b=2, t=SLOTS),
+        nc.vector.tensor_copy(
+            planes[:, wp_cols].bitcast(U8).rearrange("p (b t m) -> p b m t", b=2, t=SLOTS),
+            wp_rows[:].bitcast(U8).rearrange("p (b m t) -> p b m t", b=2, t=SLOTS),
         )
         nc.vector.tensor_copy(planes[:, v2_cols], picked_words[:, v2_cols])
         for r in range(1, 4):
@@ -111,8 +110,8 @@ def tile_list_crystal_laplace_energies_kernel(
 
         amp_sorted, amp_turned = held("amp_sorted", [P, P], F32), held("amp_turned", [P, P], F32)
         nc.scalar.copy(
-            amp_sorted[:].rearrange("p (t u e) -> p t u e", t=SLOTS, e=RUN),
-            amp_rows[:].rearrange("p (u t e) -> p t u e", t=SLOTS, e=RUN),
+            amp_sorted[:].rearrange("p (t m) -> p t m", t=SLOTS),
+            amp_rows[:].rearrange("p (m t) -> p t m", t=SLOTS),
         )
         nc.vector.transpose(amp_turned[:], amp_sorted[:])
         amp_sb = amp_turned[:].rearrange("p (t b x) -> p b t x", t=SLOTS, b=2)
@@ -142,13 +141,14 @@ def tile_list_crystal_laplace_energies_kernel(
             wc_codes[a, b] = held("wc_codes%d%d" % (a, b), [P, PASS], U32, None if a or b else "tab_sb1")
             wc_scales[a, b] = held("wc_scales%d%d" % (a, b), [P, PASS], U8)
 
-        def round_wc(a, b, t, on_scalar):
-            rounded = wc_bf[a, b][:].rearrange("p t (u e) i -> p t u i e", e=RUN)
-            loaded = wc_sb[a, b][:].rearrange("p i (u t e) -> p t u i e", t=SLOTS, e=RUN)
+        def round_wc(a, b, pair, on_scalar):
+            slots = slice(2 * pair, 2 * pair + 2)
+            rounded = wc_bf[a, b][:].rearrange("p t m i -> p m i t")[:, :, :, slots]
+            loaded = wc_sb[a, b][:].rearrange("p i (m t) -> p m i t", t=SLOTS)[:, :, :, slots]
             if on_scalar:
-                nc.scalar.activation(rounded[:, t], loaded[:, t], ACT.Copy, scale=-1.0)
+                nc.scalar.activation(rounded, loaded, ACT.Copy, scale=-1.0)
             else:
-                nc.vector.tensor_scalar(rounded[:, t], loaded[:, t], -1.0, None, ALU.mult)
+                nc.vector.tensor_scalar(rounded, loaded, -1.0, None, ALU.mult)
 
         def quantize_wc(a, b, first, last):
             cols = slice(first * P, last * P)
@@ -157,8 +157,8 @@ def tile_list_crystal_laplace_energies_kernel(
 
         def prepare_wc(a, b, scalar_slots, width):
             wc_tiles(a, b)
-            for t in range(SLOTS):
-                round_wc(a, b, t, t in scalar_slots)
+            for pair in range(2):
+                round_wc(a, b, pair, 2 * pair in scalar_slots)
             for first in range(0, SLOTS, width):
                 quantize_wc(a, b, first, first + width)
 
@@ -167,8 +167,8 @@ def tile_list_crystal_laplace_energies_kernel(
             v_codes[1, s] = gather("v_codes1%d" % s, tab_sb1, idx, s)
         wp_codes = held("wp_codes", [P, 2 * H], U8)
         nc.scalar.copy(
-            wp_codes[:].bitcast(U32).rearrange("p (b t u w) -> p b t u w", b=2, t=SLOTS, w=2),
-            wp_sb[:].bitcast(U32).rearrange("p (b u t w) -> p b t u w", b=2, t=SLOTS, w=2),
+            wp_codes[:].bitcast(U16).rearrange("p (b t m) -> p b t m", b=2, t=SLOTS),
+            wp_sb[:].bitcast(U16).rearrange("p (b m t) -> p b t m", b=2, t=SLOTS),
         )
         prepare_wc(0, 0, range(SLOTS), SLOTS)
 
@@ -203,11 +203,10 @@ def tile_list_crystal_laplace_energies_kernel(
         v_codes[0, 1] = gather("v_codes01", tab_sb0, idx, 1)
         for a in range(2):
             wc_tiles(a, 1)
-            for t in range(SLOTS):
-                round_wc(a, 1, t, False)
-                if t == SLOTS // 2:
-                    quantize_wc(a, 1, 0, SLOTS // 2)
-            quantize_wc(a, 1, SLOTS // 2, SLOTS)
+            for pair in range(2):
+                round_wc(a, 1, pair, False)
+            for pair in range(2):
+                quantize_wc(a, 1, 2 * pair, 2 * pair + 2)
 
         def bank_tile(index):
             return psum.tile([P, BANK], F32, name="bank%d" % index, tag="bank%d" % index)

@@ -28,7 +28,6 @@ SPREAD = P // 16
 SECOND = 4
 STEPS = 3
 CENTRE = 0.043
-MOVED_BY_DMA = ("tab", "wp_sb", "wc_sb", "coef_sb", "first", "early", "near", "end")
 RUN = 4
 
 
@@ -42,8 +41,7 @@ def tile_list_crystal_laplace_energies_kernel(
         psum = ctx.enter_context(tc.psum_pool(name="psum", bufs=1))
 
         def held(name, shape, dtype, tag=None):
-            moved = (tag or name).startswith(MOVED_BY_DMA)
-            return keep.tile(shape, dtype, name=name, tag=tag or name, align_bytes=256 if moved else 64)
+            return keep.tile(shape, dtype, name=name, tag=tag or name, align_bytes=256)
 
         idx = lists.tile([P, S // 16], U16, name="idx")
         idx2 = lists.tile([P, S // 16], U16, name="idx2")
@@ -359,7 +357,7 @@ def tile_list_crystal_laplace_energies_kernel(
 
         opening = [chunk_tiles("00", QUARTER, None, "wc_bf00"), chunk_tiles("01", QUARTER)]
         wide = chunk_tiles("10", HALF, "tab2_sb")
-        narrow = [chunk_tiles("e%d" % b, QUARTER) for b in range(2)]
+        narrow = [chunk_tiles("e%d" % b, QUARTER, "dist0%d" % b) for b in range(2)]
         laplace(opening[0], project(0, 0, early, (0, 1)), 0)
         laplace(opening[1], project(0, 0, late, (2, 3)), 0)
         laplace(narrow[0], project(0, 1, early, (4, 5)), 0)
@@ -376,7 +374,7 @@ def tile_list_crystal_laplace_energies_kernel(
         quantize_h(wide, early, 1, 0, 0)
         interleave(wide, late)
         quantize_h(wide, late, 1, 0, 0)
-        late_first = chunk_tiles("l0", QUARTER)
+        late_first = chunk_tiles("l0", QUARTER, "dist00")
         laplace(late_first, project(0, 1, late, (4, 5)), 0)
 
         first_out = [bank_tile(n_tile) for n_tile in n_tiles]

@@ -76,12 +76,12 @@ def tile_list_crystal_laplace_energies_kernel(
         wp_sb = held("wp_sb", [P, H // 2], I32)
         nc.sync.dma_start(wp_sb[:], wp_words[0].bitcast(I32))
         nc.sync.dma_start(tab_rows[0 : P : SPREAD // 2, :], tab_scales.rearrange("a q t -> q a t").bitcast(I32))
-        load_wc(0, 0)
+        load_wc(1, 0)
         nc.sync.dma_start(idx2[:], offs2)
         nc.sync.dma_start(tab2_rows[0:P:SPREAD, :], tab2_scales[0].bitcast(I32))
         nc.sync.dma_start(wp_rows[0:P:SPREAD, :], wp_scales[0].bitcast(I32))
         nc.sync.dma_start(amp_rows[0 : P : QUADRANT // 2, :], amp.rearrange("(b q x) -> q b x", b=2, x=P))
-        tab_sb1 = load_words("tab_sb1", tab_words[1])
+        tab_sb0 = load_words("tab_sb0", tab_words[0])
         tab2_sb = load_words("tab2_sb", tab2_words[0])
 
         picked_rows = held("picked_rows", [P, 2 * S], U8)
@@ -90,19 +90,16 @@ def tile_list_crystal_laplace_energies_kernel(
         nc.vector.tensor_copy(picked_rows[:, S : 2 * S], tab2_rows[:].bitcast(U8).indirect(idx2[:]))
         picked_words = picked_rows[:].bitcast(I32)
         v_cols, v2_cols, wp_cols = slice(0, S // 4), slice(S // 4, S // 2), slice(S // 2, S // 2 + H // 4)
-        nc.vector.tensor_copy(planes[:, v_cols], picked_words[:, v_cols])
+        second_plane = held("second_plane", [P, S // 4], I32)
+        nc.vector.tensor_copy(second_plane[:], picked_words[:, v_cols])
         nc.vector.tensor_copy(
             planes[:, wp_cols].bitcast(U8).rearrange("p (b t m) -> p b m t", b=2, t=SLOTS),
             wp_rows[:].bitcast(U8).rearrange("p (b m t) -> p b m t", b=2, t=SLOTS),
         )
-        nc.vector.tensor_copy(planes[:, v2_cols], picked_words[:, v2_cols])
+        nc.vector.tensor_copy(planes[:, 0 : S // 2], picked_words)
         for r in range(1, 4):
             nc.sync.dma_start(planes[r:P:QUADRANT, :], planes[SPREAD * r : P : QUADRANT, :])
-        for r in range(1, 4):
-            nc.sync.dma_start(
-                planes[SECOND + r : P : QUADRANT, v_cols], planes[SECOND + SPREAD * r : P : QUADRANT, v_cols]
-            )
-        v_scales = planes[:, v_cols].bitcast(U8).rearrange("p (s j) -> p s j", s=2)
+        v_scales = [plane.bitcast(U8).rearrange("p (s j) -> p s j", s=2) for plane in (planes[:, v_cols], second_plane[SECOND:P, :])]
         v2_scales = planes[:, v2_cols].bitcast(U8).rearrange("p (s j) -> p s j", s=2)
         wp_sorted_scales = planes[:, wp_cols].bitcast(U8)
 
@@ -114,8 +111,10 @@ def tile_list_crystal_laplace_energies_kernel(
         nc.vector.transpose(amp_turned[:], amp_sorted[:])
         amp_sb = amp_turned[:].rearrange("p (t b x) -> p b t x", t=SLOTS, b=2)
 
-        load_wc(1, 0)
-        tab_sb0 = load_words("tab_sb0", tab_words[0])
+        load_wc(0, 0)
+        tab_sb1 = load_words("tab_sb1", tab_words[1])
+        for r in range(1, 4):
+            nc.sync.dma_start(second_plane[SECOND + r : P : QUADRANT, :], second_plane[SECOND + SPREAD * r : P : QUADRANT, :])
         load_wc(0, 1)
         load_wc(1, 1)
         load_coef(0)
@@ -136,7 +135,7 @@ def tile_list_crystal_laplace_energies_kernel(
 
         def wc_tiles(a, b):
             wc_bf[a, b] = held("wc_bf%d%d" % (a, b), [P, SLOTS, P, SLOTS], BF16)
-            wc_codes[a, b] = held("wc_codes%d%d" % (a, b), [P, PASS], U32, None if a or b else "tab_sb1")
+            wc_codes[a, b] = held("wc_codes%d%d" % (a, b), [P, PASS], U32, "tab_sb0" if (a, b) == (1, 0) else None)
             wc_scales[a, b] = held("wc_scales%d%d" % (a, b), [P, PASS], U8)
 
         def round_wc(a, b, pair, on_scalar):
@@ -162,15 +161,15 @@ def tile_list_crystal_laplace_energies_kernel(
 
         v_codes, v2_codes = {}, {}
         for s in range(2):
-            v_codes[1, s] = gather("v_codes1%d" % s, tab_sb1, idx, s)
+            v_codes[0, s] = gather("v_codes0%d" % s, tab_sb0, idx, s)
         wp_codes = held("wp_codes", [P, 2 * H], U8)
         nc.scalar.copy(
             wp_codes[:].bitcast(U16).rearrange("p (b t m) -> p b t m", b=2, t=SLOTS),
             wp_sb[:].bitcast(U16).rearrange("p (b m t) -> p b t m", b=2, t=SLOTS),
         )
-        prepare_wc(0, 0, range(SLOTS), SLOTS)
+        prepare_wc(1, 0, range(SLOTS), SLOTS)
 
-        shifted = [held("shifted%d" % k, [P, 2, SLOTS], F32, None if k else "wc_sb00") for k in range(STEPS + 1)]
+        shifted = [held("shifted%d" % k, [P, 2, SLOTS], F32, None if k else "wc_sb10") for k in range(STEPS + 1)]
         nc.scalar.activation(
             shifted[0][:],
             amp_turned[:].bitcast(U32).rearrange("p (t b x) -> p b t x", t=SLOTS, b=2)[:, :, :, 0],
@@ -196,9 +195,9 @@ def tile_list_crystal_laplace_energies_kernel(
 
         for s in range(2):
             v2_codes[s] = gather("v2_codes%d" % s, tab2_sb, idx2, s)
-        prepare_wc(1, 0, range(SLOTS // 2, SLOTS), SLOTS // 2)
-        v_codes[0, 0] = gather("v_codes00", tab_sb0, idx, 0, QUARTER)
-        v_codes[0, 1] = gather("v_codes01", tab_sb0, idx, 1)
+        prepare_wc(0, 0, range(SLOTS // 2, SLOTS), SLOTS // 2)
+        v_codes[1, 0] = gather("v_codes10", tab_sb1, idx, 0, QUARTER)
+        v_codes[1, 1] = gather("v_codes11", tab_sb1, idx, 1)
         for a in range(2):
             wc_tiles(a, 1)
             for pair in range(2):
@@ -225,7 +224,7 @@ def tile_list_crystal_laplace_energies_kernel(
                 lhsT=wc_codes[a, b][:, rows].bitcast(FP8X4),
                 lhsT_scale=wc_scales[a, b][:, rows],
                 rhs=v_codes[a, s][:, cols].bitcast(FP8X4),
-                rhs_scale=v_scales[SECOND * a : P, s, cols],
+                rhs_scale=v_scales[a][:, s, cols],
                 start=start,
                 stop=stop,
             )
@@ -256,9 +255,9 @@ def tile_list_crystal_laplace_energies_kernel(
                         if step == (0 if opens else 1):
                             prototype_pass(sums, b, s, t, cols, start)
                         elif opens:
-                            crystal_pass(sums, b, s, t, 2 - step, cols, start, stop)
+                            crystal_pass(sums, b, s, t, step - 1, cols, start, stop)
                         else:
-                            crystal_pass(sums, b, s, t, step // 2, cols, start, stop)
+                            crystal_pass(sums, b, s, t, step // 2 if b else 1 - step // 2, cols, start, stop)
             return banks
 
         def chunk_tiles(name, width, dist_tag=None, h_bf_tag=None):
@@ -355,7 +354,7 @@ def tile_list_crystal_laplace_energies_kernel(
         def second_half(cols):
             return slice(HALF + cols.start, HALF + cols.stop)
 
-        opening = [chunk_tiles("00", QUARTER, None, "wc_bf00"), chunk_tiles("01", QUARTER)]
+        opening = [chunk_tiles("00", QUARTER, None, "wc_bf10"), chunk_tiles("01", QUARTER)]
         wide = chunk_tiles("10", HALF, "tab2_sb")
         narrow = [chunk_tiles("e%d" % b, QUARTER, "dist0%d" % b) for b in range(2)]
         laplace(opening[0], project(0, 0, early, (0, 1)), 0)
@@ -386,11 +385,12 @@ def tile_list_crystal_laplace_energies_kernel(
         for i in range(2):
             laplace(last[i], project(1, 1, ends[i], (6 + i,)), 1)
         finish_h(narrow[1], 1, 1, early.start)
+        nc.gpsimd.tensor_copy(late_first[2][:], late_first[1][:].rearrange("p t j -> p j t"))
         for n_tile in n_tiles:
             store("first%d" % n_tile, first_out[n_tile], out_tiles[:, n_tile : n_tile + 1, whole], False)
 
         early_out = read_out_paired((4, 7), early)
-        finish_h(late_first, 0, 1, late.start)
+        quantize_h(late_first, early, 0, 1, late.start)
         for pair in range(2):
             store("early%d" % pair, early_out[pair], out_tiles[:, 2 * pair : 2 * pair + 2, second_half(early)], True)
 

@@ -91,12 +91,12 @@ def tile_list_crystal_laplace_energies_kernel(
         picked_words = picked_rows[:].bitcast(I32)
         v_cols, v2_cols, wp_cols = slice(0, S // 4), slice(S // 4, S // 2), slice(S // 2, S // 2 + H // 4)
         second_plane = held("second_plane", [P, S // 4], I32)
-        nc.vector.tensor_copy(second_plane[:], picked_words[:, v_cols])
-        nc.vector.tensor_copy(
-            planes[:, wp_cols].bitcast(U8).rearrange("p (b t m) -> p b m t", b=2, t=SLOTS),
-            wp_rows[:].bitcast(U8).rearrange("p (b m t) -> p b m t", b=2, t=SLOTS),
+        nc.gpsimd.tensor_copy(
+            planes[:, wp_cols].bitcast(U8).rearrange("p (b t m) -> p b t m", b=2, t=SLOTS),
+            wp_rows[:].bitcast(U8).rearrange("p (b m t) -> p b t m", b=2, t=SLOTS),
         )
         nc.vector.tensor_copy(planes[:, 0 : S // 2], picked_words)
+        nc.vector.tensor_copy(second_plane[:], planes[:, v_cols])
         for r in range(1, 4):
             nc.sync.dma_start(planes[r:P:QUADRANT, :], planes[SPREAD * r : P : QUADRANT, :])
         v_scales = [plane.bitcast(U8).rearrange("p (s j) -> p s j", s=2) for plane in (planes[:, v_cols], second_plane[SECOND:P, :])]
@@ -120,12 +120,12 @@ def tile_list_crystal_laplace_energies_kernel(
         load_coef(0)
         load_coef(1)
 
-        def gather(name, table, offsets, s, width=HALF):
+        def gather(name, table, offsets, s, cuts=(0, HALF)):
             picked = held(name, [P, HALF], U32)
             window = table[:].bitcast(U32)
-            for first in range(0, HALF, width):
-                entries = slice((s * HALF + first) // 16, (s * HALF + first + width) // 16)
-                nc.vector.tensor_copy(picked[:, first : first + width], window.indirect(offsets[:, entries]))
+            for first, last in zip(cuts, cuts[1:]):
+                entries = slice((s * HALF + first) // 16, (s * HALF + last) // 16)
+                nc.vector.tensor_copy(picked[:, first:last], window.indirect(offsets[:, entries]))
             return picked
 
         def quantize(codes, scales, grouped):
@@ -134,13 +134,17 @@ def tile_list_crystal_laplace_energies_kernel(
         wc_bf, wc_codes, wc_scales = {}, {}, {}
 
         def wc_tiles(a, b):
-            wc_bf[a, b] = held("wc_bf%d%d" % (a, b), [P, SLOTS, P, SLOTS], BF16)
+            if (a, b) == (1, 1):
+                wc_bf[a, b] = [held("wc_bf11%d" % pair, [P, 2, P, SLOTS], BF16, "wc_bf11")[:] for pair in range(2)]
+            else:
+                whole_block = held("wc_bf%d%d" % (a, b), [P, SLOTS, P, SLOTS], BF16)
+                wc_bf[a, b] = [whole_block[:, 0:2], whole_block[:, 2:4], whole_block[:]]
             wc_codes[a, b] = held("wc_codes%d%d" % (a, b), [P, PASS], U32, "tab_sb0" if (a, b) == (1, 0) else None)
             wc_scales[a, b] = held("wc_scales%d%d" % (a, b), [P, PASS], U8)
 
         def round_wc(a, b, pair, on_scalar):
             slots = slice(2 * pair, 2 * pair + 2)
-            rounded = wc_bf[a, b][:].rearrange("p t m i -> p m i t")[:, :, :, slots]
+            rounded = wc_bf[a, b][pair].rearrange("p t m i -> p m i t")
             loaded = wc_sb[a, b][:].rearrange("p i (m t) -> p m i t", t=SLOTS)[:, :, :, slots]
             if on_scalar:
                 nc.scalar.activation(rounded, loaded, ACT.Copy, scale=-1.0)
@@ -149,7 +153,7 @@ def tile_list_crystal_laplace_energies_kernel(
 
         def quantize_wc(a, b, first, last):
             cols = slice(first * P, last * P)
-            grouped = wc_bf[a, b][:, first:last].rearrange("p t m i -> p (t m i)")
+            grouped = wc_bf[a, b][first // 2 if last - first == 2 else 2].rearrange("p t m i -> p (t m i)")
             quantize(wc_codes[a, b][:, cols], wc_scales[a, b][:, cols], grouped)
 
         def prepare_wc(a, b, scalar_slots, width):
@@ -193,16 +197,15 @@ def tile_list_crystal_laplace_energies_kernel(
         def log_amp(b, t):
             return shifted[STEPS][:, b, t : t + 1]
 
-        for s in range(2):
-            v2_codes[s] = gather("v2_codes%d" % s, tab2_sb, idx2, s)
+        v2_codes[0] = gather("v2_codes0", tab2_sb, idx2, 0, (0, QUARTER, HALF))
+        v2_codes[1] = gather("v2_codes1", tab2_sb, idx2, 1)
         prepare_wc(0, 0, range(SLOTS // 2, SLOTS), SLOTS // 2)
-        v_codes[1, 0] = gather("v_codes10", tab_sb1, idx, 0, QUARTER)
+        v_codes[1, 0] = gather("v_codes10", tab_sb1, idx, 0, (0, P, QUARTER, HALF))
         v_codes[1, 1] = gather("v_codes11", tab_sb1, idx, 1)
         for a in range(2):
             wc_tiles(a, 1)
             for pair in range(2):
                 round_wc(a, 1, pair, False)
-            for pair in range(2):
                 quantize_wc(a, 1, 2 * pair, 2 * pair + 2)
 
         def bank_tile(index):
@@ -246,6 +249,7 @@ def tile_list_crystal_laplace_energies_kernel(
             width = cols.stop - cols.start
             slots_a_bank = SLOTS // len(banks)
             opens = (b, s) == (0, 0)
+            ahead = cols.start < QUARTER
             for i, bank in enumerate(banks):
                 slots = range(i * slots_a_bank, (i + 1) * slots_a_bank)
                 for step in range(3):
@@ -255,7 +259,7 @@ def tile_list_crystal_laplace_energies_kernel(
                         if step == (0 if opens else 1):
                             prototype_pass(sums, b, s, t, cols, start)
                         elif opens:
-                            crystal_pass(sums, b, s, t, step - 1, cols, start, stop)
+                            crystal_pass(sums, b, s, t, step - 1 if ahead else 2 - step, cols, start, stop)
                         else:
                             crystal_pass(sums, b, s, t, step // 2 if b else 1 - step // 2, cols, start, stop)
             return banks
@@ -357,7 +361,12 @@ def tile_list_crystal_laplace_energies_kernel(
         opening = [chunk_tiles("00", QUARTER, None, "wc_bf10"), chunk_tiles("01", QUARTER)]
         wide = chunk_tiles("10", HALF, "tab2_sb")
         narrow = [chunk_tiles("e%d" % b, QUARTER, "dist0%d" % b) for b in range(2)]
-        laplace(opening[0], project(0, 0, early, (0, 1)), 0)
+        opening_dist = opening[0][0][:].rearrange("p (t j) -> p t j", t=SLOTS)
+        for i, cols in enumerate(pieces(early, P)):
+            bank = project(0, 0, cols, (i,))[0]
+            nc.scalar.activation(opening_dist[:, :, cols], bank[:].rearrange("p (t j) -> p t j", t=SLOTS), ACT.Abs)
+        for t in range(SLOTS):
+            take_exp(opening[0], 0, t, early)
         laplace(opening[1], project(0, 0, late, (2, 3)), 0)
         laplace(narrow[0], project(0, 1, early, (4, 5)), 0)
         laplace(wide, project(1, 0, whole, (6, 7, 0, 1)), 1)

import math
from contextlib import ExitStack

import concourse.mybir as mybir

K, K2, T, T2, S, H, N = 1024, 512, 2048, 4096, 1024, 1024, 512
FLOPS = 2 * S * (K * H + K2 * H + H * N)

F32 = mybir.dt.float32
BF16 = mybir.dt.bfloat16
I32 = mybir.dt.int32
U32 = mybir.dt.uint32
U16 = mybir.dt.uint16
U8 = mybir.dt.uint8
FP8X4 = mybir.dt.float8_e4m3fn_x4
FP4X4 = mybir.dt.float4_e2m1fn_x4
ACT = mybir.ActivationFunctionType
ALU = mybir.AluOpType

P = 128
QUADRANT = 32
SLOTS = 4
PASS = P * SLOTS
BANK = 512
HALF = S // 2
QUARTER = S // 4
SPREAD = P // 16
SECOND = 4
STEPS = 3
CENTRE = 0.043
RUN = 4


def tile_list_crystal_laplace_energies_kernel(
    tc, tab_words, tab_scales, tab2_words, tab2_scales, offs, offs2, wc, wp_words, wp_scales, amp, coef, out
):
    nc = tc.nc
    with ExitStack() as ctx:
        lists = ctx.enter_context(tc.tile_pool(name="lists", bufs=1))
        keep = ctx.enter_context(tc.tile_pool(name="keep", bufs=1))
        psum = ctx.enter_context(tc.psum_pool(name="psum", bufs=1))

        def held(name, shape, dtype, tag=None):
            return keep.tile(shape, dtype, name=name, tag=tag or name, align_bytes=256)

        idx = lists.tile([P, S // 16], U16, name="idx")
        idx2 = lists.tile([P, S // 16], U16, name="idx2")

        tab_rows = held("tab_rows", [P, T // 4], I32)
        tab2_rows = held("tab2_rows", [P, T2 // 4], I32)
        wp_rows = held("wp_rows", [P, H // 4], I32)
        nc.vector.memset(tab_rows[:], 0)
        nc.vector.memset(tab2_rows[:], 0)
        nc.vector.memset(wp_rows[:], 0)

        def load_words(name, words):
            table = held(name, [P, words.shape[1]], I32)
            nc.sync.dma_start(table[:], words.rearrange("p t i -> p (t i)").bitcast(I32))
            return table

        wc_sb, coef_sb = {}, {}

        def load_wc(a, b):
            wc_sb[a, b] = held("wc_sb%d%d" % (a, b), [P, SLOTS, PASS], F32)
            rows = wc[a * PASS : (a + 1) * PASS, b * PASS : (b + 1) * PASS]
            nc.sync.dma_start(wc_sb[a, b][:], rows.rearrange("(p i) c -> p i c", i=SLOTS))

        def load_coef(b):
            coef_sb[b] = held("coef_sb%d" % b, [P, SLOTS, N], F32)
            rows = coef[b * PASS : (b + 1) * PASS, :]
            nc.sync.dma_start(coef_sb[b][:], rows.rearrange("(p t) n -> p t n", t=SLOTS))

        amp_rows = held("amp_rows", [P, P], F32)
        nc.vector.memset(amp_rows[:], 0.0)
        nc.sync.dma_start(idx[:], offs)
        wp_sb = held("wp_sb", [P, H // 2], I32)
        nc.sync.dma_start(wp_sb[:], wp_words[0].bitcast(I32))
        nc.sync.dma_start(tab_rows[0 : P : SPREAD // 2, :], tab_scales.rearrange("a q t -> q a t").bitcast(I32))
        load_wc(1, 0)
        nc.sync.dma_start(idx2[:], offs2)
        nc.sync.dma_start(tab2_rows[0:P:SPREAD, :], tab2_scales[0].bitcast(I32))
        nc.sync.dma_start(wp_rows[0:P:SPREAD, :], wp_scales[0].bitcast(I32))
        nc.sync.dma_start(amp_rows[0 : P : QUADRANT // 2, :], amp.rearrange("(b q x) -> q b x", b=2, x=P))
        tab_sb0 = load_words("tab_sb0", tab_words[0])
        tab2_sb = load_words("tab2_sb", tab2_words[0])

        picked_rows = held("picked_rows", [P, 2 * S], U8)
        planes = held("planes", [P, (2 * S + H) // 4], I32)
        nc.vector.tensor_copy(picked_rows[:, 0:S], tab_rows[:].bitcast(U8).indirect(idx[:]))
        nc.vector.tensor_copy(picked_rows[:, S : 2 * S], tab2_rows[:].bitcast(U8).indirect(idx2[:]))
        picked_words = picked_rows[:].bitcast(I32)
        v_cols, v2_cols, wp_cols = slice(0, S // 4), slice(S // 4, S // 2), slice(S // 2, S // 2 + H // 4)
        second_plane = held("second_plane", [P, S // 4], I32)
        nc.gpsimd.tensor_copy(
            planes[:, wp_cols].bitcast(U8).rearrange("p (b t m) -> p b t m", b=2, t=SLOTS),
            wp_rows[:].bitcast(U8).rearrange("p (b m t) -> p b t m", b=2, t=SLOTS),
        )
        nc.vector.tensor_copy(planes[:, 0 : S // 2], picked_words)
        nc.vector.tensor_copy(second_plane[:], planes[:, v_cols])
        for r in range(1, 4):
            nc.sync.dma_start(planes[r:P:QUADRANT, :], planes[SPREAD * r : P : QUADRANT, :])
        v_scales = [plane.bitcast(U8).rearrange("p (s j) -> p s j", s=2) for plane in (planes[:, v_cols], second_plane[SECOND:P, :])]
        v2_scales = planes[:, v2_cols].bitcast(U8).rearrange("p (s j) -> p s j", s=2)
        wp_sorted_scales = planes[:, wp_cols].bitcast(U8)

        amp_sorted, amp_turned = held("amp_sorted", [P, P], F32), held("amp_turned", [P, P], F32)
        nc.scalar.copy(
            amp_sorted[:].rearrange("p (t m) -> p t m", t=SLOTS),
            amp_rows[:].rearrange("p (m t) -> p t m", t=SLOTS),
        )
        nc.vector.transpose(amp_turned[:], amp_sorted[:])
        amp_sb = amp_turned[:].rearrange("p (t b x) -> p b t x", t=SLOTS, b=2)

        load_wc(0, 0)
        tab_sb1 = load_words("tab_sb1", tab_words[1])
        for r in range(1, 4):
            nc.sync.dma_start(second_plane[SECOND + r : P : QUADRANT, :], second_plane[SECOND + SPREAD * r : P : QUADRANT, :])
        load_wc(0, 1)
        load_wc(1, 1)
        load_coef(0)
        load_coef(1)

        def gather(name, table, offsets, s, cuts=(0, HALF)):
            picked = held(name, [P, HALF], U32)
            window = table[:].bitcast(U32)
            for first, last in zip(cuts, cuts[1:]):
                entries = slice((s * HALF + first) // 16, (s * HALF + last) // 16)
                nc.vector.tensor_copy(picked[:, first:last], window.indirect(offsets[:, entries]))
            return picked

        def quantize(codes, scales, grouped):
            nc.vector.quantize_mx(out=codes.bitcast(FP8X4), scales=scales, in_=grouped)

        wc_bf, wc_codes, wc_scales = {}, {}, {}

        def wc_tiles(a, b):
            if (a, b) == (1, 1):
                wc_bf[a, b] = [held("wc_bf11%d" % pair, [P, 2, P, SLOTS], BF16, "wc_bf11")[:] for pair in range(2)]
            else:
                whole_block = held("wc_bf%d%d" % (a, b), [P, SLOTS, P, SLOTS], BF16)
                wc_bf[a, b] = [whole_block[:, 0:2], whole_block[:, 2:4], whole_block[:]]
            wc_codes[a, b] = held("wc_codes%d%d" % (a, b), [P, PASS], U32, "tab_sb0" if (a, b) == (1, 0) else None)
            wc_scales[a, b] = held("wc_scales%d%d" % (a, b), [P, PASS], U8)

        def round_wc(a, b, pair, on_scalar):
            slots = slice(2 * pair, 2 * pair + 2)
            rounded = wc_bf[a, b][pair].rearrange("p t m i -> p m i t")
            loaded = wc_sb[a, b][:].rearrange("p i (m t) -> p m i t", t=SLOTS)[:, :, :, slots]
            if on_scalar:
                nc.scalar.activation(rounded, loaded, ACT.Copy, scale=-1.0)
            else:
                nc.vector.tensor_scalar(rounded, loaded, -1.0, None, ALU.mult)

        def quantize_wc(a, b, first, last):
            cols = slice(first * P, last * P)
            grouped = wc_bf[a, b][first // 2 if last - first == 2 else 2].rearrange("p t m i -> p (t m i)")
            quantize(wc_codes[a, b][:, cols], wc_scales[a, b][:, cols], grouped)

        def prepare_wc(a, b, scalar_slots, width):
            wc_tiles(a, b)
            for pair in range(2):
                round_wc(a, b, pair, 2 * pair in scalar_slots)
            for first in range(0, SLOTS, width):
                quantize_wc(a, b, first, first + width)

        v_codes, v2_codes = {}, {}
        for s in range(2):
            v_codes[0, s] = gather("v_codes0%d" % s, tab_sb0, idx, s)
        wp_codes = held("wp_codes", [P, 2 * H], U8)
        nc.scalar.copy(
            wp_codes[:].bitcast(U16).rearrange("p (b t m) -> p b t m", b=2, t=SLOTS),
            wp_sb[:].bitcast(U16).rearrange("p (b m t) -> p b t m", b=2, t=SLOTS),
        )
        prepare_wc(1, 0, range(SLOTS), SLOTS)

        shifted = [held("shifted%d" % k, [P, 2, SLOTS], F32, None if k else "wc_sb10") for k in range(STEPS + 1)]
        nc.scalar.activation(
            shifted[0][:],
            amp_turned[:].bitcast(U32).rearrange("p (t b x) -> p b t x", t=SLOTS, b=2)[:, :, :, 0],
            ACT.Copy,
            scale=math.log(2.0) / 2.0**23,
            bias=(CENTRE - 127.0) * math.log(2.0) - STEPS,
        )
        for k in range(STEPS):
            decay = held("decay%d" % k, [P, 2, SLOTS], F32)
            nc.scalar.activation(decay[:], shifted[k][:], ACT.Exp, scale=-1.0, bias=float(k - STEPS))
            for b in range(2):
                for t in range(SLOTS):
                    nc.scalar.activation(
                        shifted[k + 1][:, b, t : t + 1],
                        decay[:, b, t : t + 1],
                        ACT.Identity,
                        scale=amp_sb[:, b, t, 0:1],
                        bias=shifted[k][:, b, t : t + 1],
                    )

        def log_amp(b, t):
            return shifted[STEPS][:, b, t : t + 1]

        v2_codes[0] = gather("v2_codes0", tab2_sb, idx2, 0, (0, QUARTER, HALF))
        v2_codes[1] = gather("v2_codes1", tab2_sb, idx2, 1)
        prepare_wc(0, 0, range(SLOTS // 2, SLOTS), SLOTS // 2)
        v_codes[1, 0] = gather("v_codes10", tab_sb1, idx, 0, (0, P, QUARTER, HALF))
        v_codes[1, 1] = gather("v_codes11", tab_sb1, idx, 1)
        for a in range(2):
            wc_tiles(a, 1)
            for pair in range(2):
                round_wc(a, 1, pair, False)
                quantize_wc(a, 1, 2 * pair, 2 * pair + 2)

        def bank_tile(index):
            return psum.tile([P, BANK], F32, name="bank%d" % index, tag="bank%d" % index)

        h_codes = {(b, s): held("h_codes%d%d" % (b, s), [P, HALF], U32) for b in range(2) for s in range(2)}
        h_scales = {(b, s): held("h_scales%d%d" % (b, s), [P, HALF], U8) for b in range(2) for s in range(2)}

        def pieces(cols, width):
            return [slice(first, first + width) for first in range(cols.start, cols.stop, width)]

        whole = slice(0, HALF)
        early, late = pieces(whole, QUARTER)

        def crystal_pass(sums, b, s, t, a, cols, start, stop):
            rows = slice(t * P, (t + 1) * P)
            nc.tensor.matmul_mx(
                out=sums,
                lhsT=wc_codes[a, b][:, rows].bitcast(FP8X4),
                lhsT_scale=wc_scales[a, b][:, rows],
                rhs=v_codes[a, s][:, cols].bitcast(FP8X4),
                rhs_scale=v_scales[a][:, s, cols],
                start=start,
                stop=stop,
            )

        def prototype_pass(sums, b, s, t, cols, start):
            first = b * PASS + t * P
            nc.tensor.matmul_mx(
                out=sums,
                lhsT=wp_codes[:, 2 * first : 2 * (first + P)].bitcast(FP4X4),
                lhsT_scale=wp_sorted_scales[:, first : first + P],
                rhs=v2_codes[s][:, cols].bitcast(FP8X4),
                rhs_scale=v2_scales[:, s, cols],
                start=start,
                stop=False,
            )

        def project(b, s, cols, indices):
            banks = [bank_tile(index) for index in indices]
            width = cols.stop - cols.start
            slots_a_bank = SLOTS // len(banks)
            opens = (b, s) == (0, 0)
            ahead = cols.start < QUARTER
            for i, bank in enumerate(banks):
                slots = range(i * slots_a_bank, (i + 1) * slots_a_bank)
                for step in range(3):
                    for t in slots:
                        sums = bank[:, (t - slots[0]) * width : (t - slots[0] + 1) * width]
                        start, stop = step == 0 and t == slots[0], step == 2 and t == slots[-1]
                        if step == (0 if opens else 1):
                            prototype_pass(sums, b, s, t, cols, start)
                        elif opens:
                            crystal_pass(sums, b, s, t, step - 1 if ahead else 2 - step, cols, start, stop)
                        else:
                            crystal_pass(sums, b, s, t, step // 2 if b else 1 - step // 2, cols, start, stop)
            return banks

        def chunk_tiles(name, width, dist_tag=None, h_bf_tag=None):
            dist = held("dist" + name, [P, SLOTS * width], F32, dist_tag)
            h_slots = held("h_slots" + name, [P, SLOTS, width], BF16)
            h_bf = held("h_bf" + name, [P, width, SLOTS], BF16, h_bf_tag)
            return dist, h_slots, h_bf

        def take_abs(tiles, banks, i):
            nc.scalar.activation(tiles[0][:, i * BANK : (i + 1) * BANK], banks[i][:], ACT.Abs)

        def take_exp(tiles, b, t, cols):
            dist = tiles[0][:].rearrange("p (t j) -> p t j", t=SLOTS)
            nc.scalar.activation(tiles[1][:, t, cols], dist[:, t, cols], ACT.Exp, bias=log_amp(b, t), scale=-1.0)

        def laplace(tiles, banks, b):
            width = tiles[1].shape[2]
            slots_a_bank = SLOTS // len(banks)
            for i in range(len(banks) + 1):
                if i < len(banks):
                    take_abs(tiles, banks, i)
                if i > 0:
                    for t in range((i - 1) * slots_a_bank, i * slots_a_bank):
                        take_exp(tiles, b, t, slice(0, width))

        def interleave(tiles, cols):
            nc.vector.tensor_copy(
                tiles[2][:, cols, :].rearrange("p (c i) t -> p c t i", i=RUN),
                tiles[1][:, :, cols].rearrange("p t (c i) -> p c t i", i=RUN),
            )

        def quantize_h(tiles, cols, b, s, first):
            target = slice(first + cols.start, first + cols.stop)
            grouped = tiles[2][:, cols, :].rearrange("p j t -> p (j t)")
            quantize(h_codes[b, s][:, target], h_scales[b, s][:, target], grouped)

        def finish_h(tiles, b, s, first):
            width = tiles[1].shape[2]
            parts = pieces(slice(0, width), min(width, QUARTER))
            for cols in parts:
                interleave(tiles, cols)
            for cols in parts:
                quantize_h(tiles, cols, b, s, first)

        coef_bf, coef_codes, coef_scales = {}, {}, {}

        def round_coef(b):
            coef_bf[b] = held("coef_bf%d" % b, [P, N, SLOTS], BF16)
            nc.vector.tensor_copy(
                coef_bf[b][:].rearrange("p (c i) t -> p c t i", i=RUN),
                coef_sb[b][:].rearrange("p t (c i) -> p c t i", i=RUN),
            )

        def quantize_coef(b):
            coef_codes[b] = held("coef_codes%d" % b, [P, N], U32)
            coef_scales[b] = held("coef_scales%d" % b, [P, N], U8)
            quantize(coef_codes[b][:], coef_scales[b][:], coef_bf[b][:].rearrange("p n t -> p (n t)"))

        def readout_pass(sums, n_tile, b, s, cols):
            rows = slice(n_tile * P, (n_tile + 1) * P)
            nc.tensor.matmul_mx(
                out=sums,
                lhsT=coef_codes[b][:, rows].bitcast(FP8X4),
                lhsT_scale=coef_scales[b][:, rows],
                rhs=h_codes[b, s][:, cols].bitcast(FP8X4),
                rhs_scale=h_scales[b, s][:, cols],
                start=(b == 0),
                stop=(b == 1),
            )

        def read_out_paired(indices, cols):
            banks = [bank_tile(index) for index in indices]
            width = cols.stop - cols.start
            for n_tile in n_tiles:
                for b in range(2):
                    first = (n_tile % 2) * width
                    readout_pass(banks[n_tile // 2][:, first : first + width], n_tile, b, 1, cols)
            return banks

        def copy_out(target, source, on_scalar):
            if on_scalar:
                nc.scalar.copy(target, source)
            else:
                nc.vector.tensor_copy(target, source)

        def store(name, bank, target, on_scalar):
            staged = held(name, [P, BANK], F32)
            copy_out(staged[:], bank[:], on_scalar)
            nc.sync.dma_start(target, staged[:].rearrange("p (a j) -> p a j", a=target.shape[1]))

        out_tiles = out.rearrange("(a p) j -> p a j", p=P)
        n_tiles = range(N // P)

        def second_half(cols):
            return slice(HALF + cols.start, HALF + cols.stop)

        opening = [chunk_tiles("00", QUARTER, None, "wc_bf10"), chunk_tiles("01", QUARTER)]
        wide = chunk_tiles("10", HALF, "tab2_sb")
        narrow = [chunk_tiles("e%d" % b, QUARTER, "dist0%d" % b) for b in range(2)]
        opening_dist = opening[0][0][:].rearrange("p (t j) -> p t j", t=SLOTS)
        for i, cols in enumerate(pieces(early, P)):
            bank = project(0, 0, cols, (i,))[0]
            nc.scalar.activation(opening_dist[:, :, cols], bank[:].rearrange("p (t j) -> p t j", t=SLOTS), ACT.Abs)
        for t in range(SLOTS):
            take_exp(opening[0], 0, t, early)
        laplace(opening[1], project(0, 0, late, (2, 3)), 0)
        laplace(narrow[0], project(0, 1, early, (4, 5)), 0)
        laplace(wide, project(1, 0, whole, (6, 7, 0, 1)), 1)
        laplace(narrow[1], project(1, 1, early, (2, 3)), 1)
        finish_h(opening[0], 0, 0, early.start)
        finish_h(opening[1], 0, 0, late.start)
        round_coef(0)
        finish_h(narrow[0], 0, 1, early.start)
        quantize_coef(0)
        round_coef(1)
        interleave(wide, early)
        quantize_coef(1)
        quantize_h(wide, early, 1, 0, 0)
        interleave(wide, late)
        quantize_h(wide, late, 1, 0, 0)
        late_first = chunk_tiles("l0", QUARTER, "dist00")
        laplace(late_first, project(0, 1, late, (4, 5)), 0)

        first_out = [bank_tile(n_tile) for n_tile in n_tiles]
        for b in range(2):
            for n_tile in n_tiles:
                readout_pass(first_out[n_tile][:], n_tile, b, 0, whole)
        ends = pieces(late, P)
        last = [chunk_tiles("l1%d" % i, P) for i in range(2)]
        for i in range(2):
            laplace(last[i], project(1, 1, ends[i], (6 + i,)), 1)
        finish_h(narrow[1], 1, 1, early.start)
        nc.gpsimd.tensor_copy(late_first[2][:], late_first[1][:].rearrange("p t j -> p j t"))
        for n_tile in n_tiles:
            store("first%d" % n_tile, first_out[n_tile], out_tiles[:, n_tile : n_tile + 1, whole], False)

        early_out = read_out_paired((4, 7), early)
        quantize_h(late_first, early, 0, 1, late.start)
        for pair in range(2):
            store("early%d" % pair, early_out[pair], out_tiles[:, 2 * pair : 2 * pair + 2, second_half(early)], True)

        finish_h(last[0], 1, 1, ends[0].start)
        near_out = read_out_paired((5, 6), ends[0])
        end_out = [bank_tile(n_tile) for n_tile in n_tiles]
        for n_tile in n_tiles:
            readout_pass(end_out[n_tile][:, 0:P], n_tile, 0, 1, ends[1])
        finish_h(last[1], 1, 1, ends[1].start)
        near = held("near", [P, N // P, P], F32)
        for pair in range(2):
            target = near[:, 2 * pair : 2 * pair + 2, :].rearrange("p a j -> p (a j)")
            copy_out(target, near_out[pair][:, 0 : 2 * P], pair == 0)
        nc.sync.dma_start(out_tiles[:, :, second_half(ends[0])], near[:])
        for n_tile in n_tiles:
            readout_pass(end_out[n_tile][:, 0:P], n_tile, 1, 1, ends[1])
        for parity in range(2):
            staged = held("end%d" % parity, [P, 2, P], F32)
            for i in range(2):
                copy_out(staged[:, i, :], end_out[2 * i + parity][:, 0:P], parity == 0)
            nc.sync.dma_start(out_tiles[:, parity : N // P : 2, second_half(ends[1])], staged[:])
